import numpy as np, ml_dtypes
CORES = [24,25,26,27,28,29,30,31]
N = 8
BF = ml_dtypes.bfloat16
V, G, RO, RW, TU, TD = 2560, 128, 4, 2, 5, 4
W = V + (N - 1) * G
def parts(rng):
    S = rng.integers(0, W, (N, 8, 16, V)); T = rng.integers(0, W, (N, 8, 16, V))
    cs = rng.integers(0, 16, (N, 8, V)); ct = rng.integers(0, 16, (N, 8, V))
    return S, T, cs, ct, rng.integers(-256, 257, (N, 8, 16, V)) * 0.00390625
def pack(S, T, cs, ct, s):
    return {"s0": np.ascontiguousarray(s.reshape(N, 128, V)).astype(BF), "pt": (S + 4096 * T).reshape(N, 128, V).astype(np.int32), "cur": (cs + 16 * ct).astype(np.int32)}
def plant(S, T, cs, ct, s):
    def put(v, a, b):
        np.put_along_axis(S[..., v], cs[..., v][..., None], a, 2); np.put_along_axis(T[..., v], ct[..., v][..., None], b, 2)
    s[..., 1] = 0.25; put(1, W - 1, 0); s[..., 3] = 1.0; put(3, 3, 3)
    for k in range(17):
        m = 16 + k; s[:, ::2, :k, m] = -1.0; s[:, 1::2, :k, m] = -2.0 ** -20; s[:, :, k:, m] = 0.5; put(m, 1, m)
        for v in (40 + 2 * k, V - 33 + 2 * k): s[..., v] = -1.0; put(v, 1, m)
        for v in (41 + 2 * k, V - 34 + 2 * k): s[..., v] = 1.0; put(v, 3, m)
    for j in range(8):
        for e in (80 + 3 * j, V - 64 + 3 * j):
            s[..., e] = 0.130859375; s[..., e + 1] = 0.9140625; s[..., e + 2] = 0.1875
            put(e, 1, e + 2); put(e + 1, e, e + 1); put(e + 2, e + 1, e + 2)
    for h in (106, V - 72):
        o, g, b, e, a, v, x = range(h, h + 7)
        for m, t in ((o, 0.0), (g, 0.96484375), (b, 0.388671875), (e, 0.58984375), (a, 0.84765625), (v, 0.000732421875), (x, -1.0)): s[..., m] = t
        put(o, o, o); put(g, o, g); put(b, g, b); put(e, o, e); put(a, e, a); put(v, a, 32); put(x, x, v)
        np.put_along_axis(S[..., v], ((cs[..., v] + 1) & 15)[..., None], b, 2)
def setup_inputs(rng):
    return pack(*parts(rng))
def setup_inputs_spread(rng):
    S, T, cs, ct, s = parts(rng)
    s = s * np.exp2(rng.integers(-2, 1, (N, 8, 1, V))) * (rng.random((N, 8, 1, V)) > 0.0625)
    S = np.minimum((W * rng.random(S.shape) ** 2).astype(np.int64), W - 1); T = W - 1 - np.minimum((W * rng.random(T.shape) ** 3).astype(np.int64), W - 1)
    cs = np.minimum((16 * rng.random(cs.shape) ** 3).astype(np.int64), 15); ct = 15 - np.minimum((16 * rng.random(ct.shape) ** 3).astype(np.int64), 15)
    return pack(S, T, cs, ct, s)
def setup_inputs_ends(rng):
    S, T, cs, ct, s = parts(rng)
    u = rng.random(S.shape); lo, hi = 0, W - 1
    S = np.where(u < 0.36, lo, np.where(u < 0.72, hi, np.where(u < 0.79, lo, np.where(u < 0.86, hi, S))))
    T = np.where(u < 0.36, lo, np.where(u < 0.72, hi, np.where(u < 0.79, hi, np.where(u < 0.86, lo, T))))
    u = rng.random(cs.shape)
    cs = np.where(u < 0.36, 0, np.where(u < 0.72, 15, np.where(u < 0.79, 0, np.where(u < 0.86, 15, cs))))
    ct = np.where(u < 0.36, 0, np.where(u < 0.72, 15, np.where(u < 0.79, 15, np.where(u < 0.86, 0, ct))))
    sg = np.where(rng.random((N, 8, 1, V)) < 0.5, rng.integers(0, 2, (N, 8, 1, V)), rng.integers(0, 2, s.shape)) * 2.0 - 1.0
    m = rng.random((N, 8, 1, V)) < 0.7; m[..., 0] = False; m[..., G - 1] = False
    s = np.where(m, sg, s); plant(S, T, cs, ct, s)
    return pack(S, T, cs, ct, s)
def setup_inputs_corners(rng):
    S, T, cs, ct, s = parts(rng); v = np.arange(V); z = 0 * v
    tbl = np.stack([v, (v - 1) % V, (v + 1) % V, V - 1 - v, z, z + V - 1, z + V, z + W - 1, z + G - 1, V + v % G, W - 1 - v % G, v % G])
    S = np.where(rng.random(S.shape) < 0.25, S, tbl[rng.integers(0, len(tbl), (N, 8, 16))])
    T = np.where(rng.random(T.shape) < 0.25, T, tbl[rng.integers(0, len(tbl), (N, 8, 16))])
    e = np.array([0, 1, 14, 15]); cs = rng.choice(e, cs.shape); ct = rng.choice(e, ct.shape)
    s = np.where(rng.random(s.shape) < 0.7, rng.choice(np.array([0.0, 0.25, -0.25, 0.5, -0.5, 1.0, -1.0]), s.shape), s)
    plant(S, T, cs, ct, s)
    return pack(S, T, cs, ct, s)
def setup_inputs_crowd(rng):
    S, T, cs, ct, s = parts(rng); pl = np.array([0, G - 1, G, V - 1, V, W - 1]); g = np.arange(8).reshape(1, 8, 1, 1); v = np.arange(V); home = (g == 4) | (g == 7)
    for X in (S, T):
        same = np.where(home, rng.choice(pl[:4], (N, 8, 16, 1)), rng.choice(pl, (N, 8, 16, 1)))
        few = np.where(home, rng.choice(pl[:4], X.shape), rng.choice(pl, X.shape)); but = rng.integers(0, V, (N, 8, 16, 1))
        X[...] = np.where(g % 4 == 3, few, np.where((g % 2 == 1) & (v == but), X, same))
    s[:, 4] = s[:, 4, :1] + 0.0; s[:, 7, :15] = s[:, 7, :1] + 0.0
    return pack(S, T, cs, ct, s)
def setup_inputs_calm(rng):
    S, T, cs, ct, s = parts(rng); r = np.arange(N).reshape(N, 1, 1); g = np.arange(8).reshape(1, 8, 1)
    cs = 0 * cs + (g + r) % 4; ct = 0 * ct + (g // 2 + r) % 4
    share = np.array([0.97, 0.95, 0.9, 0.8]).reshape(1, 4, 1, 1); share = np.concatenate([share, share], axis=1)
    return pack(S, T, cs, ct, np.where(rng.random(s.shape) < share, 0.5, s))
def check_ranges(d):
    bad = []; p = np.asarray(d["pt"]).astype(np.int64); c = np.asarray(d["cur"]).astype(np.int64); a = np.abs(np.asarray(d["s0"]).astype(np.float64))
    if np.min(p) < 0 or np.max(p) > 4097 * (W - 1) or np.max(p & 4095) > W - 1 or np.max(p >> 12) > W - 1: bad.append("range of pt")
    if np.min(c) < 0 or np.max(c) > 255: bad.append("range of cur")
    if not np.all((a == 0) | ((a >= 2.0 ** -20) & (a <= 1))): bad.append("size of s0")
    return bad
def pick(t, ix):
    out = []
    for r in range(N):
        w = [t[r]] + [t[(r - d) % N][(np.arange(8) + d * (d + 1) // 2) % 8][..., :G] for d in range(1, N)]
        out.append(np.take_along_axis(np.concatenate(w, axis=2), ix[r][:, None, :], 2))
    return np.stack(out)
def reference(s0, pt, cur):
    s = s0.astype(np.float32).reshape(N, 8, 16, V); y = s.astype(np.float64); c = np.zeros(s.shape, np.int64)
    p = pt.astype(np.int64).reshape(N, 8, 16, V); S = p & 4095; T = p >> 12
    cs = cur.astype(np.int64) & 15; ct = cur.astype(np.int64) >> 4; row = np.arange(16).reshape(1, 1, 16, 1)
    for step in range(RO):
        a = np.take_along_axis(S, cs[:, :, None], 2)[:, :, 0]; b = np.take_along_axis(T, ct[:, :, None], 2)[:, :, 0]
        sa, ya, cb = pick(s, a), pick(y, a), pick(c, b)
        new = np.float32(1) - np.float32(2) * np.abs(sa * s)
        z = np.add.reduce(np.where(s >= 0, cb, -cb), axis=2)
        hold = z <= -TD
        y = np.where(hold[:, :, None], y, np.tanh((1.0 + ya) * new))
        if step < RO - 1:
            via = np.take_along_axis(a, np.minimum(a, V - 1), 2)
            m = (a < V) & (z >= RW) & (z < TU)
            S = np.where(m[:, :, None] & (row == cs[:, :, None]), via[:, :, None], S)
        c = ((s < 0) & (new >= 0)).astype(np.int64) - ((s >= 0) & (new < 0)).astype(np.int64)
        cs = (cs + (z >= TU)) & 15; ct = (ct + hold) & 15; s = new
    return {"y": y.reshape(N, 128, V).astype(np.float32), "q": (cs + 16 * ct).astype(np.float32)}

def check_inputs(d):
    bad = list(check_ranges(d))
    if not bad:
        for name, y in reference(**d).items():
            for q in range(N):
                v = np.abs(np.asarray(y[q], np.float64)); s = np.sqrt(np.mean(v * v))
                if v.max() > 4 * s or s < 2.0 ** -2: bad.append('%s of rank %d is uneven or too small' % (name, q))
    return bad

@@ -1,0 +1,563 @@
+from concourse.bass import DstId, RemoteDMATransfer
+from concourse.mybir import AluOpType, ActivationFunctionType
+
+V, NB, WN, N = 2560, 128, 3456, 8
+C = V // 16
+OFF = 1720.0
+MAGIC = 12582912.0
+TC = 512
+
+SCRATCH = {}
+for _n, _w, _d in [
+    ("PT", V, "int32"), ("XS", WN, "float32"), ("P", V, "float32"), ("S0", WN, "bfloat16"), ("UL", V, "float32"), ("SB", NB, "bfloat16"),
+    ("U1", WN, "float32"), ("U2", WN, "float32"), ("U3", WN, "float32"),
+    ("W0", WN, "float32"), ("W1", WN, "float32"), ("W2", WN, "float32"),
+    ("SG0", WN, "bfloat16"), ("SG1", WN, "bfloat16"),
+    ("TH", 4 * V, "float32"), ("SP", V, "float32"), ("VO", V, "float32"),
+    ("CW", C, "float32"), ("CI", C, "int32"), ("C3", 2 * C, "int32"), ("MW", 512, "bfloat16"), ("LM", 32, "uint16"),
+    ("CB", C, "bfloat16"), ("LC", C, "uint16"), ("IOT", 160, "float32"), ("PI", 8, "int32"), ("PJ", 8, "int32"),
+    ("PF", 16, "float32"), ("M3I", 16, "int32"), ("M3J", 16, "int32"), ("M3", 16, "float32"),
+    ("B1", 144, "float32"), ("B2", 144, "float32"), ("BV", 144, "float32"), ("ID", 128, "float32"), ("NID", 128, "float32"),
+    ("BZ", 144, "bfloat16"), ("BT0", 144, "bfloat16"), ("BT1", 144, "bfloat16"), ("BT2", 144, "bfloat16"), ("BT3", 144, "bfloat16"),
+    ("IB", 128, "bfloat16"), ("IB16", 128, "bfloat16"), ("IBL", 128, "bfloat16"),
+    ("SN", 3 * C, "float32"), ("TN", 3 * C, "float32"),
+    ("LS0", 2 * C, "uint16"), ("LS1", 3 * C, "uint16"), ("LS2", 3 * C, "uint16"),
+    ("AB", 2 * C, "float32"), ("FL1", 4 * C, "bfloat16"), ("FL2", 5 * C, "bfloat16"), ("FL3", 5 * C, "bfloat16"),
+    ("PR1", 5 * C, "float32"), ("BK", 3 * C, "float32"), ("BC", C, "float32"),
+]:
+    SCRATCH[_n] = ("sbuf", [128, _w], _d)
+SCRATCH["CN"] = ("sbuf", [128, 2, 5, 16], "int32")
+for _n in ("NF", "NA", "NQ"):
+    SCRATCH[_n] = ("sbuf", [128, 2, 5, 16], "float32")
+for _k in range(8):
+    SCRATCH["K%d" % _k] = ("psum", [128, 512], "float32")
+for _n in ("DU1", "DU2", "DU3", "DW1", "DW2", "DW3"):
+    SCRATCH[_n] = ("dram", [256, NB], "float32")
+for _n in ("DS0", "DG0", "DG1", "DG2", "DG3"):
+    SCRATCH[_n] = ("dram", [256, NB], "bfloat16")
+
+XCH = ["s0", "u1", "u2", "u3", "c1", "c2", "c3", "w1", "w2", "w3"]
+SEMAPHORES = (["e_v", "e_a", "e_t", "e_g"] + ["d%d" % _k for _k in range(70)] + ["arr_" + _x for _x in XCH]
+              + ["out_" + _x for _x in XCH])
+
+ALIAS = {"SG2": ("S0", 0), "SG3": ("SG0", 0), "OH": ("SG1", 1280), "MG": ("TH", 8192 + TC), "MT": ("TH", 8192 + TC),
+         "MH": ("TH", 8192 + TC + 640), "PR2": ("PR1", 0), "PRD1": ("S0", 0), "PRD2": ("SG0", 0), "PRD3": ("SG1", 0),
+         "U0": ("U3", 0), "LS3": ("LS0", -2 * C), "QI": ("PT", 0), "QF": ("CW", 0), "C3B": ("SG1", 0)}
+
+ORDER = [7, 17, 1, 9, 19, 0, 18, 8, 14, 16, 15, 28, 21, 20, 30, 23, 22, 25, 35, 27, 29, 26, 45, 49, 50, 36, 2, 46, 47, 48, 12, 5, 51, 54, 56, 52, 70, 6, 31, 58, 59, 57, 55, 40, 3, 60, 76, 74, 4, 61, 34, 62, 64, 66, 67, 63, 69, 109, 24, 65, 77, 10, 68, 71, 78, 41, 37, 110, 80, 91, 79, 88, 89, 81, 92, 42, 11, 83, 82, 72, 93, 101, 94, 95, 96, 104, 105, 106, 122, 121, 73, 103, 124, 107, 123, 125, 127, 90, 102, 86, 140, 151, 108, 141, 98, 144, 143, 118, 142, 75, 145, 97, 113, 117, 85, 146, 175, 179, 116, 87, 112, 126, 84, 111, 115, 153, 176, 129, 135, 133, 156, 13, 132, 119, 128, 134, 154, 166, 147, 158, 180, 100, 162, 99, 148, 159, 177, 187, 114, 155, 137, 38, 33, 186, 139, 138, 170, 161, 178, 149, 171, 136, 160, 181, 172, 44, 188, 120, 130, 167, 193, 163, 168, 150, 195, 198, 194, 131, 197, 164, 212, 209, 182, 207, 199, 157, 196, 169, 32, 185, 206, 165, 183, 173, 210, 184, 208, 200, 216, 189, 219, 201, 226, 227, 192, 191, 214, 211, 221, 218, 213, 152, 220, 222, 174, 237, 234, 235, 233, 204, 223, 230, 232, 43, 202, 190, 203, 243, 215, 236, 245, 265, 249, 224, 228, 225, 244, 231, 252, 253, 254, 257, 285, 238, 205, 239, 241, 217, 240, 242, 246, 247, 250, 288, 286, 292, 282, 266, 268, 248, 229, 259, 260, 290, 271, 267, 261, 272, 251, 262, 258, 297, 264, 284, 263, 269, 279, 287, 295, 270, 283, 296, 255, 289, 256, 293, 294, 309, 308, 275, 280, 314, 304, 305, 312, 302, 39, 276, 303, 315, 53, 319, 291, 306, 273, 317, 321, 274, 318, 281, 329, 277, 322, 278, 323, 325, 324, 298, 307, 299, 328, 334, 311, 310, 339, 313, 300, 341, 332, 316, 320, 301, 340, 342, 330, 345, 351, 333, 344, 331, 335, 336, 347, 337, 348, 326, 327, 338, 350, 354, 346, 343, 349, 353, 359, 364, 355, 362, 366, 356, 368, 363, 369, 367, 370, 352, 360, 361, 357, 358, 371, 372, 365, 374, 373, 376, 378, 377, 375, 379, 380]
+
+A = AluOpType
+F = ActivationFunctionType
+
+
+def build(g, core, T, topo):
+    rank = T.rank_of(core)
+    ops = []
+
+    def real(x):
+        if x[0] not in ALIAS:
+            return x
+        n, o = ALIAS[x[0]]
+        return (n, x[1] + o, x[2] + o) + tuple(x[3:])
+
+    def buf(n):
+        return T[ALIAS[n][0]] if n in ALIAS else T[n]
+
+    def ap(x):
+        if len(x) == 1:
+            return T[x[0]][:]
+        x = real(x)
+        if len(x) == 3:
+            return T[x[0]][:, x[1]:x[2]]
+        return T[x[0]][:, x[1]:x[2]:x[3]]
+
+    def reg(x):
+        return (x[0], 0, 1 << 20) if len(x) == 1 else real(x)[:3]
+
+    def op(q, fn, rd, wr, kind="c", **kw):
+        ops.append(dict(q=q, fn=fn, rd=[reg(x) for x in rd], wr=[reg(x) for x in wr], kind=kind, **kw))
+
+    def sc(s):
+        return ap(s) if isinstance(s, tuple) else s
+
+    def ts(out, x, s1, o0, s2=None, o1=None):
+        rd = [x] + [s for s in (s1, s2) if isinstance(s, tuple)]
+        if o1 is None:
+            op("v", lambda: g.vector.tensor_scalar(ap(out), ap(x), sc(s1), None, o0), rd, [out])
+        else:
+            op("v", lambda: g.vector.tensor_scalar(ap(out), ap(x), sc(s1), sc(s2), o0, o1), rd, [out])
+
+    def tt(out, x, y, o):
+        op("v", lambda: g.vector.tensor_tensor(ap(out), ap(x), ap(y), o), [x, y], [out])
+
+    def cp(out, x):
+        op("v", lambda: g.vector.tensor_copy(ap(out), ap(x)), [x], [out])
+
+    def gtt(out, win, lst, y):
+        op("v", lambda: g.vector.tensor_tensor(ap(out), ap(win).indirect(ap(lst)), ap(y), A.mult), [win, lst, y], [out])
+
+    def act(out, x, f, scale=1.0, bias=0.0, lst=None):
+        if lst is None:
+            op("a", lambda: g.scalar.activation(ap(out), ap(x), f, bias=sc(bias), scale=sc(scale)),
+               [x] + [s for s in (scale, bias) if isinstance(s, tuple)], [out])
+        else:
+            op("a", lambda: g.scalar.activation(ap(out), ap(x).indirect(ap(lst)), f, bias=bias, scale=scale), [x, lst], [out])
+
+    def mm(out, terms, first=True, last=True):
+        def fn():
+            ins = None
+            for j, (l, r) in enumerate(terms):
+                ins = g.tensor.matmul(ap(out), ap(l), ap(r), first and j == 0, last and j == len(terms) - 1)
+            return ins
+        op("t", fn, [x for t in terms for x in t], [out])
+
+    def iota(out, pat, base, cm, flt):
+        if flt:
+            op("g", lambda: g.iota(ap(out), pat, base, cm, allow_small_or_imprecise_dtypes=True), [], [out])
+        else:
+            op("g", lambda: g.iota(ap(out), pat, base, cm), [], [out])
+
+    def dma(q, o, i, rd, wr):
+        e = g.sync if q == "s" else g.scalar
+        op(q, lambda: e.dma_start(o, i), rd, wr, kind="d")
+
+    def turn_in(out, src):
+        for b in range(5):
+            op("v", lambda b=b: g.vector.transpose(T[out][:, b:C:5], T[src][:, :, b, :]), [(src,)], [(out, 0, C)], par=1)
+
+    def turn_out(out, src, c0):
+        for b in range(5):
+            op("v", lambda b=b: g.vector.transpose(T[out][:, :, b, :], buf(src)[:, c0 + b:c0 + C:5]), [(src, c0, c0 + C)], [(out,)], par=1)
+
+    peers = [T.cores[(rank + d) % N] for d in range(1, N)]
+    masks, nxt = [], [0, 0]
+    for c in peers:
+        e = topo.engines(core, c)
+        far = 0 if topo.die(c) != topo.die(core) else 1
+        j = 4 * nxt[far] + far
+        nxt[far] += 1
+        masks.append((1 << e[j]) | (1 << e[j + 2]))
+
+    def stage(dn, src_ap, rd):
+        dma("s", T[dn][16:128, :], src_ap[16:128, 0:NB], rd, [(dn, 0, 1)])
+        dma("s", T[dn][128:240, :], src_ap[0:112, 0:NB], rd, [(dn, 1, 2)])
+
+    def send(x, dns, win, after=()):
+        def fn():
+            trs = []
+            for d in range(1, N):
+                rid, pid, _se = topo.addr(peers[d - 1])
+                r0 = 16 * ((d * (d + 1) // 2) % 8)
+                dst = buf(win)[:, V + (d - 1) * NB:V + d * NB]
+                kw = dict(dst_ids=[DstId(rid=rid, pnc=pid)], dma_engine_mask=masks[d - 1], remote_sem=T.sem["arr_" + x])
+                if len(dns) == 1:
+                    trs.append(RemoteDMATransfer(src=T[dns[0]][r0:r0 + 128, :], dst=dst, **kw))
+                else:
+                    trs.append(RemoteDMATransfer(srcs=[T[n][r0:r0 + 128, :] for n in dns], dsts=[dst], alu_op=1, **kw))
+            return g.remote_dma_fused(trs, local_sem=T.sem["out_" + x])
+        op("g", fn, [(n,) for n in dns] + list(after), [("X" + x,)], kind="r", x=x)
+        ops.append(dict(q=None, kind="arr", x=x, rd=[reg(("X" + x,))], wr=[reg((win, V, WN))]))
+
+    H = V // 2
+    for gg in range(2):
+        dma("s", T.CN[:, gg], T.cur[gg:8:2, :], [], [("CN", gg, gg + 1)])
+    dma("s", T.PT[:, 0:H], T.pt[:, 0:H], [], [("PT", 0, H)])
+    stage("DS0", T.s0, [])
+    dma("s", T.S0[:, 0:V], T.s0[:, :], [], [("S0", 0, V)])
+    dma("s", T.PT[:, H:V], T.pt[:, H:V], [], [("PT", H, V)])
+
+    iota(("PI", 0, 8), [[0, 8]], 0, 1, False)
+    iota(("M3I", 0, 16), [[-1, 16]], 16, 1, False)
+    iota(("IOT", 0, 160), [[1, 160]], -15, 0, True)
+    send("s0", ["DS0"], "S0")
+    iota(("BC", 0, C), [[0, 5], [16, 32]], TC, 0, True)
+    iota(("XS", V, WN), [[1, WN - V]], V - int(OFF), 0, True)
+    for j, m in enumerate((112, 3, 12, 15, 115, 127)):
+        ts(("PJ", j, j + 1), ("PI", j, j + 1), m, A.bitwise_and)
+    ts(("M3J", 0, 16), ("M3I", 0, 16), 15, A.bitwise_and)
+    cp(("PF", 0, 6), ("PJ", 0, 6))
+    ts(("M3", 0, 16), ("M3J", 0, 16), 3.0, A.is_lt)
+    col = lambda j: ("PF", j, j + 1)
+    ts(col(6), col(1), 4.0, A.mult, col(0), A.add)
+    ts(col(7), col(3), 1000.0, A.mult, col(0), A.add)
+    ts(("PF", 8, 12), ("IOT", 15, 31, 4), col(2), A.is_equal)
+    ts(("B1", 0, 144), ("IOT", 12, 156), col(6), A.is_equal)
+    ts(("LM", 0, 16), ("IOT", 15, 31), 0.0, A.mult, col(3), A.add)
+    cp(("LM", 16, 32), ("IOT", 15, 31))
+    act(("MW", 0, 512), ("M3", 0, 16), F.Identity, lst=("LM", 0, 32))
+    ts(("B2", 0, 144), ("IOT", 3, 147), col(4), A.is_equal)
+    ts(("ID", 0, 128), ("IOT", 15, 143), col(5), A.is_equal)
+    ts(("BZ", 0, 144), ("IOT", 0, 144), col(0), A.is_equal)
+    ts(("BV", 0, 144), ("IOT", 0, 144), col(7), A.is_equal)
+    for t in range(4):
+        act(("BT%d" % t, 0, 144), ("B2", 0, 144), F.Identity, col(8 + t))
+    for n, w in (("NID", -1.0), ("IB", 1.0), ("IB16", 16.0), ("IBL", -float(TC))):
+        act((n, 0, 128), ("ID", 0, 128), F.Identity, w)
+    act(("BK", 0, C), ("BC", 0, C), F.Identity, 1.0, col(3))
+    for k in (1, 2):
+        act(("BK", k * C, (k + 1) * C), ("BK", 0, C), F.Identity, 1.0, float(TC * k))
+
+    cp(("NF",), ("CN",))
+    turn_in("CW", "NF")
+    cp(("LC", 0, C), ("CW", 0, C))
+    cp(("CI", 0, C), ("CW", 0, C))
+    act(("CB", 0, C), ("CW", 0, C), F.Identity)
+
+    XB = ("XS", "P")
+    tile = lambda n: ("TH", 2048 * (n // 2) + TC + 640 * (n % 2))
+
+    def half(x, a, b):
+        return (x[0], x[1] + a, x[1] + b)
+
+    def masked(tau, h):
+        gtt((XB[tau], h * H, (h + 1) * H), ("MW", 256 * tau, 256 * (tau + 1)), ("LC", 80 * h, 80 * (h + 1)), ("PT", h * H, (h + 1) * H))
+
+    def stage1(tau, h):
+        for t in range(4):
+            c0 = (t % 2) * C + 80 * h
+            mm(("K%d" % (2 * tau + t // 2), c0, c0 + 80),
+               [(("B1", 3 - u, 131 - u), (XB[tau], h * H + 4 * t + u, (h + 1) * H, 16)) for u in range(4)])
+
+    def evac(tau):
+        for j in range(2):
+            act(half(tile(tau), 320 * j, 320 * (j + 1)), ("K%d" % (2 * tau + j), 0, 320), F.Identity, 1.0, -OFF)
+
+    def sel(tau, d, kb):
+        for t in range(4):
+            c0 = (t % 2) * C
+            mm(("K%d" % (kb + t // 2), c0, c0 + C),
+               [(("BT%d" % t, 12 - 4 * ((k + d) % 4), 140 - 4 * ((k + d) % 4)), ("OH", (2 * k + tau) * C, (2 * k + tau + 1) * C)) for k in range(4)])
+
+    def pickd(tau, d, kb):
+        for j in range(2):
+            tt(half(tile(2 + 3 * tau + d), 320 * j, 320 * (j + 1)), half(tile(tau), 320 * j, 320 * (j + 1)), ("K%d" % (kb + j), 0, 320), A.mult)
+
+    def stage2(tau, d, kb):
+        mm(("K%d" % kb, d * C, (d + 1) * C), [(("B2", 12 - 4 * t, 140 - 4 * t), half(tile(2 + 3 * tau + d), t * C, (t + 1) * C)) for t in range(4)])
+
+    def field_s_act(kb, a, b):
+        act(("MG", a, b), ("K%d" % kb, a, b), F.Identity, 2.0 ** -12, MAGIC)
+        act(("MH", a, b), ("MG", a, b), F.Identity, 4096.0, -4096.0 * MAGIC)
+
+    def field_s(kb, a, b):
+        tt(("SN", a, b), ("K%d" % kb, a, b), ("MH", a, b), A.subtract)
+
+    def field_t(kb):
+        act(("MT", 0, 3 * C), ("K%d" % kb, 0, 3 * C), F.Identity, 2.0 ** -12, MAGIC)
+        act(("TN", 0, 3 * C), ("MT", 0, 3 * C), F.Identity, 1.0, -MAGIC)
+
+    def own_copy(k, a, b):
+        dma("s", T.UL[:, a:b], buf("U%d" % k)[:, a:b], [("U%d" % k, a, b)], [("UL", a, b)])
+
+    masked(0, 0)
+    stage1(0, 0)
+    masked(0, 1)
+    ts(("C3", 0, C), ("CI", 0, C), 3, A.bitwise_and)
+    ts(("C3", C, 2 * C), ("CI", 0, C), 4, A.logical_shift_right, 3, A.bitwise_and)
+    cp(("C3B", 0, 2 * C), ("C3", 0, 2 * C))
+    for k in range(4):
+        ts(("OH", 2 * k * C, 2 * (k + 1) * C), ("C3B", 0, 2 * C), float(k), A.is_equal)
+    act(("SB", 0, NB), ("S0", 0, NB), F.Sign, 1.0, 2.0 ** -30)
+    stage("DG0", T.SB, [("SB", 0, NB)])
+    for h in range(2):
+        act(("U0", h * H, (h + 1) * H), ("S0", h * H, (h + 1) * H), F.Abs)
+        own_copy(0, h * H, (h + 1) * H)
+    for h in range(2):
+        act(("W0", h * H, (h + 1) * H), ("S0", h * H, (h + 1) * H), F.Identity, 0.5, 0.5)
+    stage1(0, 1)
+    sel(0, 0, 4)
+    sel(0, 1, 6)
+    evac(0)
+    act(("U0", V, WN), ("S0", V, WN), F.Abs)
+    masked(1, 0)
+    pickd(0, 0, 4)
+    stage2(0, 0, 0)
+    field_s_act(0, 0, C)
+    sel(0, 2, 4)
+    stage1(1, 0)
+    masked(1, 1)
+    field_s(0, 0, C)
+    ts(("LS0", 0, C), ("SN", 0, C), OFF, A.add)
+    act(("W0", V, WN), ("S0", V, WN), F.Identity, 0.5, 0.5)
+    for h in range(2):
+        act(("SG0", h * H, (h + 1) * H), ("S0", h * H, (h + 1) * H), F.Sign, 1.0, 2.0 ** -30)
+    pickd(0, 1, 6)
+    pickd(0, 2, 4)
+    stage1(1, 1)
+    stage2(0, 1, 1)
+    stage2(0, 2, 1)
+    turn_out("NA", "SN", 0)
+
+    def via_load():
+        for gg in range(2):
+            dma("s", T.XS[16 * gg:128:32, 0:V], T.NA[:, gg], [("NA",)], [("XS", gg * H, (gg + 1) * H)])
+
+    def via_gather(ls, h):
+        act(("VO", h * H, (h + 1) * H), ("XS", 0, WN), F.Identity, lst=(ls, 80 * h, 80 * (h + 1)))
+
+    def via_turn(h, a_old):
+        mm(("K3", 80 * h, 80 * (h + 1)), [(("NID", 0, 128), half(a_old, 80 * h, 80 * (h + 1)))]
+           + [(("BV", 15 - i, 143 - i), ("VO", h * H + i, (h + 1) * H, 16)) for i in range(16)])
+
+    via_load()
+    evac(1)
+    field_s_act(1, C, 3 * C)
+    sel(1, 0, 6)
+    sel(1, 1, 4)
+
+    U = ("U0", "U1", "U2", "U3")
+    W = ("W0", "W1", "W2", "W0")
+    LA = ("LS0", "LS0", "LS1", "LS2")
+    PCH = ((0, NB), (NB, H), (H, V))
+    SGB = 1.75 + 2.0 ** -23
+
+    def p_op(k, a, b):
+        gtt(("P", a, b), (U[k], 0, WN), (LA[k], a // 16, b // 16), ("UL", a, b))
+
+    def u_op(k, a, b):
+        act((U[k + 1], a, b), ("P", a, b), F.Abs, -2.0, 1.0)
+
+    def s_op(a, b):
+        act(("SP", a, b), ("P", a, b), F.Identity, -2.0, 1.0)
+
+    def sg_op(k, a, b, to=None):
+        e = 1.0 if k % 2 else -1.0
+        act((to or "SG%d" % (k + 1), a, b), ("P", a, b), F.Sign, -3.5 * e, SGB * e)
+
+    def bus(k):
+        p_op(k, 0, NB)
+        u_op(k, 0, NB)
+        sg_op(k, 0, NB, "SB")
+        stage("DU%d" % (k + 1), T[U[k + 1]], [(U[k + 1], 0, NB)])
+        stage("DG%d" % (k + 1), T.SB, [("SB", 0, NB)])
+        send("u%d" % (k + 1), ["DU%d" % (k + 1)], U[k + 1], [("W0", V, WN)] if k == 1 else [])
+        send("c%d" % (k + 1), ["DG%d" % (k + 1), "DG%d" % k], "SG%d" % k)
+
+    def cross(k, h):
+        o, i, a, b = "SG%d" % (k - 1), "SG%d" % k, h * H, (h + 1) * H
+        op("g", lambda: g.dma_start(buf(o)[:, a:b], buf(i)[:, a:b], accum_op=A.add), [(i, a, b), (o, a, b)], [(o, a, b)], kind="d")
+
+    def rest(k):
+        for h in range(2):
+            u_op(k, *PCH[h + 1])
+            own_copy(k + 1, h * H, (h + 1) * H)
+        for h in range(2):
+            sg_op(k, h * H, (h + 1) * H)
+            cross(k + 1, h)
+
+    def th_op(k, c):
+        gtt(("TH", 2048 * c + TC * k, 2048 * c + TC * (k + 1)), (W[k], 0, WN), (LA[k], 32 * c, 32 * (c + 1)), ("SP", TC * c, TC * (c + 1)))
+
+    def w_op(k, c):
+        out = (W[k + 1] if k < 3 else "VO", TC * c, TC * (c + 1))
+        win = ("TH", 2048 * c, 2048 * c + TC * (k + 1))
+        f, s = (F.Sigmoid, 4.0) if k < 3 else (F.Tanh, 2.0)
+        lst = None if k == 0 else ("LS%d" % k, 2 * C + 32 * c, 2 * C + 32 * (c + 1))
+        if (k, c) == (2, 4):
+            act(("VO", out[1], out[2]), win, F.Tanh, 2.0, 0.0, lst=lst)
+            act(out, ("VO", out[1], out[2]), F.Identity, 0.5, 0.5)
+        else:
+            act(out, win, f, s, 0.0, lst=lst)
+        if c == 0 and k < 3:
+            stage("DW%d" % (k + 1), T[W[k + 1]], [(W[k + 1], 0, NB)])
+            send("w%d" % (k + 1), ["DW%d" % (k + 1)], W[k + 1])
+        if k == 3:
+            dma("s", T.y[:, TC * c:TC * (c + 1)], T.VO[:, TC * c:TC * (c + 1)], [out], [])
+
+    def prod(k, h):
+        gtt(("PRD%d" % k, h * H, (h + 1) * H), ("SG%d" % (k - 1), 0, WN), (LA[k], C + 80 * h, C + 80 * (h + 1)), ("SG%d" % k, h * H, (h + 1) * H))
+        mm(("K2", 80 * h, 80 * (h + 1)), [(("BZ", 15 - i, 143 - i), ("PRD%d" % k, h * H + i, (h + 1) * H, 16)) for i in range(16)])
+
+    I, NI, IB, IB16, IBL = (("ID", 0, 128), ("NID", 0, 128), ("IB", 0, 128), ("IB16", 0, 128), ("IBL", 0, 128))
+    sl = lambda n, j: (n, j * C, (j + 1) * C)
+
+    def flags(k):
+        fl = "FL%d" % k
+        if k < 3:
+            ts(sl(fl, 0), sl("K2", 0), 3.0, A.is_ge)
+        ts(sl(fl, 1), sl("K2", 0), 9.0, A.is_ge)
+        ts(sl(fl, 2), sl("K2", 0), -7.0, A.is_le)
+        if k < 3:
+            tt(sl(fl, 3), sl(fl, 0), sl(fl, 1), A.subtract)
+
+    bus(0)
+    p_op(0, *PCH[1])
+    field_s(1, C, 3 * C)
+    s_op(0, H)
+    pickd(1, 0, 6)
+    p_op(0, *PCH[2])
+    stage2(1, 0, 0)
+    sel(1, 2, 6)
+    s_op(H, V)
+    pickd(1, 1, 4)
+    stage2(1, 1, 0)
+    th_op(0, 0)
+    pickd(1, 2, 6)
+    stage2(1, 2, 0)
+    w_op(0, 0)
+    rest(0)
+    field_t(0)
+    for c in range(1, 5):
+        th_op(0, c)
+    cp(("LS0", C, 2 * C), ("TN", 0, C))
+    mm(sl("K4", 2), [(I, sl("SN", 2)), (NI, sl("SN", 1))])
+    mm(sl("K5", 0), [(I, sl("TN", 1)), (NI, sl("TN", 0))])
+    mm(sl("K5", 1), [(I, sl("TN", 2)), (NI, sl("TN", 1))])
+
+    for k in (1, 2):
+        fl, pr, ls = "FL%d" % k, "PR%d" % k, "LS%d" % k
+        a_old, b_old = (sl("SN", 0), sl("TN", 0)) if k == 1 else (sl("AB", 0), sl("AB", 1))
+        bus(k)
+        via_gather(LA[k], 0)
+        via_turn(0, a_old)
+        p_op(k, *PCH[1])
+        via_gather(LA[k], 1)
+        via_turn(1, a_old)
+        p_op(k, *PCH[2])
+        for c in range(1, 5):
+            w_op(k - 1, c)
+        s_op(0, H)
+        if k == 1:
+            mm(sl("K4", 1), [(I, sl("SN", 1)), (NI, a_old)])
+        else:
+            mm(sl("K4", 1), [(I, sl("SN", 1)), (I, sl("PR1", 2)), (NI, a_old)])
+            mm(sl("K5", 0), [(I, sl("TN", 1)), (I, sl("PR1", 4)), (NI, b_old)])
+        mm(sl("K6", 0), [(I, a_old)], True, False)
+        mm(sl("K7", 0), [(I, b_old)], True, False)
+        mm(sl("K0", 0), [(I, sl("BK", k - 1))], True, False)
+        prod(k, 0)
+        prod(k, 1)
+        s_op(H, V)
+        rest(k)
+        th_op(k, 0)
+        flags(k)
+        th_op(k, 1)
+        tt(sl(pr, 1), sl("K4", 1), sl(fl, 1), A.mult)
+        tt(sl(pr, 0), sl("K3", 0), sl(fl, 3), A.mult)
+        tt(sl(pr, 3), sl("K5", 0), sl(fl, 2), A.mult)
+        if k == 2:
+            tt(sl(fl, 4), sl(fl, 2), sl("FL1", 2), A.mult)
+        mm(sl("K6", 0), [(I, sl(pr, 1)), (I, sl(pr, 0))], False, True)
+        mm(sl("K7", 0), [(I, sl(pr, 3))], False, True)
+        mm(sl("K0", 0), [(IBL, sl(fl, 2))] + ([(IBL, sl(fl, 4))] if k == 2 else []), False, True)
+        if k == 1:
+            tt(sl(pr, 2), sl("K4", 2), sl(fl, 1), A.mult)
+            tt(sl(pr, 4), sl("K5", 1), sl(fl, 2), A.mult)
+        th_op(k, 2)
+        ts(sl(ls, 0), sl("K6", 0), OFF, A.add)
+        cp(sl(ls, 1), sl("K7", 0))
+        cp(sl(ls, 2), sl("K0", 0))
+        if k == 1:
+            act(sl("AB", 0), sl("K6", 0), F.Identity)
+            act(sl("AB", 1), sl("K7", 0), F.Identity)
+        w_op(k, 0)
+        th_op(k, 3)
+        if k == 1:
+            turn_out("NA", "AB", 0)
+            via_load()
+        th_op(k, 4)
+
+    p_op(3, 0, H)
+    p_op(3, H, V)
+    for c in range(1, 5):
+        w_op(2, c)
+    s_op(0, H)
+    s_op(H, V)
+    prod(3, 0)
+    prod(3, 1)
+    th_op(3, 0)
+    flags(3)
+    tt(sl("FL3", 3), sl("FL3", 2), sl("FL2", 2), A.mult)
+    tt(sl("FL3", 4), sl("FL3", 2), sl("FL2", 4), A.mult)
+    mm(sl("K0", 0), [(I, sl("BK", 2))], True, False)
+    mm(sl("K0", 0), [(IBL, sl("FL3", 2)), (IBL, sl("FL3", 3)), (IBL, sl("FL3", 4))], False, True)
+    mm(sl("K1", 0), [(IB, sl("CB", 0))] + [(IB, sl("FL%d" % k, 1)) for k in (1, 2, 3)])
+    mm(sl("K1", 1), [(IB, sl("CB", 0))] + [(IB16, sl("FL%d" % k, 2)) for k in (1, 2, 3)])
+    th_op(3, 1)
+    cp(sl("LS3", 2), sl("K0", 0))
+    cp(("QI", 0, 2 * C), ("K1", 0, 2 * C))
+    w_op(3, 0)
+    w_op(3, 1)
+    th_op(3, 2)
+    ts(sl("QI", 2), sl("QI", 0), 15, A.bitwise_and)
+    ts(sl("QI", 3), sl("QI", 1), 240, A.bitwise_and)
+    w_op(3, 2)
+    th_op(3, 3)
+    tt(sl("QF", 0), sl("QI", 2), sl("QI", 3), A.add)
+    w_op(3, 3)
+    for j in range(2):
+        a, b = 4 * TC + 256 * j, 4 * TC + 256 * (j + 1)
+        gtt(("TH", 8192 + 3 * TC + 256 * j, 8192 + 3 * TC + 256 * (j + 1)), (W[3], 0, WN), (LA[3], a // 16, b // 16), ("SP", a, b))
+        act(("VO", a, b), ("TH", 8192, 8192 + 3 * TC + 256 * (j + 1)), F.Tanh, 2.0, 0.0, lst=("LS3", 2 * C + a // 16, 2 * C + b // 16))
+        dma("s", T.y[:, a:b], T.VO[:, a:b], [("VO", a, b)], [])
+    turn_out("NQ", "QF", 0)
+    for gg in range(2):
+        dma("a", T.q[gg:8:2, :], T.NQ[:, gg], [("NQ",)], [])
+    return ops
+
+
+def conflict(o, e):
+    q = o["q"]
+    for (mine, theirs, ww) in ((o["rd"], e["wr"], 0), (o["wr"], e["wr"], 1), (o["wr"], e["rd"], 0), (o["rd"], e["rd"], 2)):
+        for x in mine:
+            for y in theirs:
+                if x[0] != y[0]:
+                    continue
+                if x[0][0] == "K" and e["q"] != q:
+                    return True
+                if ww == 2 or (ww == 1 and o.get("par") and e.get("par") and e["q"] == q and e["rd"] == o["rd"]):
+                    continue
+                if x[1] < y[2] and y[1] < x[2]:
+                    return True
+    return False
+
+
+def emit(g, T, ops):
+    Q = {"v": g.vector, "a": g.scalar, "t": g.tensor, "g": g, "s": g.sync}
+    esem = {"v": "e_v", "a": "e_a", "t": "e_t", "g": "e_g"}
+    known = {q: {} for q in Q}
+    count = {}
+    nd = [0]
+    done = []
+    for o in ops:
+        q = o["q"]
+        if o["kind"] == "arr":
+            o["sig"], o["clock"] = ("arr_" + o["x"], 2 * (N - 1)), {}
+            count[o["sig"][0]] = o["sig"][1]
+            done.append(o)
+            continue
+        for e in reversed(done):
+            s, n = e["sig"]
+            if known[q].get(s, 0) >= n:
+                continue
+            if conflict(o, e):
+                Q[q].wait_ge(T.sem[s], n)
+                known[q][s] = n
+                for s2, n2 in e["clock"].items():
+                    if known[q].get(s2, 0) < n2:
+                        known[q][s2] = n2
+        ins = o["fn"]()
+        if o["kind"] == "c":
+            s = esem[q]
+            count[s] = count.get(s, 0) + 1
+            ins.then_inc(T.sem[s], 1)
+        elif o["kind"] == "d":
+            s = "d%d" % nd[0]
+            nd[0] += 1
+            count[s] = 16
+            ins.then_inc(T.sem[s], 16)
+        else:
+            s = "out_" + o["x"]
+            count[s] = 2 * (N - 1)
+        o["sig"], o["clock"] = (s, count[s]), dict(known[q])
+        done.append(o)
+    for s, n in count.items():
+        if max(known[q].get(s, 0) for q in Q) < n:
+            g.sync.wait_ge(T.sem[s], n)
+
+
+def rank_program(g, core, T, topo):
+    if T.rank_of(core) is None:
+        return
+    ops = build(g, core, T, topo)
+    emit(g, T, ops if ORDER is None else [ops[j] for j in ORDER])

@@ -2,57 +2,70 @@ from concourse.bass import DstId, RemoteDMATransfer
 from concourse.mybir import AluOpType, ActivationFunctionType
 
 V, NB, WN, N = 2560, 128, 3456, 8
-C = V // 16
-OFF = 1720.0
-MAGIC = 12582912.0
+C, H, HC = V // 16, V // 2, V // 32
+OFF = 1728.0
+HB = (0, WN, 2 * WN, 2 * WN + V)
 TC = 512
 
 SCRATCH = {}
 for _n, _w, _d in [
-    ("PT", V, "int32"), ("XS", WN, "float32"), ("P", V, "float32"), ("S0", WN, "bfloat16"), ("UL", V, "float32"), ("SB", NB, "bfloat16"),
-    ("U1", WN, "float32"), ("U2", WN, "float32"), ("U3", WN, "float32"),
-    ("W0", WN, "float32"), ("W1", WN, "float32"), ("W2", WN, "float32"),
-    ("SG0", WN, "bfloat16"), ("SG1", WN, "bfloat16"),
-    ("TH", 4 * V, "float32"), ("SP", V, "float32"), ("VO", V, "float32"),
-    ("CW", C, "float32"), ("CI", C, "int32"), ("C3", 2 * C, "int32"), ("MW", 512, "bfloat16"), ("LM", 32, "uint16"),
-    ("CB", C, "bfloat16"), ("LC", C, "uint16"), ("IOT", 160, "float32"), ("PI", 8, "int32"), ("PJ", 8, "int32"),
-    ("PF", 16, "float32"), ("M3I", 16, "int32"), ("M3J", 16, "int32"), ("M3", 16, "float32"),
-    ("B1", 144, "float32"), ("B2", 144, "float32"), ("BV", 144, "float32"), ("ID", 128, "float32"), ("NID", 128, "float32"),
-    ("BZ", 144, "bfloat16"), ("BT0", 144, "bfloat16"), ("BT1", 144, "bfloat16"), ("BT2", 144, "bfloat16"), ("BT3", 144, "bfloat16"),
-    ("IB", 128, "bfloat16"), ("IB16", 128, "bfloat16"), ("IBL", 128, "bfloat16"),
-    ("SN", 3 * C, "float32"), ("TN", 3 * C, "float32"),
-    ("LS0", 2 * C, "uint16"), ("LS1", 3 * C, "uint16"), ("LS2", 3 * C, "uint16"),
-    ("AB", 2 * C, "float32"), ("FL1", 4 * C, "bfloat16"), ("FL2", 5 * C, "bfloat16"), ("FL3", 5 * C, "bfloat16"),
-    ("PR1", 5 * C, "float32"), ("BK", 3 * C, "float32"), ("BC", C, "float32"),
+    ("PT", V, "int32"), ("P0", V, "float32"), ("P1", V, "float32"), ("UL", V, "float32"), ("G", V, "float32"),
+    ("U1", WN, "float32"), ("U2", WN, "float32"), ("U3", WN, "float32"), ("TH", HB[3] + V, "float32"),
+    ("S0", WN, "bfloat16"), ("U0", WN, "bfloat16"), ("SG0", WN, "bfloat16"), ("SG1", WN, "bfloat16"), ("SG2", WN, "bfloat16"),
+    ("SG3", V, "bfloat16"), ("PRD", V, "bfloat16"), ("VO", V, "bfloat16"), ("SB", NB, "bfloat16"), ("TB", NB, "float32"),
+    ("BH", 256, "bfloat16"), ("ONE", TC, "bfloat16"), ("CK", 5 * C, "bfloat16"),
+    ("CB", C, "bfloat16"), ("CI", C, "int32"), ("C3", 3 * C, "int32"), ("C3B", 3 * C, "bfloat16"), ("OH", 8 * C, "bfloat16"),
+    ("MW", 512, "bfloat16"), ("LM", 32, "uint16"), ("LC", C, "uint16"),
+    ("IOT", 160, "float32"), ("PI", 8, "int32"), ("PJ", 8, "int32"), ("PF", 16, "float32"),
+    ("M3I", 16, "int32"), ("M3J", 16, "int32"), ("M3", 16, "float32"),
+    ("B1", 144, "float32"), ("ID", 128, "float32"), ("N2I", 128, "float32"), ("B2", 144, "float16"), ("NB2", 144, "float16"), ("N2B2", 144, "float16"),
+    ("B2B", 144, "bfloat16"), ("BZ", 144, "bfloat16"), ("BV", 144, "bfloat16"), ("BL", 144, "bfloat16"),
+    ("BT0", 144, "bfloat16"), ("BT1", 144, "bfloat16"), ("BT2", 144, "bfloat16"), ("BT3", 144, "bfloat16"),
+    ("IB", 128, "bfloat16"), ("NIB", 128, "bfloat16"), ("IB16", 128, "bfloat16"), ("IBL", 128, "bfloat16"),
+    ("EX0", 4 * C, "float16"), ("EX1", 4 * C, "float16"),
+    ("E00", 4 * C, "float16"), ("E01", 4 * C, "float16"), ("E10", 4 * C, "float16"), ("E11", 4 * C, "float16"),
+    ("LS0", 2 * C, "uint16"), ("LS1", 2 * C + 8, "uint16"), ("LS2", 3 * C, "uint16"), ("LS3", C, "uint16"), ("LG", C, "uint16"),
+    ("F0", C, "bfloat16"), ("WR", 2 * C, "bfloat16"), ("PR1", 5 * C, "float32"), ("PR2", 4 * C, "float32"), ("PR3", C, "float32"),
+    ("BC", C, "float32"), ("BK", C, "float32"), ("HI", C, "float32"), ("HF", H, "bfloat16"), ("P2I", 128, "float32"),
 ]:
     SCRATCH[_n] = ("sbuf", [128, _w], _d)
+for _k in range(4):
+    SCRATCH["FL%d" % _k] = ("sbuf", [128, 5, C], "bfloat16")
 SCRATCH["CN"] = ("sbuf", [128, 2, 5, 16], "int32")
-for _n in ("NF", "NA", "NQ"):
-    SCRATCH[_n] = ("sbuf", [128, 2, 5, 16], "float32")
+SCRATCH["NF"] = ("sbuf", [128, 2, 5, 16], "bfloat16")
+SCRATCH["NQ"] = ("sbuf", [128, 2, 5, 16], "float32")
+SCRATCH["NA"] = ("sbuf", [128, 3, 2, 5, 16], "bfloat16")
 for _k in range(8):
-    SCRATCH["K%d" % _k] = ("psum", [128, 512], "float32")
-for _n in ("DU1", "DU2", "DU3", "DW1", "DW2", "DW3"):
+    SCRATCH["K%d" % _k] = ("psum", [128, TC], "float32")
+for _n in ("DU1", "DU2", "DU3", "DT1", "DT2", "DW3"):
     SCRATCH[_n] = ("dram", [256, NB], "float32")
-for _n in ("DS0", "DG0", "DG1", "DG2", "DG3"):
+for _n in ("DS0", "DU0", "DG1", "DG2", "DG3"):
     SCRATCH[_n] = ("dram", [256, NB], "bfloat16")
 
-XCH = ["s0", "u1", "u2", "u3", "c1", "c2", "c3", "w1", "w2", "w3"]
-SEMAPHORES = (["e_v", "e_a", "e_t", "e_g"] + ["d%d" % _k for _k in range(70)] + ["arr_" + _x for _x in XCH]
+XCH = ["s0", "u0", "u1", "u2", "u3", "c1", "c2", "c3", "t1", "t2", "w3"]
+SEMAPHORES = (["e_v", "e_a", "e_t", "e_g"] + ["d%d" % _k for _k in range(60)] + ["arr_" + _x for _x in XCH]
               + ["out_" + _x for _x in XCH])
 
-ALIAS = {"SG2": ("S0", 0), "SG3": ("SG0", 0), "OH": ("SG1", 1280), "MG": ("TH", 8192 + TC), "MT": ("TH", 8192 + TC),
-         "MH": ("TH", 8192 + TC + 640), "PR2": ("PR1", 0), "PRD1": ("S0", 0), "PRD2": ("SG0", 0), "PRD3": ("SG1", 0),
-         "U0": ("U3", 0), "LS3": ("LS0", -2 * C), "QI": ("PT", 0), "QF": ("CW", 0), "C3B": ("SG1", 0)}
+ALIAS = {"XS": ("U0", 0), "UL0": ("SG3", 0), "W3": ("U1", 0), "SP": ("U2", 0), "YO": ("P0", 0), "SR": ("TH", HB[3])}
 
-ORDER = [7, 17, 1, 9, 19, 0, 18, 8, 14, 16, 15, 28, 21, 20, 30, 23, 22, 25, 35, 27, 29, 26, 45, 49, 50, 36, 2, 46, 47, 48, 12, 5, 51, 54, 56, 52, 70, 6, 31, 58, 59, 57, 55, 40, 3, 60, 76, 74, 4, 61, 34, 62, 64, 66, 67, 63, 69, 109, 24, 65, 77, 10, 68, 71, 78, 41, 37, 110, 80, 91, 79, 88, 89, 81, 92, 42, 11, 83, 82, 72, 93, 101, 94, 95, 96, 104, 105, 106, 122, 121, 73, 103, 124, 107, 123, 125, 127, 90, 102, 86, 140, 151, 108, 141, 98, 144, 143, 118, 142, 75, 145, 97, 113, 117, 85, 146, 175, 179, 116, 87, 112, 126, 84, 111, 115, 153, 176, 129, 135, 133, 156, 13, 132, 119, 128, 134, 154, 166, 147, 158, 180, 100, 162, 99, 148, 159, 177, 187, 114, 155, 137, 38, 33, 186, 139, 138, 170, 161, 178, 149, 171, 136, 160, 181, 172, 44, 188, 120, 130, 167, 193, 163, 168, 150, 195, 198, 194, 131, 197, 164, 212, 209, 182, 207, 199, 157, 196, 169, 32, 185, 206, 165, 183, 173, 210, 184, 208, 200, 216, 189, 219, 201, 226, 227, 192, 191, 214, 211, 221, 218, 213, 152, 220, 222, 174, 237, 234, 235, 233, 204, 223, 230, 232, 43, 202, 190, 203, 243, 215, 236, 245, 265, 249, 224, 228, 225, 244, 231, 252, 253, 254, 257, 285, 238, 205, 239, 241, 217, 240, 242, 246, 247, 250, 288, 286, 292, 282, 266, 268, 248, 229, 259, 260, 290, 271, 267, 261, 272, 251, 262, 258, 297, 264, 284, 263, 269, 279, 287, 295, 270, 283, 296, 255, 289, 256, 293, 294, 309, 308, 275, 280, 314, 304, 305, 312, 302, 39, 276, 303, 315, 53, 319, 291, 306, 273, 317, 321, 274, 318, 281, 329, 277, 322, 278, 323, 325, 324, 298, 307, 299, 328, 334, 311, 310, 339, 313, 300, 341, 332, 316, 320, 301, 340, 342, 330, 345, 351, 333, 344, 331, 335, 336, 347, 337, 348, 326, 327, 338, 350, 354, 346, 343, 349, 353, 359, 364, 355, 362, 366, 356, 368, 363, 369, 367, 370, 352, 360, 361, 357, 358, 371, 372, 365, 374, 373, 376, 378, 377, 375, 379, 380]
+PAR = dict(cyc=0.00083 * 1.1, gat=1.4, pe=0.00042 * 1.1, vfix=0.05, afix=0.07, hop=0.06, wake=0.2, dma=1.5, gdma=1.8, far=1.6, first=3.4,
+           rate=6.0e5, row=0.015, farrate=3.0e4, slack=(0.07, 0.15, 0.25), lam=8.0, tries=25000, sort=100, give=0.0005, use=(0, 1, 3, 4), gis=0.5, ris=0.75, wt=128, rounds=4, sgv=0,
+           alt="w0 sp11 sp14 sr0 sr1 sb0 sb1 sb2 oc10 oc11 oc20 oc21 oc30 oc31")
+CASES = [dict(), dict(gat=1.3, dma=1.1, gdma=1.4, far=1.1, row=0.005, farrate=3.8e4, gis=0.9, ris=1.3, wake=0.15),
+         dict(gat=1.3, dma=1.6, gdma=2.0, far=2.0, row=0.025, farrate=2.5e4, wake=0.3, first=4.4),
+         dict(gat=1.3, dma=2.2, gdma=2.8, far=4.0, row=0.008, farrate=3.5e4, wake=0.5, first=7.4),
+         dict(cyc=0.00083 * 1.35, pe=0.00042 * 1.35, gat=1.9), dict(cyc=0.00083 * 1.35, pe=0.00042 * 1.35, gat=1.15)]
+LOG = []
+ORDER = {}
 
 A = AluOpType
 F = ActivationFunctionType
 
 
-def build(g, core, T, topo):
+def build(g, core, T, topo, PAR):
     rank = T.rank_of(core)
     ops = []
+    ALT = PAR["alt"].split()
 
     def real(x):
         if x[0] not in ALIAS:
@@ -60,74 +73,94 @@ def build(g, core, T, topo):
         n, o = ALIAS[x[0]]
         return (n, x[1] + o, x[2] + o) + tuple(x[3:])
 
-    def buf(n):
-        return T[ALIAS[n][0]] if n in ALIAS else T[n]
-
     def ap(x):
         if len(x) == 1:
             return T[x[0]][:]
         x = real(x)
+        if x[0][:2] == "FL":
+            j, a, b = x[1] // C, x[1] % C, x[2] - x[1] // C * C
+            return T[x[0]][:, j, a:b] if b <= C else T[x[0]][:, j:x[2] // C, :]
+        if x[-1] == "row":
+            return T[x[0]][0:1, x[1]:x[2]]
         if len(x) == 3:
             return T[x[0]][:, x[1]:x[2]]
         return T[x[0]][:, x[1]:x[2]:x[3]]
 
+    def width(x):
+        return C if len(x) == 1 else len(range(x[1], x[2], x[3] if len(x) > 3 and x[3] != "row" else 1))
+
+    def size(x):
+        return 4 if SCRATCH[real(x)[0] if len(x) > 1 else x[0]][2] in ("float32", "int32") else 2
+
     def reg(x):
         return (x[0], 0, 1 << 20) if len(x) == 1 else real(x)[:3]
 
-    def op(q, fn, rd, wr, kind="c", **kw):
-        ops.append(dict(q=q, fn=fn, rd=[reg(x) for x in rd], wr=[reg(x) for x in wr], kind=kind, **kw))
+    def op(q, fn, rd, wr, dur, kind="c", **kw):
+        ops.append(dict(q=q, fn=fn, rd=[reg(x) for x in rd], wr=[reg(x) for x in wr], kind=kind, dur=dur, **kw))
+
+    def vdur(n, c):
+        return PAR["vfix"] + max(64, n * c) * PAR["cyc"]
 
     def sc(s):
         return ap(s) if isinstance(s, tuple) else s
 
     def ts(out, x, s1, o0, s2=None, o1=None):
         rd = [x] + [s for s in (s1, s2) if isinstance(s, tuple)]
+        d = vdur(width(x), max(size(out), size(x)) / 4)
         if o1 is None:
-            op("v", lambda: g.vector.tensor_scalar(ap(out), ap(x), sc(s1), None, o0), rd, [out])
+            op("v", lambda: g.vector.tensor_scalar(ap(out), ap(x), sc(s1), None, o0), rd, [out], d)
         else:
-            op("v", lambda: g.vector.tensor_scalar(ap(out), ap(x), sc(s1), sc(s2), o0, o1), rd, [out])
+            op("v", lambda: g.vector.tensor_scalar(ap(out), ap(x), sc(s1), sc(s2), o0, o1), rd, [out], d)
 
     def tt(out, x, y, o):
-        op("v", lambda: g.vector.tensor_tensor(ap(out), ap(x), ap(y), o), [x, y], [out])
+        op("v", lambda: g.vector.tensor_tensor(ap(out), ap(x), ap(y), o), [x, y], [out], vdur(width(x), 1))
 
     def cp(out, x):
-        op("v", lambda: g.vector.tensor_copy(ap(out), ap(x)), [x], [out])
+        op("v", lambda: g.vector.tensor_copy(ap(out), ap(x)), [x], [out], vdur(width(x), max(size(out), size(x)) / 4))
+
+    def fill(out, c):
+        op("v", lambda: g.vector.memset(ap(out), c), [], [out], vdur(width(out), size(out) / 4))
 
     def gtt(out, win, lst, y):
-        op("v", lambda: g.vector.tensor_tensor(ap(out), ap(win).indirect(ap(lst)), ap(y), A.mult), [win, lst, y], [out])
+        op("v", lambda: g.vector.tensor_tensor(ap(out), ap(win).indirect(ap(lst)), ap(y), A.mult), [win, lst, y], [out], vdur(width(out), PAR["gat"]))
 
     def act(out, x, f, scale=1.0, bias=0.0, lst=None):
+        d = PAR["afix"] + max(64, width(out) * (1 if lst is None else PAR["gat"])) * PAR["cyc"]
         if lst is None:
             op("a", lambda: g.scalar.activation(ap(out), ap(x), f, bias=sc(bias), scale=sc(scale)),
-               [x] + [s for s in (scale, bias) if isinstance(s, tuple)], [out])
+               [x] + [s for s in (scale, bias) if isinstance(s, tuple)], [out], d, f=f)
         else:
-            op("a", lambda: g.scalar.activation(ap(out), ap(x).indirect(ap(lst)), f, bias=bias, scale=scale), [x, lst], [out])
+            op("a", lambda: g.scalar.activation(ap(out), ap(x).indirect(ap(lst)), f, bias=bias, scale=scale), [x, lst], [out], d, f=f)
 
-    def mm(out, terms, first=True, last=True):
+    def mm(terms, first=True, last=True):
         def fn():
             ins = None
-            for j, (l, r) in enumerate(terms):
-                ins = g.tensor.matmul(ap(out), ap(l), ap(r), first and j == 0, last and j == len(terms) - 1)
+            for j, (o, l, r) in enumerate(terms):
+                ins = g.tensor.matmul(ap(o), ap(l), ap(r), first and j == 0, last and j == len(terms) - 1)
             return ins
-        op("t", fn, [x for t in terms for x in t], [out])
+        d = sum(max(64, width(r)) * (4 if size(r) == 4 else 1) * PAR["pe"] + 0.005 for o, l, r in terms)
+        op("t", fn, [x for t in terms for x in t[1:]], [t[0] for t in terms], d)
 
     def iota(out, pat, base, cm, flt):
+        d = 0.13 + 2 * width(out) * PAR["cyc"]
         if flt:
-            op("g", lambda: g.iota(ap(out), pat, base, cm, allow_small_or_imprecise_dtypes=True), [], [out])
+            op("g", lambda: g.iota(ap(out), pat, base, cm, allow_small_or_imprecise_dtypes=True), [], [out], d)
         else:
-            op("g", lambda: g.iota(ap(out), pat, base, cm), [], [out])
+            op("g", lambda: g.iota(ap(out), pat, base, cm), [], [out], d)
 
-    def dma(q, o, i, rd, wr):
+    def dma(pairs, rd, wr, nbytes, q="s"):
         e = g.sync if q == "s" else g.scalar
-        op(q, lambda: e.dma_start(o, i), rd, wr, kind="d")
+        op(q, lambda: [e.dma_start(o, i) for o, i in pairs], rd, wr, 0.06 * len(pairs), kind="d", lat=PAR["dma"],
+           busy=8 * len(pairs) * PAR["row"] + nbytes / PAR["rate"])
 
-    def turn_in(out, src):
-        for b in range(5):
-            op("v", lambda b=b: g.vector.transpose(T[out][:, b:C:5], T[src][:, :, b, :]), [(src,)], [(out, 0, C)], par=1)
+    def add(x, o, i, rd, nbytes):
+        first = not any(e["q"] == "g" and e["kind"] == "d" for e in ops)
+        op("g", lambda: [g.dma_start(o, i, accum_op=A.add)], rd + [x], [x], PAR["gis"] + (1.5 if first else 0), kind="d",
+           lat=PAR["gdma"], busy=1.5 * nbytes / PAR["rate"])
 
-    def turn_out(out, src, c0):
+    def turn(out, src, rd, wr, n):
         for b in range(5):
-            op("v", lambda b=b: g.vector.transpose(T[out][:, :, b, :], buf(src)[:, c0 + b:c0 + C:5]), [(src, c0, c0 + C)], [(out,)], par=1)
+            op("v", lambda b=b: g.vector.transpose(out(b), src(b)), [rd], [wr], vdur(n, size(rd) / 4), par=1)
 
     peers = [T.cores[(rank + d) % N] for d in range(1, N)]
     masks, nxt = [], [0, 0]
@@ -138,361 +171,395 @@ def build(g, core, T, topo):
         nxt[far] += 1
         masks.append((1 << e[j]) | (1 << e[j + 2]))
 
-    def stage(dn, src_ap, rd):
-        dma("s", T[dn][16:128, :], src_ap[16:128, 0:NB], rd, [(dn, 0, 1)])
-        dma("s", T[dn][128:240, :], src_ap[0:112, 0:NB], rd, [(dn, 1, 2)])
+    def share(x, dn, src, win, c0, after=()):
+        s, s0 = T[src[0]], src[1]
+        dma([(T[dn][16:128, :], s[16:128, s0:s0 + NB]), (T[dn][128:240, :], s[0:112, s0:s0 + NB])],
+            [] if src[0] == "s0" else [(src[0], s0, s0 + NB)], [(dn,)], 1e5)
 
-    def send(x, dns, win, after=()):
         def fn():
             trs = []
             for d in range(1, N):
                 rid, pid, _se = topo.addr(peers[d - 1])
                 r0 = 16 * ((d * (d + 1) // 2) % 8)
-                dst = buf(win)[:, V + (d - 1) * NB:V + d * NB]
-                kw = dict(dst_ids=[DstId(rid=rid, pnc=pid)], dma_engine_mask=masks[d - 1], remote_sem=T.sem["arr_" + x])
-                if len(dns) == 1:
-                    trs.append(RemoteDMATransfer(src=T[dns[0]][r0:r0 + 128, :], dst=dst, **kw))
-                else:
-                    trs.append(RemoteDMATransfer(srcs=[T[n][r0:r0 + 128, :] for n in dns], dsts=[dst], alu_op=1, **kw))
+                trs.append(RemoteDMATransfer(src=T[dn][r0:r0 + 128, :], dst=T[win][:, c0 + (d - 1) * NB:c0 + d * NB],
+                                             dst_ids=[DstId(rid=rid, pnc=pid)], dma_engine_mask=masks[d - 1], remote_sem=T.sem["arr_" + x]))
             return g.remote_dma_fused(trs, local_sem=T.sem["out_" + x])
-        op("g", fn, [(n,) for n in dns] + list(after), [("X" + x,)], kind="r", x=x)
-        ops.append(dict(q=None, kind="arr", x=x, rd=[reg(("X" + x,))], wr=[reg((win, V, WN))]))
+        op("g", fn, [(dn,)] + list(after), [("X" + x,)], PAR["ris"], kind="r", x=x, lat=PAR["far"], once=PAR["first"] if x == "s0" else 0.0,
+           busy=64 * (PAR["row"] + NB * size((dn,)) / PAR["farrate"]))
+        ops.append(dict(q=None, kind="arr", x=x, rd=[reg(("X" + x,))], wr=[(win, c0, c0 + WN - V)], dur=0.0))
 
-    H = V // 2
-    for gg in range(2):
-        dma("s", T.CN[:, gg], T.cur[gg:8:2, :], [], [("CN", gg, gg + 1)])
-    dma("s", T.PT[:, 0:H], T.pt[:, 0:H], [], [("PT", 0, H)])
-    stage("DS0", T.s0, [])
-    dma("s", T.S0[:, 0:V], T.s0[:, :], [], [("S0", 0, V)])
-    dma("s", T.PT[:, H:V], T.pt[:, H:V], [], [("PT", H, V)])
+    dma([(T.CN[:, gg], T.cur[gg:8:2, :]) for gg in range(2)], [], [("CN",)], 8e4)
+    dma([(T.PT[:, 0:H], T.pt[:, 0:H])], [], [("PT", 0, H)], 512 * H)
+    dma([(T.S0[:, 0:V], T.s0[:, :])], [], [("S0", 0, V)], 256 * V)
+    dma([(T.PT[:, H:V], T.pt[:, H:V])], [], [("PT", H, V)], 512 * H)
 
     iota(("PI", 0, 8), [[0, 8]], 0, 1, False)
     iota(("M3I", 0, 16), [[-1, 16]], 16, 1, False)
     iota(("IOT", 0, 160), [[1, 160]], -15, 0, True)
-    send("s0", ["DS0"], "S0")
-    iota(("BC", 0, C), [[0, 5], [16, 32]], TC, 0, True)
-    iota(("XS", V, WN), [[1, WN - V]], V - int(OFF), 0, True)
-    for j, m in enumerate((112, 3, 12, 15, 115, 127)):
+    share("s0", "DS0", ("s0", 0), "S0", V)
+    iota(("BC", 0, C), [[16, C]], HB[2] - int(OFF), 0, True)
+    for x, n in ((0, ("BH", 0, 128)), (1, ("ONE", 0, TC)), (-OFF, ("CK", 0, 2 * C)), (-V, ("CK", 2 * C, 3 * C)), (-6, ("CK", 4 * C, 5 * C))):
+        iota(n, [[0, width(n)]], int(x), 0, True)
+    act(("CK", 3 * C, 3 * C + 128), ("ONE", 0, 128), F.Identity, 2.0 ** -12)
+    row = {1.0: ("ONE", 0), -OFF: ("CK", 0), -float(V): ("CK", 2 * C), -6.0: ("CK", 4 * C)}
+
+    def const(out, x, by=("ONE", 0, 128, "row")):
+        n, c0 = row[x]
+        return (out, by, (n, c0, c0 + width(out)) + by[3:])
+
+    sgn = -1.0 if "pa" in ALT else 1.0
+    if "w0" in ALT:
+        for a, b in ((0, H), (H, V), (V, WN)):
+            if "wd" in ALT:
+                if a == 0:
+                    iota(("G", 0, H), [[0, H]], 1, 0, True)
+                dma([(T.U3[:, a:b], T.G[:, 0:b - a])], [("G", 0, H)], [("U3", a, b)], 512 * (b - a))
+            else:
+                iota(("U3", a, b), [[0, b - a]], 1, 0, True)
+            add(("U3", a, b), T.U3[:, a:b], (T.s0 if a < V else T.S0)[:, a:b], [] if a < V else [("S0", V, WN)], 512 * (b - a))
+    if "pa" in ALT:
+        op("g", lambda: g.affine_select(T.HF[:], T.S0[:, 0:H], [[0, H]], A.not_equal, -0.5, 0, 0), [("S0", 0, H)], [("HF", 0, H)], 0.17 + 2 * H * PAR["cyc"])
+        op("g", lambda: g.affine_select(T.P2I[:], T.BH[:, 0:128], [[-1, 128]], A.not_equal, 2.0, 0, 1), [("BH", 0, 128)], [("P2I", 0, 128)], 0.4)
+    col = lambda j: ("PF", j, j + 1)
+    for j, m in enumerate((112, 3, 15)):
         ts(("PJ", j, j + 1), ("PI", j, j + 1), m, A.bitwise_and)
     ts(("M3J", 0, 16), ("M3I", 0, 16), 15, A.bitwise_and)
-    cp(("PF", 0, 6), ("PJ", 0, 6))
+    cp(("PF", 0, 3), ("PJ", 0, 3))
     ts(("M3", 0, 16), ("M3J", 0, 16), 3.0, A.is_lt)
-    col = lambda j: ("PF", j, j + 1)
-    ts(col(6), col(1), 4.0, A.mult, col(0), A.add)
-    ts(col(7), col(3), 1000.0, A.mult, col(0), A.add)
-    ts(("PF", 8, 12), ("IOT", 15, 31, 4), col(2), A.is_equal)
-    ts(("B1", 0, 144), ("IOT", 12, 156), col(6), A.is_equal)
-    ts(("LM", 0, 16), ("IOT", 15, 31), 0.0, A.mult, col(3), A.add)
+    ts(("LM", 0, 16), ("IOT", 15, 31), 0.0, A.mult, col(2), A.add)
     cp(("LM", 16, 32), ("IOT", 15, 31))
-    act(("MW", 0, 512), ("M3", 0, 16), F.Identity, lst=("LM", 0, 32))
-    ts(("B2", 0, 144), ("IOT", 3, 147), col(4), A.is_equal)
-    ts(("ID", 0, 128), ("IOT", 15, 143), col(5), A.is_equal)
+    act(col(3), col(1), F.Identity, 4.0, col(0))
+    act(col(4), col(1), F.Identity, 1.0, col(0))
+    act(col(6), col(1), F.Identity, -1.0, col(2))
+    act(("MW", 0, 256), ("M3", 0, 16), F.Identity, lst=("LM", 0, 16))
+    act(("MW", 256, 512), ("M3", 0, 16), F.Identity, 2.0 ** -12, lst=("LM", 16, 32))
+    ts(("PF", 8, 12), ("IOT", 15, 31, 4), col(6), A.is_equal)
+    ts(("PF", 12, 15), ("IOT", 15, 27, 4), col(2), A.is_equal)
+    ts(("B1", 0, 144), ("IOT", 12, 156), col(3), A.is_equal)
+    ts(("B2B", 0, 144), ("IOT", 3, 147), col(4), A.is_equal)
+    ts(("B2", 0, 144), ("B2B", 0, 144), 1.0, A.mult)
+    ts(("NB2", 0, 144), ("B2B", 0, 144), -1.0, A.mult)
+    ts(("N2B2", 0, 144), ("B2B", 0, 144), -2.0, A.mult)
     ts(("BZ", 0, 144), ("IOT", 0, 144), col(0), A.is_equal)
-    ts(("BV", 0, 144), ("IOT", 0, 144), col(7), A.is_equal)
+    act(col(12), col(12), F.Identity, -float(WN))
+    act(col(13), col(13), F.Identity, 1.0, col(14))
+    act(("BL", 0, 144), ("BZ", 0, 144), F.Identity, col(12))
+    act(("BV", 0, 144), ("BZ", 0, 144), F.Identity, col(13))
     for t in range(4):
-        act(("BT%d" % t, 0, 144), ("B2", 0, 144), F.Identity, col(8 + t))
-    for n, w in (("NID", -1.0), ("IB", 1.0), ("IB16", 16.0), ("IBL", -float(TC))):
-        act((n, 0, 128), ("ID", 0, 128), F.Identity, w)
-    act(("BK", 0, C), ("BC", 0, C), F.Identity, 1.0, col(3))
-    for k in (1, 2):
-        act(("BK", k * C, (k + 1) * C), ("BK", 0, C), F.Identity, 1.0, float(TC * k))
+        act(("BT%d" % t, 0, 144), ("B2B", 0, 144), F.Identity, col(8 + t))
+    for n, w in (("N2I", -2.0), ("IB", 1.0), ("NIB", -1.0), ("ID", 1.0), ("IBL", -float(WN)), ("IB16", 16.0)):
+        op("g", lambda n=n, w=w: g.affine_select(T[n][:], T.BH[:, 0:128], [[-1, 128]], A.not_equal, w, 0, 1),
+           [("BH", 0, 128)], [(n, 0, 128)], 0.17 + 256 * PAR["cyc"])
+    act(("BK", 0, C), ("BC", 0, C), F.Identity, 1.0, col(2))
+    act(col(7), col(2), F.Identity, 56.0, V - OFF)
+    act(("BH", 128, 128 + 56), ("ONE", 0, 56), F.Identity, col(7))
+    act(("BH", 192, 192 + 56), ("IOT", 15, 15 + 56), F.Identity)
+    I, N2I, IB, NIB, IB16, IBL = ((n, 0, 128) for n in ("ID", "N2I", "IB", "NIB", "IB16", "IBL"))
+    sl = lambda n, j, w=1: (n, j * C, (j + w) * C)
 
     cp(("NF",), ("CN",))
-    turn_in("CW", "NF")
-    cp(("LC", 0, C), ("CW", 0, C))
-    cp(("CI", 0, C), ("CW", 0, C))
-    act(("CB", 0, C), ("CW", 0, C), F.Identity)
-
-    XB = ("XS", "P")
-    tile = lambda n: ("TH", 2048 * (n // 2) + TC + 640 * (n % 2))
-
-    def half(x, a, b):
-        return (x[0], x[1] + a, x[1] + b)
+    turn(lambda b: T.CB[:, b:C:5], lambda b: T.NF[:, :, b, :], ("NF",), ("CB", 0, C), 32)
+    cp(("LC", 0, C), ("CB", 0, C))
+    cp(("CI", 0, C), ("CB", 0, C))
 
     def masked(tau, h):
-        gtt((XB[tau], h * H, (h + 1) * H), ("MW", 256 * tau, 256 * (tau + 1)), ("LC", 80 * h, 80 * (h + 1)), ("PT", h * H, (h + 1) * H))
+        gtt(("P%d" % tau, h * H, (h + 1) * H), ("MW", 256 * tau, 256 * (tau + 1)), ("LC", HC * h, HC * (h + 1)), ("PT", h * H, (h + 1) * H))
 
-    def stage1(tau, h):
+    def classes(tau, h):
+        k = "K%d" % (2 * tau + h)
+        mm([const((k, 0, 4 * HC), -OFF, (("ONE", 0, 128, "row"), ("CK", 3 * C, 3 * C + 128, "row"))[tau])], True, False)
         for t in range(4):
-            c0 = (t % 2) * C + 80 * h
-            mm(("K%d" % (2 * tau + t // 2), c0, c0 + 80),
-               [(("B1", 3 - u, 131 - u), (XB[tau], h * H + 4 * t + u, (h + 1) * H, 16)) for u in range(4)])
+            mm([((k, t * HC, (t + 1) * HC), ("B1", 3 - u, 131 - u), ("P%d" % tau, h * H + 4 * t + u, (h + 1) * H, 16)) for u in range(4)], False, t == 3)
 
-    def evac(tau):
-        for j in range(2):
-            act(half(tile(tau), 320 * j, 320 * (j + 1)), ("K%d" % (2 * tau + j), 0, 320), F.Identity, 1.0, -OFF)
+    def field(tau, h):
+        k, o = ("K%d" % (2 * tau + h), 0, 4 * HC), ("EX%d" % tau, 4 * HC * h, 4 * HC * (h + 1))
+        if tau == 0:
+            r = ("SR", 4 * HC * h, 4 * HC * (h + 1))
+            if "sr%d" % h in ALT:
+                act(r, k, F.Identity, 1.0, 1.5 * 2.0 ** 35)
+                act(r, r, F.Identity, 1.0, -1.5 * 2.0 ** 35)
+            else:
+                ts(r, k, 1.5 * 2.0 ** 35, A.add, -1.5 * 2.0 ** 35, A.add)
+            tt(o, k, r, A.subtract)
+        else:
+            ts(o, k, 1.5 * 2.0 ** 23, A.add, -1.5 * 2.0 ** 23 - OFF, A.add)
 
-    def sel(tau, d, kb):
+    nsel = [0]
+
+    def pick(tau, d, h):
+        k = "K%d" % (4 + nsel[0] % 2)
+        nsel[0] += 1
         for t in range(4):
-            c0 = (t % 2) * C
-            mm(("K%d" % (kb + t // 2), c0, c0 + C),
-               [(("BT%d" % t, 12 - 4 * ((k + d) % 4), 140 - 4 * ((k + d) % 4)), ("OH", (2 * k + tau) * C, (2 * k + tau + 1) * C)) for k in range(4)])
+            mm([((k, t * HC, (t + 1) * HC), ("BT%d" % t, 12 - 4 * ((j + d) % 4), 140 - 4 * ((j + d) % 4)),
+                 ("OH", (2 * j + tau) * C + HC * h, (2 * j + tau) * C + HC * (h + 1))) for j in range(4)])
+        a, b = 4 * HC * h, 4 * HC * (h + 1)
+        tt(("E%d%d" % (tau, d), a, b), ("EX%d" % tau, a, b), (k, 0, 4 * HC), A.mult)
 
-    def pickd(tau, d, kb):
-        for j in range(2):
-            tt(half(tile(2 + 3 * tau + d), 320 * j, 320 * (j + 1)), half(tile(tau), 320 * j, 320 * (j + 1)), ("K%d" % (kb + j), 0, 320), A.mult)
+    def name(out, src, sign, hs=(0, 1)):
+        return [((out[0], out[1] + HC * h, out[1] + HC * (h + 1)), ({1: "B2", -1: "NB2", -2: "N2B2"}[sign], 12 - 4 * t, 140 - 4 * t),
+                 (src, 4 * HC * h + HC * t, 4 * HC * h + HC * (t + 1))) for h in hs for t in range(4)]
 
-    def stage2(tau, d, kb):
-        mm(("K%d" % kb, d * C, (d + 1) * C), [(("B2", 12 - 4 * t, 140 - 4 * t), half(tile(2 + 3 * tau + d), t * C, (t + 1) * C)) for t in range(4)])
+    def zero(out):
+        return (out, ("BH", 0, 128, "row"), ("ONE", 0, width(out), "row"))
 
-    def field_s_act(kb, a, b):
-        act(("MG", a, b), ("K%d" % kb, a, b), F.Identity, 2.0 ** -12, MAGIC)
-        act(("MH", a, b), ("MG", a, b), F.Identity, 4096.0, -4096.0 * MAGIC)
+    def parts(k, src):
+        fl = "FL%d" % k
+        if "hi%d" % k in ALT:
+            act(sl("HI", 0), src, F.Identity, 1.0, 1.5 * 2.0 ** 29)
+            act(sl(fl, 3), sl("HI", 0), F.Identity, 1.0, -1.5 * 2.0 ** 29)
+        else:
+            ts(sl(fl, 3), src, 1.5 * 2.0 ** 29, A.add, -1.5 * 2.0 ** 29, A.add)
+        if "lo%d" % k in ALT:
+            act(sl(fl, 4), sl("HI", 0), F.Identity)
+        else:
+            tt(sl(fl, 4), src, sl(fl, 3), A.subtract)
 
-    def field_s(kb, a, b):
-        tt(("SN", a, b), ("K%d" % kb, a, b), ("MH", a, b), A.subtract)
-
-    def field_t(kb):
-        act(("MT", 0, 3 * C), ("K%d" % kb, 0, 3 * C), F.Identity, 2.0 ** -12, MAGIC)
-        act(("TN", 0, 3 * C), ("MT", 0, 3 * C), F.Identity, 1.0, -MAGIC)
+    def rows(k):
+        j0 = 1 if k == 0 else 0
+        fl = T["FL%d" % k]
+        turn(lambda b: T.NA[:, j0:3, :, b, :], lambda b: fl[:, 2 + j0:5, b:C:5], sl("FL%d" % k, 2 + j0, 3 - j0), ("NA",), 32 * (3 - j0))
+        dma([(T.U0[16 * gg + 4 * j:128:32, 0:V], T.NA[:, j, gg]) for j in range(j0, 3) for gg in range(2)], [("NA",)], [("XS", 0, V)], 1e5)
 
     def own_copy(k, a, b):
-        dma("s", T.UL[:, a:b], buf("U%d" % k)[:, a:b], [("U%d" % k, a, b)], [("UL", a, b)])
+        o = T.SG3 if k == 0 else T.UL
+        if "oc%d%d" % (k, a // H) in ALT:
+            for c in range(a, b, H // 2):
+                x, y = ("UL0" if k == 0 else "UL", c, c + H // 2), ("U%d" % k, c, c + H // 2)
+                op("g", lambda x=x, y=y: g.affine_select(ap(x), ap(y), [[0, H // 2]], A.is_ge, 0.0, 0, 0), [y], [x], 0.17 + H * PAR["cyc"])
+            return
+        dma([(o[:, a:b], T["U%d" % k][:, a:b])], [("U%d" % k, a, b)], [("UL0" if k == 0 else "UL", a, b)], (256 if k == 0 else 512) * (b - a))
 
-    masked(0, 0)
-    stage1(0, 0)
-    masked(0, 1)
-    ts(("C3", 0, C), ("CI", 0, C), 3, A.bitwise_and)
-    ts(("C3", C, 2 * C), ("CI", 0, C), 4, A.logical_shift_right, 3, A.bitwise_and)
-    cp(("C3B", 0, 2 * C), ("C3", 0, 2 * C))
+    for h in range(2):
+        masked(0, h)
+        classes(0, h)
+    ts(sl("C3", 0), ("CI", 0, C), 3, A.bitwise_and)
+    ts(sl("C3", 1), ("CI", 0, C), 4, A.logical_shift_right, 3, A.bitwise_and)
+    cp(sl("C3B", 0, 2), sl("C3", 0, 2))
     for k in range(4):
-        ts(("OH", 2 * k * C, 2 * (k + 1) * C), ("C3B", 0, 2 * C), float(k), A.is_equal)
-    act(("SB", 0, NB), ("S0", 0, NB), F.Sign, 1.0, 2.0 ** -30)
-    stage("DG0", T.SB, [("SB", 0, NB)])
+        ts(sl("OH", 2 * k, 2), sl("C3B", 0, 2), float(k), A.is_equal)
+    if "u0" in ALT:
+        dma([(T.VO[:, 0:NB], T.s0[:, 0:NB])], [], [("VO", 0, NB)], 3e4)
+        act(("SB", 0, NB), ("VO", 0, NB), F.Abs)
+        share("u0", "DU0", ("SB", 0), "U0", V)
     for h in range(2):
         act(("U0", h * H, (h + 1) * H), ("S0", h * H, (h + 1) * H), F.Abs)
         own_copy(0, h * H, (h + 1) * H)
     for h in range(2):
-        act(("W0", h * H, (h + 1) * H), ("S0", h * H, (h + 1) * H), F.Identity, 0.5, 0.5)
-    stage1(0, 1)
-    sel(0, 0, 4)
-    sel(0, 1, 6)
-    evac(0)
-    act(("U0", V, WN), ("S0", V, WN), F.Abs)
-    masked(1, 0)
-    pickd(0, 0, 4)
-    stage2(0, 0, 0)
-    field_s_act(0, 0, C)
-    sel(0, 2, 4)
-    stage1(1, 0)
-    masked(1, 1)
-    field_s(0, 0, C)
-    ts(("LS0", 0, C), ("SN", 0, C), OFF, A.add)
-    act(("W0", V, WN), ("S0", V, WN), F.Identity, 0.5, 0.5)
+        if h < PAR["sgv"]:
+            ts(("SG0", h * H, (h + 1) * H), ("S0", h * H, (h + 1) * H), 0.0, A.is_ge, 0.5, A.subtract)
+        else:
+            act(("SG0", h * H, (h + 1) * H), ("S0", h * H, (h + 1) * H), F.Sign, 1.0, 2.0 ** -30)
+    if "u0" not in ALT:
+        act(("U0", V, WN), ("S0", V, WN), F.Abs)
     for h in range(2):
-        act(("SG0", h * H, (h + 1) * H), ("S0", h * H, (h + 1) * H), F.Sign, 1.0, 2.0 ** -30)
-    pickd(0, 1, 6)
-    pickd(0, 2, 4)
-    stage1(1, 1)
-    stage2(0, 1, 1)
-    stage2(0, 2, 1)
-    turn_out("NA", "SN", 0)
+        field(0, h)
+        pick(0, 0, h)
+        kb = "K%d" % (6 + h)
+        mm(name((kb, 0, C), "E00", 1, (h,)))
+        ts(("LS0", HC * h, HC * (h + 1)), (kb, HC * h, HC * (h + 1)), OFF, A.add)
+    for h in range(2):
+        mm(name(sl("K6", 1), "E00", 1, (h,)))
+    parts(0, sl("K6", 1))
+    for h in range(2):
+        masked(1, h)
+        classes(1, h)
 
-    def via_load():
-        for gg in range(2):
-            dma("s", T.XS[16 * gg:128:32, 0:V], T.NA[:, gg], [("NA",)], [("XS", gg * H, (gg + 1) * H)])
-
-    def via_gather(ls, h):
-        act(("VO", h * H, (h + 1) * H), ("XS", 0, WN), F.Identity, lst=(ls, 80 * h, 80 * (h + 1)))
-
-    def via_turn(h, a_old):
-        mm(("K3", 80 * h, 80 * (h + 1)), [(("NID", 0, 128), half(a_old, 80 * h, 80 * (h + 1)))]
-           + [(("BV", 15 - i, 143 - i), ("VO", h * H + i, (h + 1) * H, 16)) for i in range(16)])
-
-    via_load()
-    evac(1)
-    field_s_act(1, C, 3 * C)
-    sel(1, 0, 6)
-    sel(1, 1, 4)
-
-    U = ("U0", "U1", "U2", "U3")
-    W = ("W0", "W1", "W2", "W0")
     LA = ("LS0", "LS0", "LS1", "LS2")
-    PCH = ((0, NB), (NB, H), (H, V))
     SGB = 1.75 + 2.0 ** -23
+    nsp = [0]
 
     def p_op(k, a, b):
-        gtt(("P", a, b), (U[k], 0, WN), (LA[k], a // 16, b // 16), ("UL", a, b))
+        gtt(("P%d" % (k % 2), a, b), ("U%d" % k, 0, WN), (LA[k], a // 16, b // 16), ("UL0" if k == 0 else "UL", a, b))
 
     def u_op(k, a, b):
-        act((U[k + 1], a, b), ("P", a, b), F.Abs, -2.0, 1.0)
+        act(("U%d" % (k + 1), a, b), ("P%d" % (k % 2), a, b), F.Abs, -2.0, 1.0)
 
-    def s_op(a, b):
-        act(("SP", a, b), ("P", a, b), F.Identity, -2.0, 1.0)
-
-    def sg_op(k, a, b, to=None):
+    def sg_op(k, a, b):
         e = 1.0 if k % 2 else -1.0
-        act((to or "SG%d" % (k + 1), a, b), ("P", a, b), F.Sign, -3.5 * e, SGB * e)
-
-    def bus(k):
-        p_op(k, 0, NB)
-        u_op(k, 0, NB)
-        sg_op(k, 0, NB, "SB")
-        stage("DU%d" % (k + 1), T[U[k + 1]], [(U[k + 1], 0, NB)])
-        stage("DG%d" % (k + 1), T.SB, [("SB", 0, NB)])
-        send("u%d" % (k + 1), ["DU%d" % (k + 1)], U[k + 1], [("W0", V, WN)] if k == 1 else [])
-        send("c%d" % (k + 1), ["DG%d" % (k + 1), "DG%d" % k], "SG%d" % k)
+        act(("SG%d" % (k + 1), a, b), ("P%d" % (k % 2), a, b), F.Sign, -3.5 * e, SGB * e)
 
     def cross(k, h):
         o, i, a, b = "SG%d" % (k - 1), "SG%d" % k, h * H, (h + 1) * H
-        op("g", lambda: g.dma_start(buf(o)[:, a:b], buf(i)[:, a:b], accum_op=A.add), [(i, a, b), (o, a, b)], [(o, a, b)], kind="d")
+        add((o, a, b), T[o][:, a:b], T[i][:, a:b], [(i, a, b)], 256 * H)
 
-    def rest(k):
+    def s_path(k):
+        p_op(k, 0, NB)
+        u_op(k, 0, NB)
+        sg_op(k, 0, NB)
+        if "sb%d" % k in ALT:
+            mm([(("K7", 0, NB), IB, ("SG%d" % j, 0, NB)) for j in (k, k + 1)])
+            act(("SB", 0, NB), ("K7", 0, NB), F.Identity)
+        else:
+            tt(("SB", 0, NB), ("SG%d" % k, 0, NB), ("SG%d" % (k + 1), 0, NB), A.add)
+        share("u%d" % (k + 1), "DU%d" % (k + 1), ("U%d" % (k + 1), 0), "U%d" % (k + 1), V,
+              [("TH", 0, V)] if k == 1 and "w0" in ALT else [])
+        share("c%d" % (k + 1), "DG%d" % (k + 1), ("SB", 0), "SG%d" % k, V)
+        p_op(k, NB, H)
+        p_op(k, H, V)
+
+    def s_rest(k):
         for h in range(2):
-            u_op(k, *PCH[h + 1])
-            own_copy(k + 1, h * H, (h + 1) * H)
-        for h in range(2):
-            sg_op(k, h * H, (h + 1) * H)
+            sg_op(k, max(NB, h * H), (h + 1) * H)
             cross(k + 1, h)
+        for h in range(2):
+            u_op(k, max(NB, h * H), (h + 1) * H)
+            own_copy(k + 1, h * H, (h + 1) * H)
 
-    def th_op(k, c):
-        gtt(("TH", 2048 * c + TC * k, 2048 * c + TC * (k + 1)), (W[k], 0, WN), (LA[k], 32 * c, 32 * (c + 1)), ("SP", TC * c, TC * (c + 1)))
+    def y_path(k):
+        if k == 0 and "w0" in ALT:
+            for a, b in ((0, NB), (NB, H), (H, V)):
+                if "pa" in ALT:
+                    add(("P0", a, b), T.P0[:, a:b], T.HF[:, 0:b - a], [("HF", 0, H)], 512 * (b - a))
+                else:
+                    act(("G", a, b), ("P0", a, b), F.Identity, -1.0, 0.5)
+                gtt(("TH", a, b), ("U3", 0, WN), ("LS0", a // 16, b // 16), ("P0" if "pa" in ALT else "G", a, b))
+                if a == 0:
+                    share("t1", "DT1", ("TH", 0), "TH", V)
+            return
+        for a, b in ((0, TC), (TC, H), (H, V)) if k == 0 else ((0, TC), (TC, 3 * TC), (3 * TC, V)):
+            if k == 0 and "g%d" % min(2, a // TC) in ALT:
+                x, w, lst = ("G", a, b), ("S0", 0, WN), ("LS0", a // 16, b // 16)
+                op("v", lambda x=x, w=w, lst=lst: g.vector.tensor_scalar(ap(x), ap(w).indirect(ap(lst)), 0.5, 0.5, A.mult, A.add),
+                   [w, lst], [x], vdur(b - a, PAR["gat"]))
+            elif k == 0:
+                act(("G", a, b), ("S0", 0, WN), F.Identity, 0.5, 0.5, lst=("LS0", a // 16, b // 16))
+            else:
+                act(("G", a, b), ("TH", 0, k * WN), F.Sigmoid, 4.0 * sgn, lst=(("LS0", "LG")[k - 1], a // 16, b // 16))
+        for a in range(0, V, TC):
+            kb, p = ("K%d" % (nsp[0] % 2), 0, TC), ("P%d" % (k % 2), a, a + TC)
+            nsp[0] += 1
+            if "sp%d%d" % (k, a // TC) in ALT:
+                act(kb, p, F.Identity, -2.0 * sgn, sgn)
+            elif sgn > 0:
+                mm([const(kb, 1.0), (kb, N2I, p)])
+            else:
+                mm([const(kb, 1.0, NIB), (kb, ("P2I", 0, 128), p)])
+            tt(("TH", HB[k] + a, HB[k] + a + TC), ("G", a, a + TC), kb, A.mult)
+            if (k, a) == (0, 0):
+                share("t1", "DT1", ("TH", 0), "TH", V)
 
-    def w_op(k, c):
-        out = (W[k + 1] if k < 3 else "VO", TC * c, TC * (c + 1))
-        win = ("TH", 2048 * c, 2048 * c + TC * (k + 1))
-        f, s = (F.Sigmoid, 4.0) if k < 3 else (F.Tanh, 2.0)
-        lst = None if k == 0 else ("LS%d" % k, 2 * C + 32 * c, 2 * C + 32 * (c + 1))
-        if (k, c) == (2, 4):
-            act(("VO", out[1], out[2]), win, F.Tanh, 2.0, 0.0, lst=lst)
-            act(out, ("VO", out[1], out[2]), F.Identity, 0.5, 0.5)
+    def via(k, h):
+        x, w, lst = ("VO", h * H, (h + 1) * H), ("XS", 0, WN), (LA[k], HC * h, HC * (h + 1))
+        if "vi%d%d" % (k, h) in ALT:
+            op("v", lambda: g.vector.tensor_copy(ap(x), ap(w).indirect(ap(lst))), [w, lst], [x], vdur(H, PAR["gat"]))
         else:
-            act(out, win, f, s, 0.0, lst=lst)
-        if c == 0 and k < 3:
-            stage("DW%d" % (k + 1), T[W[k + 1]], [(W[k + 1], 0, NB)])
-            send("w%d" % (k + 1), ["DW%d" % (k + 1)], W[k + 1])
-        if k == 3:
-            dma("s", T.y[:, TC * c:TC * (c + 1)], T.VO[:, TC * c:TC * (c + 1)], [out], [])
+            act(x, w, F.Identity, lst=lst)
 
-    def prod(k, h):
-        gtt(("PRD%d" % k, h * H, (h + 1) * H), ("SG%d" % (k - 1), 0, WN), (LA[k], C + 80 * h, C + 80 * (h + 1)), ("SG%d" % k, h * H, (h + 1) * H))
-        mm(("K2", 80 * h, 80 * (h + 1)), [(("BZ", 15 - i, 143 - i), ("PRD%d" % k, h * H + i, (h + 1) * H, 16)) for i in range(16)])
+    def wrap(out, sel, src, h):
+        return [((out[0], out[1] + HC * h, out[1] + HC * (h + 1)), (sel, 15 - i, 143 - i), (src, h * H + i, (h + 1) * H, 16)) for i in range(16)]
 
-    I, NI, IB, IB16, IBL = (("ID", 0, 128), ("NID", 0, 128), ("IB", 0, 128), ("IB16", 0, 128), ("IBL", 0, 128))
-    sl = lambda n, j: (n, j * C, (j + 1) * C)
-
-    def flags(k):
-        fl = "FL%d" % k
+    def z_op(k):
+        for h in range(2):
+            gtt(("PRD", h * H, (h + 1) * H), ("SG%d" % (k - 1), 0, WN), (LA[k], C + HC * h, C + HC * (h + 1)), ("SG%d" % k, h * H, (h + 1) * H))
+            mm([const(sl("K2", 0), -6.0)] * (h == 0) + wrap(sl("K2", 0), "BZ", "PRD", h), h == 0, h == 1)
+        fl, z = "FL%d" % k, sl("K2", 0)
         if k < 3:
-            ts(sl(fl, 0), sl("K2", 0), 3.0, A.is_ge)
-        ts(sl(fl, 1), sl("K2", 0), 9.0, A.is_ge)
-        ts(sl(fl, 2), sl("K2", 0), -7.0, A.is_le)
-        if k < 3:
-            tt(sl(fl, 3), sl(fl, 0), sl(fl, 1), A.subtract)
+            ts(sl(fl, 0), z, 1.5 * 2.0 ** 26 + 8, A.add, 1.5 * 2.0 ** 26 + 8, A.is_equal)
+        ts(sl(fl, 1), z, 3.0, A.is_ge)
+        ts(sl(fl, 2), z, -13.0, A.is_le)
 
-    bus(0)
-    p_op(0, *PCH[1])
-    field_s(1, C, 3 * C)
-    s_op(0, H)
-    pickd(1, 0, 6)
-    p_op(0, *PCH[2])
-    stage2(1, 0, 0)
-    sel(1, 2, 6)
-    s_op(H, V)
-    pickd(1, 1, 4)
-    stage2(1, 1, 0)
-    th_op(0, 0)
-    pickd(1, 2, 6)
-    stage2(1, 2, 0)
-    w_op(0, 0)
-    rest(0)
-    field_t(0)
-    for c in range(1, 5):
-        th_op(0, c)
-    cp(("LS0", C, 2 * C), ("TN", 0, C))
-    mm(sl("K4", 2), [(I, sl("SN", 2)), (NI, sl("SN", 1))])
-    mm(sl("K5", 0), [(I, sl("TN", 1)), (NI, sl("TN", 0))])
-    mm(sl("K5", 1), [(I, sl("TN", 2)), (NI, sl("TN", 1))])
+    old = lambda out, k, s: [(out, IB if s > 0 else NIB, sl("FL%d" % k, 3)), (out, IB if s > 0 else NIB, sl("FL%d" % k, 4))]
 
-    for k in (1, 2):
-        fl, pr, ls = "FL%d" % k, "PR%d" % k, "LS%d" % k
-        a_old, b_old = (sl("SN", 0), sl("TN", 0)) if k == 1 else (sl("AB", 0), sl("AB", 1))
-        bus(k)
-        via_gather(LA[k], 0)
-        via_turn(0, a_old)
-        p_op(k, *PCH[1])
-        via_gather(LA[k], 1)
-        via_turn(1, a_old)
-        p_op(k, *PCH[2])
-        for c in range(1, 5):
-            w_op(k - 1, c)
-        s_op(0, H)
-        if k == 1:
-            mm(sl("K4", 1), [(I, sl("SN", 1)), (NI, a_old)])
+    s_path(0)
+    dma([(T.U0[4 * j:128:16, V:WN], T.BH[:, c0:c0 + 56]) for j, c0 in enumerate((0, 128, 192))], [("BH", 0, 256)], [("XS", V, WN)], 5e4)
+    rows(0)
+    for h in range(2):
+        field(1, h)
+        pick(1, 0, h)
+        mm(name(sl("K7", 1), "E10", 1, (h,)))
+    ts(sl("LS0", 1), sl("K7", 1), OFF, A.add)
+    s_rest(0)
+    y_path(0)
+    for tau in range(2):
+        for h in range(2):
+            pick(tau, 1, h)
+    ts(sl("C3", 2), ("CI", 0, C), 15, A.bitwise_and)
+    cp(sl("C3B", 2), sl("C3", 2))
+
+    s_path(1)
+    mm(old(sl("K3", 1), 0, -1) + name(sl("K3", 1), "E01", 1))
+    for h in range(2):
+        mm(name(sl("K3", 2), "E11", 1, (h,)) + name(sl("K3", 2), "E10", -1, (h,)))
+    mm(old(sl("K3", 0), 0, -1), True, False)
+    for h in range(2):
+        via(1, h)
+        mm(wrap(sl("K3", 0), "BV", "VO", h), False, h == 1)
+    for tau in range(2):
+        mm([const(sl("K4", tau), -OFF, NIB)] + name(sl("K4", tau), "EX%d" % tau, 1) + name(sl("K4", tau), "E%d1" % tau, -2)
+           + (name(sl("K4", 1), "E10", -1) if tau else old(sl("K4", 0), 0, -1)))
+    lb, lo = ("K6", 0, 2 * C + 8), ("K6", 2 * C, 2 * C + 8)
+    mm([zero(lb)] + old(sl("K6", 0), 0, 1) + name(sl("K6", 1), "E10", 1) + [(lo, IBL, ("ONE", 0, 8)), (lo, I, ("BK", 0, 8))], True, False)
+    z_op(1)
+    s_rest(1)
+    tt(sl("PR1", 0, 3), sl("K3", 0, 3), sl("FL1", 0, 3), A.mult)
+    mm([(sl("K6", 0), I, sl("PR1", 0)), (sl("K6", 0), I, sl("PR1", 1)), (sl("K6", 1), I, sl("PR1", 2)), (lo, IBL, ("FL1", 2 * C, 2 * C + 8))], False, True)
+    ts(("LS1", 0, 2 * C + 8), lb, OFF, A.add)
+    parts(1, sl("K6", 0))
+    rows(1)
+    tt(sl("PR1", 3, 2), sl("K4", 0, 2), sl("FL1", 1, 2), A.mult)
+    y_path(1)
+    act(("TB", 0, NB), ("TH", 0, WN + NB), F.Identity, lst=("LS1", 2 * C, 2 * C + 8))
+    share("t2", "DT2", ("TB", 0), "TH", WN + V, [("P1", 0, V)])
+
+    s_path(2)
+    mm(old(sl("K3", 1), 1, -1) + name(sl("K3", 1), "E01", 1) + [(sl("K3", 1), I, sl("PR1", 3))])
+    mm([(sl("K3", 2), I, sl("PR1", 4)), (sl("K3", 2), N2I, sl("PR1", 2)), (sl("K3", 2), I, sl("PR1", 2))]
+       + name(sl("K3", 2), "E11", 1) + name(sl("K3", 2), "E10", -1))
+    mm(old(sl("K3", 0), 1, -1), True, False)
+    mm([(sl("K4", 0), IBL, ("ONE", 0, C)), (sl("K4", 0), IBL, sl("FL1", 2))])
+    mm([zero(sl("K6", 0, 3))] + old(sl("K6", 0), 1, 1) + name(sl("K6", 1), "E10", 1)
+       + [(sl("K6", 1), I, sl("PR1", 2)), (sl("K6", 2), I, sl("BK", 0))], True, False)
+    mm(old(sl("K5", 0), 1, 1), True, False)
+    for h in range(2):
+        via(2, h)
+        mm(wrap(sl("K5", 0), "BL", "VO", h), False, h == 1)
+        mm(wrap(sl("K3", 0), "BV", "VO", h), False, h == 1)
+    ts(sl("LG", 0), sl("K5", 0), OFF + WN, A.add)
+    z_op(2)
+    s_rest(2)
+    tt(sl("PR2", 0, 3), sl("K3", 0, 3), sl("FL2", 0, 3), A.mult)
+    tt(sl("PR2", 3), sl("K4", 0), sl("FL2", 2), A.mult)
+    mm([(sl("K6", 0), I, sl("PR2", 0)), (sl("K6", 0), I, sl("PR2", 1)), (sl("K6", 1), I, sl("PR2", 2)), (sl("K6", 2), I, sl("PR2", 3))], False, True)
+    ts(sl("LS2", 0, 3), sl("K6", 0, 3), OFF, A.add)
+    y_path(2)
+
+    for a, b in ((0, NB), (NB, H), (H, V - PAR["wt"]), (V - PAR["wt"], V)):
+        if b == V:
+            if a < b:
+                act(("G", a, b), ("TH", 0, HB[2] + b), F.Tanh, 2.0 * sgn, lst=("LS2", 2 * C + a // 16, 2 * C + b // 16))
+                act(("W3", a, b), ("G", a, b), F.Identity, 0.5, 0.5)
+            continue
+        act(("W3", a, b), ("TH", 0, HB[2] + b), F.Sigmoid, 4.0 * sgn, lst=("LS2", 2 * C + a // 16, 2 * C + b // 16))
+        if a == 0:
+            share("w3", "DW3", ("U1", 0), "U1", V)
+    for h in range(2):
+        p_op(3, h * H, (h + 1) * H)
+        if "s4%d" % h in ALT:
+            ts(("SP", h * H, (h + 1) * H), ("P1", h * H, (h + 1) * H), -2.0 * sgn, A.mult, sgn, A.add)
         else:
-            mm(sl("K4", 1), [(I, sl("SN", 1)), (I, sl("PR1", 2)), (NI, a_old)])
-            mm(sl("K5", 0), [(I, sl("TN", 1)), (I, sl("PR1", 4)), (NI, b_old)])
-        mm(sl("K6", 0), [(I, a_old)], True, False)
-        mm(sl("K7", 0), [(I, b_old)], True, False)
-        mm(sl("K0", 0), [(I, sl("BK", k - 1))], True, False)
-        prod(k, 0)
-        prod(k, 1)
-        s_op(H, V)
-        rest(k)
-        th_op(k, 0)
-        flags(k)
-        th_op(k, 1)
-        tt(sl(pr, 1), sl("K4", 1), sl(fl, 1), A.mult)
-        tt(sl(pr, 0), sl("K3", 0), sl(fl, 3), A.mult)
-        tt(sl(pr, 3), sl("K5", 0), sl(fl, 2), A.mult)
-        if k == 2:
-            tt(sl(fl, 4), sl(fl, 2), sl("FL1", 2), A.mult)
-        mm(sl("K6", 0), [(I, sl(pr, 1)), (I, sl(pr, 0))], False, True)
-        mm(sl("K7", 0), [(I, sl(pr, 3))], False, True)
-        mm(sl("K0", 0), [(IBL, sl(fl, 2))] + ([(IBL, sl(fl, 4))] if k == 2 else []), False, True)
-        if k == 1:
-            tt(sl(pr, 2), sl("K4", 2), sl(fl, 1), A.mult)
-            tt(sl(pr, 4), sl("K5", 1), sl(fl, 2), A.mult)
-        th_op(k, 2)
-        ts(sl(ls, 0), sl("K6", 0), OFF, A.add)
-        cp(sl(ls, 1), sl("K7", 0))
-        cp(sl(ls, 2), sl("K0", 0))
-        if k == 1:
-            act(sl("AB", 0), sl("K6", 0), F.Identity)
-            act(sl("AB", 1), sl("K7", 0), F.Identity)
-        w_op(k, 0)
-        th_op(k, 3)
-        if k == 1:
-            turn_out("NA", "AB", 0)
-            via_load()
-        th_op(k, 4)
+            act(("SP", h * H, (h + 1) * H), ("P1", h * H, (h + 1) * H), F.Identity, -2.0 * sgn, sgn)
+    mm([const(sl("K4", 0), -float(V)), (sl("K4", 0), I, sl("PR2", 3))])
+    mm([(sl("K6", 0), I, sl("BK", 0))], True, False)
+    z_op(3)
+    tt(sl("PR3", 0), sl("K4", 0), sl("FL3", 2), A.mult)
+    mm([(sl("K6", 0), I, sl("PR3", 0))], False, True)
+    ts(sl("LS3", 0), sl("K6", 0), V + OFF, A.add)
+    cuts = (0, TC, 2 * TC, 3 * TC, 4 * TC, 4 * TC + 256, V)
+    for a, b in zip(cuts, cuts[1:]):
+        gtt(("TH", HB[3] + a, HB[3] + b), ("W3", 0, WN), ("LS2", a // 16, b // 16), ("SP", a, b))
+        act(("YO", a, b), ("TH", 0, HB[3] + b), F.Tanh, 2.0 * sgn, lst=("LS3", a // 16, b // 16))
+        dma([(T.y[:, a:b], T.P0[:, a:b])], [("YO", a, b)], [], 512 * (b - a))
 
-    p_op(3, 0, H)
-    p_op(3, H, V)
-    for c in range(1, 5):
-        w_op(2, c)
-    s_op(0, H)
-    s_op(H, V)
-    prod(3, 0)
-    prod(3, 1)
-    th_op(3, 0)
-    flags(3)
-    tt(sl("FL3", 3), sl("FL3", 2), sl("FL2", 2), A.mult)
-    tt(sl("FL3", 4), sl("FL3", 2), sl("FL2", 4), A.mult)
-    mm(sl("K0", 0), [(I, sl("BK", 2))], True, False)
-    mm(sl("K0", 0), [(IBL, sl("FL3", 2)), (IBL, sl("FL3", 3)), (IBL, sl("FL3", 4))], False, True)
-    mm(sl("K1", 0), [(IB, sl("CB", 0))] + [(IB, sl("FL%d" % k, 1)) for k in (1, 2, 3)])
-    mm(sl("K1", 1), [(IB, sl("CB", 0))] + [(IB16, sl("FL%d" % k, 2)) for k in (1, 2, 3)])
-    th_op(3, 1)
-    cp(sl("LS3", 2), sl("K0", 0))
-    cp(("QI", 0, 2 * C), ("K1", 0, 2 * C))
-    w_op(3, 0)
-    w_op(3, 1)
-    th_op(3, 2)
-    ts(sl("QI", 2), sl("QI", 0), 15, A.bitwise_and)
-    ts(sl("QI", 3), sl("QI", 1), 240, A.bitwise_and)
-    w_op(3, 2)
-    th_op(3, 3)
-    tt(sl("QF", 0), sl("QI", 2), sl("QI", 3), A.add)
-    w_op(3, 3)
-    for j in range(2):
-        a, b = 4 * TC + 256 * j, 4 * TC + 256 * (j + 1)
-        gtt(("TH", 8192 + 3 * TC + 256 * j, 8192 + 3 * TC + 256 * (j + 1)), (W[3], 0, WN), (LA[3], a // 16, b // 16), ("SP", a, b))
-        act(("VO", a, b), ("TH", 8192, 8192 + 3 * TC + 256 * (j + 1)), F.Tanh, 2.0, 0.0, lst=("LS3", 2 * C + a // 16, 2 * C + b // 16))
-        dma("s", T.y[:, a:b], T.VO[:, a:b], [("VO", a, b)], [])
-    turn_out("NQ", "QF", 0)
-    for gg in range(2):
-        dma("a", T.q[gg:8:2, :], T.NQ[:, gg], [("NQ",)], [])
+    turns = lambda out, j, w, ks: [(out, w, sl("FL%d" % k, j)) for k in ks]
+    for ks in ((1, 2), (3,)):
+        head = [zero(sl("K5", 0, 2)), (sl("K5", 0), IB16, sl("C3B", 2)), (sl("K5", 1), IB, sl("CB", 0))] if ks[0] == 1 else []
+        mm(head + turns(sl("K5", 0), 1, IB16, ks) + turns(sl("K5", 1), 2, IB16, ks), ks[0] == 1, ks[0] == 3)
+        head = [(sl("K7", 0), IB, sl("CB", 0))] if ks[0] == 1 else []
+        mm(head + turns(sl("K7", 0), 1, IB, ks) + turns(sl("K7", 0), 2, IB16, ks), ks[0] == 1, False)
+    ts(sl("WR", 0, 2), sl("K5", 0, 2), 256.0, A.is_ge, -16.0, A.mult)
+    mm([(sl("K7", 0), IB, sl("WR", 0)), (sl("K7", 0), IB16, sl("WR", 1))], False, True)
+    turn(lambda b: T.NQ[:, :, b, :], lambda b: T.K7[:, b:C:5], sl("K7", 0), ("NQ",), 32)
+    dma([(T.q[gg:8:2, :], T.NQ[:, gg]) for gg in range(2)], [("NQ",)], [], 8e4)
     return ops
 
 
@@ -503,7 +570,7 @@ def conflict(o, e):
             for y in theirs:
                 if x[0] != y[0]:
                     continue
-                if x[0][0] == "K" and e["q"] != q:
+                if x[0][0] == "K" and (e["q"] != q or q == "t"):
                     return True
                 if ww == 2 or (ww == 1 and o.get("par") and e.get("par") and e["q"] == q and e["rd"] == o["rd"]):
                     continue
@@ -512,30 +579,155 @@ def conflict(o, e):
     return False
 
 
+def lay_out(ops, dep, prio, back, PAR, slack):
+    n = len(ops)
+    hop = [PAR["hop"] if e["kind"] == "c" else (0.0 if e["kind"] == "r" else PAR["wake"]) for e in ops]
+    fly = [o.get("lat", 0.0) + o.get("busy", 0.0) + o.get("once", 0.0) for o in ops]
+    nxt = [[] for o in ops]
+    for i in range(n):
+        for j in dep[i]:
+            nxt[j].append(i)
+    need, at = [len(d) for d in dep], [0.0] * n
+    end, free, pipe, func, order = [0.0] * n, {}, 0.0, None, []
+    ready = [i for i in range(n) if not dep[i]]
+    while ready:
+        start = {i: max(free.get(ops[i]["q"], 0.0), at[i] + (fly[i] + hop[i] if back else 0.0)) for i in ready}
+        first = min(ready, key=lambda i: (start[i], i))
+        q = ops[first]["q"]
+        i = max((j for j in ready if ops[j]["q"] == q and start[j] <= start[first] + slack),
+                key=lambda j: (prio[j] - PAR["lam"] * max(0.0, start[j] - start[first] - 0.1), -j))
+        o, t = ops[i], start[i]
+        d = o["dur"]
+        if o.get("f") in (F.Sigmoid, F.Tanh) and o["f"] != func:
+            d, func = d + 1.4, o["f"]
+        if q is not None:
+            free[q] = t + d
+        end[i] = t + d
+        if "busy" in o and not back:
+            pipe = max(pipe, t + d + o["lat"] / 2 + o.get("once", 0.0)) + o["busy"]
+            end[i] = pipe + o["lat"] / 2
+        order.append(i)
+        ready.remove(i)
+        for j in nxt[i]:
+            at[j] = max(at[j], end[i] + (0.0 if back else hop[i]))
+            need[j] -= 1
+            if need[j] == 0:
+                ready.append(j)
+    return order, end
+
+
+def replay(ops, dep, order, start=None):
+    end, free, pipe, func = [0.0] * len(ops), [0.0] * 6, 0.0, 0
+    for i in order:
+        q, dur, f, out, busy, home = ops[i]
+        t = free[q] if q else 0.0
+        for j in dep[i]:
+            if end[j] > t:
+                t = end[j]
+        if start:
+            start[i] = t
+        t += dur
+        if f and f != func:
+            t, func = t + 1.4, f
+        free[q] = t
+        if busy:
+            t += out
+            pipe = t = (t if t > pipe else pipe) + busy
+        end[i] = t + home
+    return max(end)
+
+
+def improve(order, dep, rev, queue, cost, by_time):
+    cur = cost(order)
+    best, seed, n, tries = (cur, order), 1, len(order), PAR["tries"]
+    for it in range(tries):
+        if it % PAR["sort"] == 0:
+            order = by_time(order)
+            cur = cost(order)
+            if cur < best[0]:
+                best = (cur, order)
+        seed = (seed * 1103515245 + 12345) % (1 << 31)
+        a, steps, back = (seed >> 8) % n, (1, 1, 2, 3, 5)[(seed >> 20) % 5], seed >> 28 & 1
+        seq, link = (order[::-1], dep) if back else (order, rev)
+        i = seq[a]
+        near = [b for b in range(a + 1, min(n, a + 60)) if queue[seq[b]] == queue[i]][:steps]
+        if not queue[i] or not near:
+            continue
+        moved, rest, tied = [i], [], set(link[i])
+        for x in seq[a + 1:near[-1] + 1]:
+            if x in tied:
+                moved.append(x)
+                tied.update(link[x])
+            else:
+                rest.append(x)
+        if moved[-1] == seq[near[-1]] or len(moved) > 8:
+            continue
+        new = seq[:a] + rest + moved + seq[near[-1] + 1:]
+        new = new[::-1] if back else new
+        c = cost(new)
+        if c <= cur + PAR["give"] * (1 - it / tries):
+            order, cur = new, c
+    return best[1]
+
+
+def schedule(cases):
+    ops = cases[0][0]
+    n = len(ops)
+    dep, rev, below, full = [], [[] for o in ops], [], []
+    for i in range(n):
+        d = [j for j in range(i) if conflict(ops[i], ops[j])]
+        full.append(d)
+        far = set().union(*[below[j] for j in d])
+        below.append(far.union(d))
+        dep.append([j for j in d if j not in far])
+        for j in dep[i]:
+            rev[j].append(i)
+    orders = []
+    for os, par in cases:
+        for slack in PAR["slack"]:
+            end = list(range(n))
+            for r in range(PAR["rounds"]):
+                order, end = lay_out(os, dep, lay_out(os, rev, end, True, par, slack)[1], False, par, slack)
+                orders.append(order)
+    tabs = [[((None, "v", "a", "t", "g", "s").index(o["q"]), o["dur"], {F.Sigmoid: 1, F.Tanh: 2}.get(o.get("f"), 0),
+              o.get("lat", 0.0) / 2 + o.get("once", 0.0), o.get("busy", 0.0),
+              o.get("lat", 0.0) / 2 + {"c": par["hop"], "r": 0.0}.get(o["kind"], par["wake"])) for o in os] for os, par in cases]
+    ends = [[replay(t, dep, order) for t in tabs] for order in orders]
+    least = [min(e[c] for e in ends) for c in range(len(cases))]
+    best = min(range(len(orders)), key=lambda j: sum(e / m for e, m in zip(ends[j], least)))
+    use = [(tabs[c], least[c]) for c in PAR["use"]]
+
+    def by_time(order):
+        start = [0.0] * n
+        replay(tabs[0], dep, order, start)
+        return sorted(order, key=lambda i: start[i])
+    order = improve(orders[best], dep, rev, [t[0] for t in tabs[0]], lambda o: sum(replay(t, dep, o) / m for t, m in use) / len(use), by_time)
+    LOG.append([round(replay(t, dep, order), 1) for t in tabs])
+    return order, full
+
+
 def emit(g, T, ops):
     Q = {"v": g.vector, "a": g.scalar, "t": g.tensor, "g": g, "s": g.sync}
     esem = {"v": "e_v", "a": "e_a", "t": "e_t", "g": "e_g"}
     known = {q: {} for q in Q}
     count = {}
     nd = [0]
-    done = []
-    for o in ops:
+    for at, o in enumerate(ops):
         q = o["q"]
+        o["at"] = at
         if o["kind"] == "arr":
             o["sig"], o["clock"] = ("arr_" + o["x"], 2 * (N - 1)), {}
             count[o["sig"][0]] = o["sig"][1]
-            done.append(o)
             continue
-        for e in reversed(done):
+        for e in sorted(o["dep"], key=lambda e: -e["at"]):
             s, n = e["sig"]
-            if known[q].get(s, 0) >= n:
+            if known[q].get(s, 0) >= n or q == e["q"] == "t":
                 continue
-            if conflict(o, e):
-                Q[q].wait_ge(T.sem[s], n)
-                known[q][s] = n
-                for s2, n2 in e["clock"].items():
-                    if known[q].get(s2, 0) < n2:
-                        known[q][s2] = n2
+            Q[q].wait_ge(T.sem[s], n)
+            known[q][s] = n
+            for s2, n2 in e["clock"].items():
+                if known[q].get(s2, 0) < n2:
+                    known[q][s2] = n2
         ins = o["fn"]()
         if o["kind"] == "c":
             s = esem[q]
@@ -544,13 +736,13 @@ def emit(g, T, ops):
         elif o["kind"] == "d":
             s = "d%d" % nd[0]
             nd[0] += 1
-            count[s] = 16
-            ins.then_inc(T.sem[s], 16)
+            count[s] = 16 * len(ins)
+            for x in ins:
+                x.then_inc(T.sem[s], 16)
         else:
             s = "out_" + o["x"]
             count[s] = 2 * (N - 1)
         o["sig"], o["clock"] = (s, count[s]), dict(known[q])
-        done.append(o)
     for s, n in count.items():
         if max(known[q].get(s, 0) for q in Q) < n:
             g.sync.wait_ge(T.sem[s], n)
@@ -559,5 +751,11 @@ def emit(g, T, ops):
 def rank_program(g, core, T, topo):
     if T.rank_of(core) is None:
         return
-    ops = build(g, core, T, topo)
-    emit(g, T, ops if ORDER is None else [ops[j] for j in ORDER])
+    cases = [(build(g, core, T, topo, dict(PAR, **c)), dict(PAR, **c)) for c in CASES]
+    if repr(PAR) not in ORDER:
+        ORDER[repr(PAR)] = schedule(cases)
+    order, dep = ORDER[repr(PAR)]
+    ops = cases[0][0]
+    for o, d in zip(ops, dep):
+        o["dep"] = [ops[j] for j in d]
+    emit(g, T, [ops[j] for j in order])

@@ -1,3 +1,4 @@
+import math
 from concourse.bass import DstId, RemoteDMATransfer
 from concourse.mybir import AluOpType, ActivationFunctionType
 
@@ -13,20 +14,18 @@ for _n, _w, _d in [
     ("U1", WN, "float32"), ("U2", WN, "float32"), ("U3", WN, "float32"), ("TH", HB[3] + V, "float32"),
     ("S0", WN, "bfloat16"), ("U0", WN, "bfloat16"), ("SG0", WN, "bfloat16"), ("SG1", WN, "bfloat16"), ("SG2", WN, "bfloat16"),
     ("SG3", V, "bfloat16"), ("PRD", V, "bfloat16"), ("VO", V, "bfloat16"), ("SB", NB, "bfloat16"), ("TB", NB, "float32"),
-    ("BH", 256, "bfloat16"), ("ONE", TC, "bfloat16"), ("CK", 5 * C, "bfloat16"),
-    ("CB", C, "bfloat16"), ("CI", C, "int32"), ("C3", 3 * C, "int32"), ("C3B", 3 * C, "bfloat16"), ("OH", 8 * C, "bfloat16"),
+    ("BH", 128, "bfloat16"), ("ZR", TC, "bfloat16"), ("ONE", C, "bfloat16"), ("CK", 6 * C, "bfloat16"), ("NEG", H // 2, "bfloat16"), ("P2I", 128, "float32"),
+    ("CB", C, "bfloat16"), ("HH", 3 * C, "bfloat16"), ("NP", 2 * C, "bfloat16"),
     ("MW", 512, "bfloat16"), ("LM", 32, "uint16"), ("LC", C, "uint16"),
-    ("IOT", 160, "float32"), ("PI", 8, "int32"), ("PJ", 8, "int32"), ("PF", 16, "float32"),
-    ("M3I", 16, "int32"), ("M3J", 16, "int32"), ("M3", 16, "float32"),
-    ("B1", 144, "float32"), ("ID", 128, "float32"), ("N2I", 128, "float32"), ("B2", 144, "float16"), ("NB2", 144, "float16"), ("N2B2", 144, "float16"),
-    ("B2B", 144, "bfloat16"), ("BZ", 144, "bfloat16"), ("BV", 144, "bfloat16"), ("BL", 144, "bfloat16"),
-    ("BT0", 144, "bfloat16"), ("BT1", 144, "bfloat16"), ("BT2", 144, "bfloat16"), ("BT3", 144, "bfloat16"),
-    ("IB", 128, "bfloat16"), ("NIB", 128, "bfloat16"), ("IB16", 128, "bfloat16"), ("IBL", 128, "bfloat16"),
-    ("EX0", 4 * C, "float16"), ("EX1", 4 * C, "float16"),
-    ("E00", 4 * C, "float16"), ("E01", 4 * C, "float16"), ("E10", 4 * C, "float16"), ("E11", 4 * C, "float16"),
+    ("IOT", 160, "float32"), ("PI", 8, "int32"), ("PJ", 8, "int32"), ("PF", 24, "float32"),
+    ("M3I", 16, "int32"), ("M3J", 16, "int32"), ("M3", 48, "float32"), ("SEL", 64, "float32"),
+    ("ID", 128, "float32"), ("N2I", 128, "float32"),
+    ("BZ", 144, "bfloat16"), ("BV", 144, "bfloat16"), ("BL", 144, "bfloat16"),
+    ("IB", 128, "bfloat16"), ("NIB", 128, "bfloat16"), ("IB2", 128, "bfloat16"), ("IB16", 128, "bfloat16"), ("IBW", 128, "bfloat16"), ("IBL", 128, "bfloat16"),
+    ("LW", 6 * C, "float16"), ("N2", 2 * C, "float16"), ("SF", WN - V, "bfloat16"), ("XP", 2 * C, "float32"),
     ("LS0", 2 * C, "uint16"), ("LS1", 2 * C + 8, "uint16"), ("LS2", 3 * C, "uint16"), ("LS3", C, "uint16"), ("LG", C, "uint16"),
-    ("F0", C, "bfloat16"), ("WR", 2 * C, "bfloat16"), ("PR1", 5 * C, "float32"), ("PR2", 4 * C, "float32"), ("PR3", C, "float32"),
-    ("BC", C, "float32"), ("BK", C, "float32"), ("HI", C, "float32"), ("HF", H, "bfloat16"), ("P2I", 128, "float32"),
+    ("WR", 2 * C, "bfloat16"), ("PR1", 5 * C, "float32"), ("PR2", 4 * C, "float32"), ("PR3", C, "float32"),
+    ("BC", C, "float32"), ("BK", C, "float32"),
 ]:
     SCRATCH[_n] = ("sbuf", [128, _w], _d)
 for _k in range(4):
@@ -39,22 +38,34 @@ for _k in range(8):
     SCRATCH["K%d" % _k] = ("psum", [128, TC], "float32")
 for _n in ("DU1", "DU2", "DU3", "DT1", "DT2", "DW3"):
     SCRATCH[_n] = ("dram", [256, NB], "float32")
-for _n in ("DS0", "DU0", "DG1", "DG2", "DG3"):
+for _n in ("DS0", "DG1", "DG2", "DG3"):
     SCRATCH[_n] = ("dram", [256, NB], "bfloat16")
 
-XCH = ["s0", "u0", "u1", "u2", "u3", "c1", "c2", "c3", "t1", "t2", "w3"]
-SEMAPHORES = (["e_v", "e_a", "e_t", "e_g"] + ["d%d" % _k for _k in range(60)] + ["arr_" + _x for _x in XCH]
+XCH = ["s0", "c1", "u1", "t1", "c2", "c3", "u2", "t2", "u3", "w3"]
+LEAN = ("s0", "c1", "u1")
+SEMAPHORES = (["e_v", "e_a", "e_t", "e_g"] + ["d%d" % _k for _k in range(70)] + ["arr_" + _x for _x in XCH]
               + ["out_" + _x for _x in XCH])
 
-ALIAS = {"XS": ("U0", 0), "UL0": ("SG3", 0), "W3": ("U1", 0), "SP": ("U2", 0), "YO": ("P0", 0), "SR": ("TH", HB[3])}
+ALIAS = {"XS": ("S0", 0), "UL0": ("SG3", 0), "W3": ("U1", 0), "YO": ("P0", 0), "SR": ("PR2", 0),
+         "R0": ("TH", HB[3]), "R1": ("TH", HB[3] + 2 * TC), "R2": ("TH", HB[2]),
+         "A0": ("LW", 5 * C), "T0": ("LW", 4 * C)}
 
-PAR = dict(cyc=0.00083 * 1.1, gat=1.4, pe=0.00042 * 1.1, vfix=0.05, afix=0.07, hop=0.06, wake=0.2, dma=1.5, gdma=1.8, far=1.6, first=3.4,
-           rate=6.0e5, row=0.015, farrate=3.0e4, slack=(0.07, 0.15, 0.25), lam=8.0, tries=25000, sort=100, give=0.0005, use=(0, 1, 3, 4), gis=0.5, ris=0.75, wt=128, rounds=4, sgv=0,
-           alt="w0 sp11 sp14 sr0 sr1 sb0 sb1 sb2 oc10 oc11 oc20 oc21 oc30 oc31")
-CASES = [dict(), dict(gat=1.3, dma=1.1, gdma=1.4, far=1.1, row=0.005, farrate=3.8e4, gis=0.9, ris=1.3, wake=0.15),
-         dict(gat=1.3, dma=1.6, gdma=2.0, far=2.0, row=0.025, farrate=2.5e4, wake=0.3, first=4.4),
-         dict(gat=1.3, dma=2.2, gdma=2.8, far=4.0, row=0.008, farrate=3.5e4, wake=0.5, first=7.4),
-         dict(cyc=0.00083 * 1.35, pe=0.00042 * 1.35, gat=1.9), dict(cyc=0.00083 * 1.35, pe=0.00042 * 1.35, gat=1.15)]
+PAR = dict(cyc=0.00083 * 1.1, gat=1.4, pe=0.00042 * 1.1, vfix=0.05, afix=0.07, hop=0.06, wake=0.2, dma=1.5, gdma=1.8, far=1.6, first=6.5, next=2.0, again=(40000, 0.00015),
+           rate=6.0e5, row=0.011, farrate=3.2e4, acc=1.6, slack=(0.07, 0.15, 0.25), lam=8.0, tries=120000, sort=200, give=0.0006, use=(1, 2, 4, 5, 6, 8),
+           gis=0.5, ris=0.75, wt=128, rounds=4, aim=3, most=10, seed=7, tfix=0.012, cuts=(0, 512, 1024, 1536, 2048, 2304, V),
+           first_then=("aONE.0 aMW.0 aMW.256", "vZR.0 vM3J.0 vPJ.2 vPJ.1 vPJ.0 vPF.0 vM3.16 vM3.32 vM3.0 vLM.0 vLM.16 vSEL.0 vBZ.0 vNF.0",
+                       "gM3I.0 gPI.0 gIOT.0 gSEL.32 gIB.0 gID.0", "vP0.0 vBK.0", "vP0.0 vBL.0", "vP0.0 vBV.0", "vP0.0 vHH.0", "vP0.0 vHH.160",
+                       "vP0.0 vHH.320", "vP0.0 vIB2.0", "vP0.0 vNIB.0"),
+           alt="oc10 oc20 oc30 NIB IB2 HH NP BK BV sp11 sp22")
+MARK = 16
+CASES = [dict(gis=0.8), dict(cyc=0.00083, pe=0.00042, gat=1.56, dma=1.3, gdma=1.6, far=1.5, row=0.008, farrate=3.5e4, gis=1.1, ris=1.0, wake=0.15),
+         dict(gat=1.3, dma=1.6, gdma=2.0, far=2.0, row=0.022, farrate=2.5e4, wake=0.3),
+         dict(gat=1.3, dma=2.0, gdma=2.6, far=3.5, row=0.008, farrate=3.5e4, wake=0.4),
+         dict(cyc=0.00083 * 1.35, pe=0.00042 * 1.35, gat=1.9, gis=1.0), dict(cyc=0.00083 * 1.3, pe=0.00042 * 1.3, gat=1.15),
+         dict(cyc=0.00083 * 1.05, pe=0.00042 * 1.15, gat=1.1, row=0.015, farrate=2.4e4, hop=0.14, gis=1.0),
+         dict(cyc=0.00083 * 1.2, pe=0.00042 * 1.2, gat=1.75, hop=0.14, wake=0.35, far=2.5),
+         dict(cyc=0.00083 * 1.1, pe=0.00042 * 1.1, gat=2.0, hop=0.1, gis=1.0),
+         dict(cyc=0.00083 * 1.4, pe=0.00042 * 1.4, gat=1.05, gis=0.8), dict(cyc=0.00083 * 1.15, pe=0.00042 * 1.15, gat=1.15, gis=1.0)]
 LOG = []
 ORDER = {}
 
@@ -84,7 +95,8 @@ def build(g, core, T, topo, PAR):
             return T[x[0]][0:1, x[1]:x[2]]
         if len(x) == 3:
             return T[x[0]][:, x[1]:x[2]]
-        return T[x[0]][:, x[1]:x[2]:x[3]]
+        p0, p1 = (x + ((0, 128),))[4]
+        return T[x[0]][p0:p1, x[1]:x[2]:x[3]]
 
     def width(x):
         return C if len(x) == 1 else len(range(x[1], x[2], x[3] if len(x) > 3 and x[3] != "row" else 1))
@@ -113,7 +125,7 @@ def build(g, core, T, topo, PAR):
             op("v", lambda: g.vector.tensor_scalar(ap(out), ap(x), sc(s1), sc(s2), o0, o1), rd, [out], d)
 
     def tt(out, x, y, o):
-        op("v", lambda: g.vector.tensor_tensor(ap(out), ap(x), ap(y), o), [x, y], [out], vdur(width(x), 1))
+        op("v", lambda: g.vector.tensor_tensor(ap(out), ap(x), ap(y), o), [x, y], [out], vdur(width(x), 1 if "K" in (x[0][0], y[0][0]) else 2))
 
     def cp(out, x):
         op("v", lambda: g.vector.tensor_copy(ap(out), ap(x)), [x], [out], vdur(width(x), max(size(out), size(x)) / 4))
@@ -132,13 +144,13 @@ def build(g, core, T, topo, PAR):
         else:
             op("a", lambda: g.scalar.activation(ap(out), ap(x).indirect(ap(lst)), f, bias=bias, scale=scale), [x, lst], [out], d, f=f)
 
-    def mm(terms, first=True, last=True):
+    def mm(terms, first=True, last=True, each=False):
         def fn():
             ins = None
             for j, (o, l, r) in enumerate(terms):
-                ins = g.tensor.matmul(ap(o), ap(l), ap(r), first and j == 0, last and j == len(terms) - 1)
+                ins = g.tensor.matmul(ap(o), ap(l), ap(r), each or first and j == 0, each or last and j == len(terms) - 1)
             return ins
-        d = sum(max(64, width(r)) * (4 if size(r) == 4 else 1) * PAR["pe"] + 0.005 for o, l, r in terms)
+        d = sum(max(min(64, width(l)), width(r)) * (4 if size(r) == 4 else 1) * PAR["pe"] + PAR["tfix"] for o, l, r in terms)
         op("t", fn, [x for t in terms for x in t[1:]], [t[0] for t in terms], d)
 
     def iota(out, pat, base, cm, flt):
@@ -150,29 +162,35 @@ def build(g, core, T, topo, PAR):
 
     def dma(pairs, rd, wr, nbytes, q="s"):
         e = g.sync if q == "s" else g.scalar
-        op(q, lambda: [e.dma_start(o, i) for o, i in pairs], rd, wr, 0.06 * len(pairs), kind="d", lat=PAR["dma"],
+        op(q, lambda: [e.dma_start(o, i) for o, i in pairs], rd, wr, 0.1 * len(pairs), kind="d", lat=PAR["dma"],
            busy=8 * len(pairs) * PAR["row"] + nbytes / PAR["rate"])
 
-    def add(x, o, i, rd, nbytes):
+    def add(x, o, i, rd, nbytes, **cut):
         first = not any(e["q"] == "g" and e["kind"] == "d" for e in ops)
-        op("g", lambda: [g.dma_start(o, i, accum_op=A.add)], rd + [x], [x], PAR["gis"] + (1.5 if first else 0), kind="d",
-           lat=PAR["gdma"], busy=1.5 * nbytes / PAR["rate"])
+        op("g", lambda: [g.dma_start(o, i, accum_op=A.add, **cut)], rd + [x], [x], PAR["gis"] + (1.5 if first else 0), kind="d",
+           lat=PAR["gdma"], busy=PAR["acc"] * nbytes / PAR["rate"])
 
     def turn(out, src, rd, wr, n):
         for b in range(5):
             op("v", lambda b=b: g.vector.transpose(out(b), src(b)), [rd], [wr], vdur(n, size(rd) / 4), par=1)
 
     peers = [T.cores[(rank + d) % N] for d in range(1, N)]
-    masks, nxt = [], [0, 0]
-    for c in peers:
-        e = topo.engines(core, c)
-        far = 0 if topo.die(c) != topo.die(core) else 1
-        j = 4 * nxt[far] + far
-        nxt[far] += 1
-        masks.append((1 << e[j]) | (1 << e[j + 2]))
+
+    def engines(k):
+        masks, nxt = [], [0, k // 2]
+        for c in peers:
+            e = topo.engines(core, c)
+            near = int(topo.die(c) == topo.die(core))
+            j = 4 * nxt[near] + (near + k) % 2
+            if XCH[k] in LEAN:
+                masks.append(1 << e[(4 * (nxt[near] - near * (k // 2)) + (2 * near, 3 - 2 * near)[k % 2]) % len(e)])
+            else:
+                masks.append((1 << e[j % len(e)]) | (1 << e[(j + 2) % len(e)]))
+            nxt[near] += 1
+        return masks
 
     def share(x, dn, src, win, c0, after=()):
-        s, s0 = T[src[0]], src[1]
+        s, s0, masks = T[src[0]], src[1], engines(XCH.index(x))
         dma([(T[dn][16:128, :], s[16:128, s0:s0 + NB]), (T[dn][128:240, :], s[0:112, s0:s0 + NB])],
             [] if src[0] == "s0" else [(src[0], s0, s0 + NB)], [(dn,)], 1e5)
 
@@ -184,141 +202,132 @@ def build(g, core, T, topo, PAR):
                 trs.append(RemoteDMATransfer(src=T[dn][r0:r0 + 128, :], dst=T[win][:, c0 + (d - 1) * NB:c0 + d * NB],
                                              dst_ids=[DstId(rid=rid, pnc=pid)], dma_engine_mask=masks[d - 1], remote_sem=T.sem["arr_" + x]))
             return g.remote_dma_fused(trs, local_sem=T.sem["out_" + x])
-        op("g", fn, [(dn,)] + list(after), [("X" + x,)], PAR["ris"], kind="r", x=x, lat=PAR["far"], once=PAR["first"] if x == "s0" else 0.0,
-           busy=64 * (PAR["row"] + NB * size((dn,)) / PAR["farrate"]))
+        busy = 60 * (PAR["row"] + NB * size((dn,)) / PAR["farrate"])
+        op("g", fn, [(dn,)] + list(after), [("X" + x,)], PAR["ris"], kind="r", x=x, lat=PAR["far"] + 2 * busy * (x in LEAN),
+           once={"s0": PAR["first"], "c1": PAR["next"]}.get(x, 0.0) - busy * (x in LEAN), busy=busy)
         ops.append(dict(q=None, kind="arr", x=x, rd=[reg(("X" + x,))], wr=[(win, c0, c0 + WN - V)], dur=0.0))
 
-    dma([(T.CN[:, gg], T.cur[gg:8:2, :]) for gg in range(2)], [], [("CN",)], 8e4)
-    dma([(T.PT[:, 0:H], T.pt[:, 0:H])], [], [("PT", 0, H)], 512 * H)
+    dma([(T.CN[:, gg], T.cur[gg:8:2, :]) for gg in range(2)], [], [("CN",)], 8e4, "a")
+    for a, b in ((0, TC), (TC, 3 * TC), (3 * TC, V)):
+        dma([(T.PT[:, a:b], T.pt[:, a:b])], [], [("PT", a, b)], 512 * (b - a), "s" if a else "a")
     dma([(T.S0[:, 0:V], T.s0[:, :])], [], [("S0", 0, V)], 256 * V)
-    dma([(T.PT[:, H:V], T.pt[:, H:V])], [], [("PT", H, V)], 512 * H)
 
     iota(("PI", 0, 8), [[0, 8]], 0, 1, False)
     iota(("M3I", 0, 16), [[-1, 16]], 16, 1, False)
     iota(("IOT", 0, 160), [[1, 160]], -15, 0, True)
-    share("s0", "DS0", ("s0", 0), "S0", V)
+    dma([(T.S0[:, V:WN], T.s0[:, 0:WN - V])], [], [("S0", V, WN)], 256 * (WN - V))
+    share("s0", "DS0", ("s0", 0), "SF", 0)
     iota(("BC", 0, C), [[16, C]], HB[2] - int(OFF), 0, True)
-    for x, n in ((0, ("BH", 0, 128)), (1, ("ONE", 0, TC)), (-OFF, ("CK", 0, 2 * C)), (-V, ("CK", 2 * C, 3 * C)), (-6, ("CK", 4 * C, 5 * C))):
+    fill(("ZR", 0, TC), 0.0)
+    act(("ONE", 0, C), ("ZR", 0, C), F.Sigmoid, 1.0, 256.0)
+    for x, n in ((-1, ("NEG", 0, H // 2)), (-OFF, ("CK", 0, 128)), (-V, ("CK", 2 * C, 3 * C)), (-6, ("CK", 3 * C, 4 * C))):
         iota(n, [[0, width(n)]], int(x), 0, True)
-    act(("CK", 3 * C, 3 * C + 128), ("ONE", 0, 128), F.Identity, 2.0 ** -12)
-    row = {1.0: ("ONE", 0), -OFF: ("CK", 0), -float(V): ("CK", 2 * C), -6.0: ("CK", 4 * C)}
+    iota(("CK", 4 * C, 6 * C), [[-144 * 17, 2], [0, C]], 144 * 16, 0, True)
+    row = {1.0: ("ONE", 0), -1.0: ("NEG", 0), -OFF: ("CK", 0), -float(V): ("CK", 2 * C), -6.0: ("CK", 3 * C), "wrap": ("CK", 4 * C)}
 
     def const(out, x, by=("ONE", 0, 128, "row")):
         n, c0 = row[x]
         return (out, by, (n, c0, c0 + width(out)) + by[3:])
 
-    sgn = -1.0 if "pa" in ALT else 1.0
-    if "w0" in ALT:
-        for a, b in ((0, H), (H, V), (V, WN)):
-            if "wd" in ALT:
-                if a == 0:
-                    iota(("G", 0, H), [[0, H]], 1, 0, True)
-                dma([(T.U3[:, a:b], T.G[:, 0:b - a])], [("G", 0, H)], [("U3", a, b)], 512 * (b - a))
-            else:
-                iota(("U3", a, b), [[0, b - a]], 1, 0, True)
-            add(("U3", a, b), T.U3[:, a:b], (T.s0 if a < V else T.S0)[:, a:b], [] if a < V else [("S0", V, WN)], 512 * (b - a))
-    if "pa" in ALT:
-        op("g", lambda: g.affine_select(T.HF[:], T.S0[:, 0:H], [[0, H]], A.not_equal, -0.5, 0, 0), [("S0", 0, H)], [("HF", 0, H)], 0.17 + 2 * H * PAR["cyc"])
-        op("g", lambda: g.affine_select(T.P2I[:], T.BH[:, 0:128], [[-1, 128]], A.not_equal, 2.0, 0, 1), [("BH", 0, 128)], [("P2I", 0, 128)], 0.4)
+    for a, b in ((0, H), (H, V), (V, WN)):
+        iota(("U3", a, b), [[0, b - a]], 1, 0, True)
+        add(("U3", a, b), T.U3[:, a:b], T.s0[:, a:b] if a < V else T.SF[:], [] if a < V else [("SF", 0, WN - V)], 512 * (b - a))
     col = lambda j: ("PF", j, j + 1)
-    for j, m in enumerate((112, 3, 15)):
+    for j, m in enumerate((112, 115, 15)):
         ts(("PJ", j, j + 1), ("PI", j, j + 1), m, A.bitwise_and)
     ts(("M3J", 0, 16), ("M3I", 0, 16), 15, A.bitwise_and)
     cp(("PF", 0, 3), ("PJ", 0, 3))
-    ts(("M3", 0, 16), ("M3J", 0, 16), 3.0, A.is_lt)
+    ts(("M3", 16, 32), ("M3J", 0, 16), 3.0, A.is_lt)
+    ts(("M3", 32, 48), ("M3J", 0, 16), 0.0, A.is_equal, -2.0, A.mult)
+    tt(("M3", 0, 16), ("M3", 16, 32), ("M3", 32, 48), A.add)
     ts(("LM", 0, 16), ("IOT", 15, 31), 0.0, A.mult, col(2), A.add)
     cp(("LM", 16, 32), ("IOT", 15, 31))
-    act(col(3), col(1), F.Identity, 4.0, col(0))
-    act(col(4), col(1), F.Identity, 1.0, col(0))
-    act(col(6), col(1), F.Identity, -1.0, col(2))
-    act(("MW", 0, 256), ("M3", 0, 16), F.Identity, lst=("LM", 0, 16))
-    act(("MW", 256, 512), ("M3", 0, 16), F.Identity, 2.0 ** -12, lst=("LM", 16, 32))
-    ts(("PF", 8, 12), ("IOT", 15, 31, 4), col(6), A.is_equal)
-    ts(("PF", 12, 15), ("IOT", 15, 27, 4), col(2), A.is_equal)
-    ts(("B1", 0, 144), ("IOT", 12, 156), col(3), A.is_equal)
-    ts(("B2B", 0, 144), ("IOT", 3, 147), col(4), A.is_equal)
-    ts(("B2", 0, 144), ("B2B", 0, 144), 1.0, A.mult)
-    ts(("NB2", 0, 144), ("B2B", 0, 144), -1.0, A.mult)
-    ts(("N2B2", 0, 144), ("B2B", 0, 144), -2.0, A.mult)
+    for tau in range(2):
+        act(("MW", 256 * tau, 256 * (tau + 1)), ("M3", 0, 16), F.Identity, (1.0, 2.0 ** -12)[tau], lst=("LM", 16 * tau, 16 * (tau + 1)))
+    for tau in range(2):
+        fill(("PF", 4, 5, 1, (32 * tau, 32 * tau + 32)), (0.0, -0.42)[tau])
+    iota(("SEL", 32, 64), [[1, 4], [16, 8]], 0, 0, True)
+    ts(("SEL", 0, 32), ("SEL", 32, 64), col(1), A.is_equal)
     ts(("BZ", 0, 144), ("IOT", 0, 144), col(0), A.is_equal)
-    act(col(12), col(12), F.Identity, -float(WN))
+    ts(("PF", 12, 15), ("IOT", 15, 27, 4), col(2), A.is_equal)
+
+    def lin(out, x, scale, bias):
+        if out[0] in ALT:
+            ts(out, x, scale, A.mult, bias, A.add)
+        else:
+            act(out, x, F.Identity, scale, bias)
+
     act(col(13), col(13), F.Identity, 1.0, col(14))
-    act(("BL", 0, 144), ("BZ", 0, 144), F.Identity, col(12))
-    act(("BV", 0, 144), ("BZ", 0, 144), F.Identity, col(13))
-    for t in range(4):
-        act(("BT%d" % t, 0, 144), ("B2B", 0, 144), F.Identity, col(8 + t))
-    for n, w in (("N2I", -2.0), ("IB", 1.0), ("NIB", -1.0), ("ID", 1.0), ("IBL", -float(WN)), ("IB16", 16.0)):
-        op("g", lambda n=n, w=w: g.affine_select(T[n][:], T.BH[:, 0:128], [[-1, 128]], A.not_equal, w, 0, 1),
-           [("BH", 0, 128)], [(n, 0, 128)], 0.17 + 256 * PAR["cyc"])
-    act(("BK", 0, C), ("BC", 0, C), F.Identity, 1.0, col(2))
-    act(col(7), col(2), F.Identity, 56.0, V - OFF)
-    act(("BH", 128, 128 + 56), ("ONE", 0, 56), F.Identity, col(7))
-    act(("BH", 192, 192 + 56), ("IOT", 15, 15 + 56), F.Identity)
-    I, N2I, IB, NIB, IB16, IBL = ((n, 0, 128) for n in ("ID", "N2I", "IB", "NIB", "IB16", "IBL"))
+    ts(("BL", 0, 144), ("BZ", 0, 144), col(12), A.mult, -float(WN), A.mult)
+    lin(("BV", 0, 144), ("BZ", 0, 144), col(13), 0.0)
+    for n, w in (("IB", 1.0), ("NIB", -1.0), ("IB2", 2.0), ("ID", 1.0), ("N2I", -2.0), ("P2I", 2.0), ("IBL", -float(WN)), ("IB16", 16.0), ("IBW", -16.0)):
+        if n in ALT:
+            ts((n, 0, 128), ("IB", 0, 128), w, A.mult)
+            continue
+        op("g", lambda n=n, w=w: g.affine_select(T[n][:], T.ZR[:, 0:128], [[-1, 128]], A.not_equal, w, 0, 1),
+           [("ZR", 0, 128)], [(n, 0, 128)], 0.17 + 256 * PAR["cyc"])
+    lin(("BK", 0, C), ("BC", 0, C), 1.0, col(2))
+    act(col(10), col(2), F.Identity, 56.0, V - OFF)
+    act(("BH", 0, 56), ("ZR", 0, 56), F.Identity, 1.0, col(10))
+    iota(("BH", 64, 64 + 56), [[1, 56]], 0, 0, True)
+    I, N2I, IB, NIB, IB2, IB16, IBW, IBL = ((n, 0, 128) for n in ("ID", "N2I", "IB", "NIB", "IB2", "IB16", "IBW", "IBL"))
     sl = lambda n, j, w=1: (n, j * C, (j + w) * C)
 
     cp(("NF",), ("CN",))
     turn(lambda b: T.CB[:, b:C:5], lambda b: T.NF[:, :, b, :], ("NF",), ("CB", 0, C), 32)
     cp(("LC", 0, C), ("CB", 0, C))
-    cp(("CI", 0, C), ("CB", 0, C))
+    for j, (d, o) in enumerate(((2, 128 - 0.2), (16, 144 - 0.47), (32, 200 - 0.49))):
+        lin(sl("HH", j), sl("CB", 0), 1.0 / d, o)
+    mm([(sl("K5", 0), IB2, sl("HH", 0)), (sl("K5", 0), NIB, sl("CB", 0))])
+    mm([(sl("K5", 1), IB2, sl("HH", 2)), (sl("K5", 1), NIB, sl("HH", 1))])
+    lin(sl("NP", 0, 2), sl("K5", 0, 2), 1.0, -255.0)
+
+    WC = (0, 32, C)
 
     def masked(tau, h):
-        gtt(("P%d" % tau, h * H, (h + 1) * H), ("MW", 256 * tau, 256 * (tau + 1)), ("LC", HC * h, HC * (h + 1)), ("PT", h * H, (h + 1) * H))
+        for a, b in (((0, TC),), ((TC, 3 * TC), (3 * TC, V)))[h]:
+            gtt(("P%d" % tau, a, b), ("MW", 256 * tau, 256 * (tau + 1)), ("LC", a // 16, b // 16), ("PT", a, b))
 
     def classes(tau, h):
-        k = "K%d" % (2 * tau + h)
-        mm([const((k, 0, 4 * HC), -OFF, (("ONE", 0, 128, "row"), ("CK", 3 * C, 3 * C + 128, "row"))[tau])], True, False)
-        for t in range(4):
-            mm([((k, t * HC, (t + 1) * HC), ("B1", 3 - u, 131 - u), ("P%d" % tau, h * H + 4 * t + u, (h + 1) * H, 16)) for u in range(4)], False, t == 3)
+        k, m = ("K0", "K%d" % (1 + 2 * tau))[h], ((32 * tau, 32 * tau + 32), (0, 128))[h]
+        for j0 in range(0, 16, 4):
+            mm([((k, j, TC, 16, m), ("P%d" % tau, 16 * WC[h] + j, 16 * WC[h + 1], 16), ("SEL", 0, 32)) for j in range(j0, j0 + 4)], each=True)
 
-    def field(tau, h):
-        k, o = ("K%d" % (2 * tau + h), 0, 4 * HC), ("EX%d" % tau, 4 * HC * h, 4 * HC * (h + 1))
-        if tau == 0:
-            r = ("SR", 4 * HC * h, 4 * HC * (h + 1))
-            if "sr%d" % h in ALT:
-                act(r, k, F.Identity, 1.0, 1.5 * 2.0 ** 35)
-                act(r, r, F.Identity, 1.0, -1.5 * 2.0 ** 35)
-            else:
-                ts(r, k, 1.5 * 2.0 ** 35, A.add, -1.5 * 2.0 ** 35, A.add)
-            tt(o, k, r, A.subtract)
-        else:
-            ts(o, k, 1.5 * 2.0 ** 23, A.add, -1.5 * 2.0 ** 23 - OFF, A.add)
+    def signed(tau, h, s):
+        a = TC * (s > 0)
+        if h:
+            act(("R%d" % (1 + tau), a, a + TC), ("K%d" % (1 + 2 * tau), 0, TC), F.Relu, s, (0.0, -0.42)[tau])
+        elif tau == 0:
+            act(("R0", a, a + TC, 1, (0, 64)), ("K0", 0, TC, 1, (0, 64)), F.Relu, s, ("PF", 4, 5, 1, (0, 64)))
 
-    nsel = [0]
+    def route(tau, h, s, out, some):
+        a, o = TC * (s > 0), (out[0], out[1] + WC[h], out[1] + WC[h + 1])
+        r, m = ("R0", "R%d" % (1 + tau))[h], ((32 * tau, 32 * tau + 32), (0, 128))[h]
+        mm([const(o, -OFF)] * (tau == 0) + [(o, (r, a + 128 * c, a + 128 * (c + 1), 1, m), ("ID",) + m + (1, m)) for c in some])
 
-    def pick(tau, d, h):
-        k = "K%d" % (4 + nsel[0] % 2)
-        nsel[0] += 1
-        for t in range(4):
-            mm([((k, t * HC, (t + 1) * HC), ("BT%d" % t, 12 - 4 * ((j + d) % 4), 140 - 4 * ((j + d) % 4)),
-                 ("OH", (2 * j + tau) * C + HC * h, (2 * j + tau) * C + HC * (h + 1))) for j in range(4)])
-        a, b = 4 * HC * h, 4 * HC * (h + 1)
-        tt(("E%d%d" % (tau, d), a, b), ("EX%d" % tau, a, b), (k, 0, 4 * HC), A.mult)
+    def low(out, k, r):
+        ts(r, k, 1.5 * 2.0 ** 35, A.add, -1.5 * 2.0 ** 35, A.add)
+        tt(out, k, r, A.subtract)
 
-    def name(out, src, sign, hs=(0, 1)):
-        return [((out[0], out[1] + HC * h, out[1] + HC * (h + 1)), ({1: "B2", -1: "NB2", -2: "N2B2"}[sign], 12 - 4 * t, 140 - 4 * t),
-                 (src, 4 * HC * h + HC * t, 4 * HC * h + HC * (t + 1))) for h in hs for t in range(4)]
+    def apart(out, tau):
+        return [(out, IB, sl("LW", 2 * tau + 1)), (out, NIB, sl("LW", 2 * tau))]
+
+    def second(out, tau):
+        return [(out, IB, sl("LW", 2 * tau)), (out, I, sl("XP", tau))]
 
     def zero(out):
-        return (out, ("BH", 0, 128, "row"), ("ONE", 0, width(out), "row"))
+        return (out, ("ZR", 0, 128, "row"), ("ZR", 0, width(out), "row"))
 
     def parts(k, src):
-        fl = "FL%d" % k
-        if "hi%d" % k in ALT:
-            act(sl("HI", 0), src, F.Identity, 1.0, 1.5 * 2.0 ** 29)
-            act(sl(fl, 3), sl("HI", 0), F.Identity, 1.0, -1.5 * 2.0 ** 29)
-        else:
-            ts(sl(fl, 3), src, 1.5 * 2.0 ** 29, A.add, -1.5 * 2.0 ** 29, A.add)
-        if "lo%d" % k in ALT:
-            act(sl(fl, 4), sl("HI", 0), F.Identity)
-        else:
-            tt(sl(fl, 4), src, sl(fl, 3), A.subtract)
+        hi, lo = sl("FL%d" % k, 3), sl("FL%d" % k, 4)
+        cp(hi, src)
+        tt(lo, src, hi, A.subtract)
 
     def rows(k):
         j0 = 1 if k == 0 else 0
         fl = T["FL%d" % k]
         turn(lambda b: T.NA[:, j0:3, :, b, :], lambda b: fl[:, 2 + j0:5, b:C:5], sl("FL%d" % k, 2 + j0, 3 - j0), ("NA",), 32 * (3 - j0))
-        dma([(T.U0[16 * gg + 4 * j:128:32, 0:V], T.NA[:, j, gg]) for j in range(j0, 3) for gg in range(2)], [("NA",)], [("XS", 0, V)], 1e5)
+        dma([(T.S0[16 * gg + 4 * j:128:32, 0:V], T.NA[:, j, gg]) for j in range(j0, 3) for gg in range(2)], [("NA",)], [("XS", 0, V)], 1e5)
 
     def own_copy(k, a, b):
         o = T.SG3 if k == 0 else T.UL
@@ -329,40 +338,40 @@ def build(g, core, T, topo, PAR):
             return
         dma([(o[:, a:b], T["U%d" % k][:, a:b])], [("U%d" % k, a, b)], [("UL0" if k == 0 else "UL", a, b)], (256 if k == 0 else 512) * (b - a))
 
-    for h in range(2):
-        masked(0, h)
-        classes(0, h)
-    ts(sl("C3", 0), ("CI", 0, C), 3, A.bitwise_and)
-    ts(sl("C3", 1), ("CI", 0, C), 4, A.logical_shift_right, 3, A.bitwise_and)
-    cp(sl("C3B", 0, 2), sl("C3", 0, 2))
-    for k in range(4):
-        ts(sl("OH", 2 * k, 2), sl("C3B", 0, 2), float(k), A.is_equal)
-    if "u0" in ALT:
-        dma([(T.VO[:, 0:NB], T.s0[:, 0:NB])], [], [("VO", 0, NB)], 3e4)
-        act(("SB", 0, NB), ("VO", 0, NB), F.Abs)
-        share("u0", "DU0", ("SB", 0), "U0", V)
+    for tau, h in ((0, 0), (1, 0), (0, 1)):
+        masked(tau, h)
+        classes(tau, h)
     for h in range(2):
         act(("U0", h * H, (h + 1) * H), ("S0", h * H, (h + 1) * H), F.Abs)
         own_copy(0, h * H, (h + 1) * H)
     for h in range(2):
-        if h < PAR["sgv"]:
-            ts(("SG0", h * H, (h + 1) * H), ("S0", h * H, (h + 1) * H), 0.0, A.is_ge, 0.5, A.subtract)
-        else:
-            act(("SG0", h * H, (h + 1) * H), ("S0", h * H, (h + 1) * H), F.Sign, 1.0, 2.0 ** -30)
-    if "u0" not in ALT:
-        act(("U0", V, WN), ("S0", V, WN), F.Abs)
+        act(("SG0", h * H, (h + 1) * H), ("S0", h * H, (h + 1) * H), F.Sign, 1.0, 2.0 ** -30)
+    act(("U0", V, WN), ("SF", 0, WN - V), F.Abs)
     for h in range(2):
-        field(0, h)
-        pick(0, 0, h)
-        kb = "K%d" % (6 + h)
-        mm(name((kb, 0, C), "E00", 1, (h,)))
-        ts(("LS0", HC * h, HC * (h + 1)), (kb, HC * h, HC * (h + 1)), OFF, A.add)
-    for h in range(2):
-        mm(name(sl("K6", 1), "E00", 1, (h,)))
+        a, b, kb = WC[h], WC[h + 1], "K%d" % (6 + h)
+        signed(0, h, -1)
+        route(0, h, -1, (kb, 0), range(4))
+        low(("A0", a, b), (kb, a, b), ("SR", a, b))
+        ts(("LS0", a, b), ("A0", a, b), OFF, A.add)
+    mm([(sl("K6", 1), IB, sl("A0", 0))])
     parts(0, sl("K6", 1))
+    masked(1, 1)
+    classes(1, 1)
     for h in range(2):
-        masked(1, h)
-        classes(1, h)
+        signed(1, h, -1)
+        route(1, h, -1, sl("K5", 0), range(4))
+    cp(sl("LS0", 1), sl("K5", 0))
+    ts(sl("T0", 0), sl("LS0", 1), -OFF, A.add)
+    for tau in range(2):
+        for h in range(2):
+            signed(tau, h, 1)
+            for odd in range(2):
+                route(tau, h, 1, sl("K%d" % (4 + tau), odd), (odd, odd + 2))
+    low(sl("LW", 0, 2), sl("K4", 0, 2), sl("SR", 1, 2))
+    ts(sl("LW", 2, 2), sl("K5", 0, 2), 1.5 * 2.0 ** 23, A.add, -1.5 * 2.0 ** 23 - OFF, A.add)
+    for tau in range(2):
+        mm(apart(sl("K4", tau), tau))
+    tt(sl("XP", 0, 2), sl("K4", 0, 2), sl("NP", 0, 2), A.mult)
 
     LA = ("LS0", "LS0", "LS1", "LS2")
     SGB = 1.75 + 2.0 ** -23
@@ -372,7 +381,8 @@ def build(g, core, T, topo, PAR):
         gtt(("P%d" % (k % 2), a, b), ("U%d" % k, 0, WN), (LA[k], a // 16, b // 16), ("UL0" if k == 0 else "UL", a, b))
 
     def u_op(k, a, b):
-        act(("U%d" % (k + 1), a, b), ("P%d" % (k % 2), a, b), F.Abs, -2.0, 1.0)
+        w = math.sqrt(2.0) if k == 2 else 1.0
+        act(("U%d" % (k + 1), a, b), ("P%d" % (k % 2), a, b), F.Abs, -2.0 * w, w)
 
     def sg_op(k, a, b):
         e = 1.0 if k % 2 else -1.0
@@ -380,19 +390,19 @@ def build(g, core, T, topo, PAR):
 
     def cross(k, h):
         o, i, a, b = "SG%d" % (k - 1), "SG%d" % k, h * H, (h + 1) * H
-        add((o, a, b), T[o][:, a:b], T[i][:, a:b], [(i, a, b)], 256 * H)
+        if "cw%d" % k not in ALT:
+            add((o, a, b), T[o][:, a:b], T[i][:, a:b], [(i, a, b)], 256 * H)
+        elif h:
+            add((o, 0, V), T[o][:, 0:V], T[i][:, 0:V], [(i, 0, V)], 256 * V, max_dma_last_dim=2 * H)
 
     def s_path(k):
         p_op(k, 0, NB)
         u_op(k, 0, NB)
         sg_op(k, 0, NB)
-        if "sb%d" % k in ALT:
-            mm([(("K7", 0, NB), IB, ("SG%d" % j, 0, NB)) for j in (k, k + 1)])
-            act(("SB", 0, NB), ("K7", 0, NB), F.Identity)
-        else:
-            tt(("SB", 0, NB), ("SG%d" % k, 0, NB), ("SG%d" % (k + 1), 0, NB), A.add)
+        mm([(("K7", 0, NB), IB, ("SG%d" % j, 0, NB)) for j in (k, k + 1)])
+        act(("SB", 0, NB), ("K7", 0, NB), F.Identity)
         share("u%d" % (k + 1), "DU%d" % (k + 1), ("U%d" % (k + 1), 0), "U%d" % (k + 1), V,
-              [("TH", 0, V)] if k == 1 and "w0" in ALT else [])
+              [("TH", 0, V)] if k == 1 else [])
         share("c%d" % (k + 1), "DG%d" % (k + 1), ("SB", 0), "SG%d" % k, V)
         p_op(k, NB, H)
         p_op(k, H, V)
@@ -406,44 +416,26 @@ def build(g, core, T, topo, PAR):
             own_copy(k + 1, h * H, (h + 1) * H)
 
     def y_path(k):
-        if k == 0 and "w0" in ALT:
+        if k == 0:
             for a, b in ((0, NB), (NB, H), (H, V)):
-                if "pa" in ALT:
-                    add(("P0", a, b), T.P0[:, a:b], T.HF[:, 0:b - a], [("HF", 0, H)], 512 * (b - a))
-                else:
-                    act(("G", a, b), ("P0", a, b), F.Identity, -1.0, 0.5)
-                gtt(("TH", a, b), ("U3", 0, WN), ("LS0", a // 16, b // 16), ("P0" if "pa" in ALT else "G", a, b))
+                act(("G", a, b), ("P0", a, b), F.Identity, 1.0, -0.5)
+                gtt(("TH", a, b), ("U3", 0, WN), ("LS0", a // 16, b // 16), ("G", a, b))
                 if a == 0:
                     share("t1", "DT1", ("TH", 0), "TH", V)
             return
-        for a, b in ((0, TC), (TC, H), (H, V)) if k == 0 else ((0, TC), (TC, 3 * TC), (3 * TC, V)):
-            if k == 0 and "g%d" % min(2, a // TC) in ALT:
-                x, w, lst = ("G", a, b), ("S0", 0, WN), ("LS0", a // 16, b // 16)
-                op("v", lambda x=x, w=w, lst=lst: g.vector.tensor_scalar(ap(x), ap(w).indirect(ap(lst)), 0.5, 0.5, A.mult, A.add),
-                   [w, lst], [x], vdur(b - a, PAR["gat"]))
-            elif k == 0:
-                act(("G", a, b), ("S0", 0, WN), F.Identity, 0.5, 0.5, lst=("LS0", a // 16, b // 16))
-            else:
-                act(("G", a, b), ("TH", 0, k * WN), F.Sigmoid, 4.0 * sgn, lst=(("LS0", "LG")[k - 1], a // 16, b // 16))
+        for a, b in ((0, TC), (TC, 3 * TC), (3 * TC, V)):
+            act(("G", a, b), ("TH", 0, k * WN), F.Sigmoid, -4.0, lst=(("LS0", "LG")[k - 1], a // 16, b // 16))
         for a in range(0, V, TC):
             kb, p = ("K%d" % (nsp[0] % 2), 0, TC), ("P%d" % (k % 2), a, a + TC)
             nsp[0] += 1
             if "sp%d%d" % (k, a // TC) in ALT:
-                act(kb, p, F.Identity, -2.0 * sgn, sgn)
-            elif sgn > 0:
-                mm([const(kb, 1.0), (kb, N2I, p)])
+                act(kb, p, F.Identity, 2.0, -1.0)
             else:
-                mm([const(kb, 1.0, NIB), (kb, ("P2I", 0, 128), p)])
+                mm([const(kb, -1.0), (kb, ("P2I", 0, 128), p)])
             tt(("TH", HB[k] + a, HB[k] + a + TC), ("G", a, a + TC), kb, A.mult)
-            if (k, a) == (0, 0):
-                share("t1", "DT1", ("TH", 0), "TH", V)
 
     def via(k, h):
-        x, w, lst = ("VO", h * H, (h + 1) * H), ("XS", 0, WN), (LA[k], HC * h, HC * (h + 1))
-        if "vi%d%d" % (k, h) in ALT:
-            op("v", lambda: g.vector.tensor_copy(ap(x), ap(w).indirect(ap(lst))), [w, lst], [x], vdur(H, PAR["gat"]))
-        else:
-            act(x, w, F.Identity, lst=lst)
+        act(("VO", h * H, (h + 1) * H), ("XS", 0, WN), F.Identity, lst=(LA[k], HC * h, HC * (h + 1)))
 
     def wrap(out, sel, src, h):
         return [((out[0], out[1] + HC * h, out[1] + HC * (h + 1)), (sel, 15 - i, 143 - i), (src, h * H + i, (h + 1) * H, 16)) for i in range(16)]
@@ -458,42 +450,33 @@ def build(g, core, T, topo, PAR):
         ts(sl(fl, 1), z, 3.0, A.is_ge)
         ts(sl(fl, 2), z, -13.0, A.is_le)
 
-    old = lambda out, k, s: [(out, IB if s > 0 else NIB, sl("FL%d" % k, 3)), (out, IB if s > 0 else NIB, sl("FL%d" % k, 4))]
+    def old(out, k, s):
+        d = IB if s > 0 else NIB
+        return [(out, d, sl(("A0", "N2")[k], 0))]
 
-    s_path(0)
-    dma([(T.U0[4 * j:128:16, V:WN], T.BH[:, c0:c0 + 56]) for j, c0 in enumerate((0, 128, 192))], [("BH", 0, 256)], [("XS", V, WN)], 5e4)
+    dma([(T.S0[4 * j:128:16, V:WN], x) for j, x in enumerate((T.ZR[:, 0:56], T.BH[:, 0:56], T.BH[:, 64:120]))], [("ZR", 0, 56), ("BH", 0, 128)], [("XS", V, WN)], 5e4)
     rows(0)
-    for h in range(2):
-        field(1, h)
-        pick(1, 0, h)
-        mm(name(sl("K7", 1), "E10", 1, (h,)))
-    ts(sl("LS0", 1), sl("K7", 1), OFF, A.add)
+    s_path(0)
     s_rest(0)
     y_path(0)
-    for tau in range(2):
-        for h in range(2):
-            pick(tau, 1, h)
-    ts(sl("C3", 2), ("CI", 0, C), 15, A.bitwise_and)
-    cp(sl("C3B", 2), sl("C3", 2))
 
     s_path(1)
-    mm(old(sl("K3", 1), 0, -1) + name(sl("K3", 1), "E01", 1))
-    for h in range(2):
-        mm(name(sl("K3", 2), "E11", 1, (h,)) + name(sl("K3", 2), "E10", -1, (h,)))
+    mm(old(sl("K3", 1), 0, -1) + second(sl("K3", 1), 0))
+    mm([(sl("K3", 2), NIB, sl("T0", 0))] + second(sl("K3", 2), 1))
     mm(old(sl("K3", 0), 0, -1), True, False)
     for h in range(2):
         via(1, h)
         mm(wrap(sl("K3", 0), "BV", "VO", h), False, h == 1)
     for tau in range(2):
-        mm([const(sl("K4", tau), -OFF, NIB)] + name(sl("K4", tau), "EX%d" % tau, 1) + name(sl("K4", tau), "E%d1" % tau, -2)
-           + (name(sl("K4", 1), "E10", -1) if tau else old(sl("K4", 0), 0, -1)))
+        mm(apart(sl("K4", tau), tau) + [(sl("K4", tau), N2I, sl("XP", tau))])
     lb, lo = ("K6", 0, 2 * C + 8), ("K6", 2 * C, 2 * C + 8)
-    mm([zero(lb)] + old(sl("K6", 0), 0, 1) + name(sl("K6", 1), "E10", 1) + [(lo, IBL, ("ONE", 0, 8)), (lo, I, ("BK", 0, 8))], True, False)
+    mm([zero(lb)] + old(sl("K6", 0), 0, 1) + [(sl("K6", 1), IB, sl("T0", 0)), (lo, IBL, ("ONE", 0, 8)), (lo, I, ("BK", 0, 8))], True, False)
     z_op(1)
     s_rest(1)
     tt(sl("PR1", 0, 3), sl("K3", 0, 3), sl("FL1", 0, 3), A.mult)
     mm([(sl("K6", 0), I, sl("PR1", 0)), (sl("K6", 0), I, sl("PR1", 1)), (sl("K6", 1), I, sl("PR1", 2)), (lo, IBL, ("FL1", 2 * C, 2 * C + 8))], False, True)
     ts(("LS1", 0, 2 * C + 8), lb, OFF, A.add)
+    ts(sl("N2", 0, 2), sl("LS1", 0, 2), -OFF, A.add)
     parts(1, sl("K6", 0))
     rows(1)
     tt(sl("PR1", 3, 2), sl("K4", 0, 2), sl("FL1", 1, 2), A.mult)
@@ -502,13 +485,12 @@ def build(g, core, T, topo, PAR):
     share("t2", "DT2", ("TB", 0), "TH", WN + V, [("P1", 0, V)])
 
     s_path(2)
-    mm(old(sl("K3", 1), 1, -1) + name(sl("K3", 1), "E01", 1) + [(sl("K3", 1), I, sl("PR1", 3))])
-    mm([(sl("K3", 2), I, sl("PR1", 4)), (sl("K3", 2), N2I, sl("PR1", 2)), (sl("K3", 2), I, sl("PR1", 2))]
-       + name(sl("K3", 2), "E11", 1) + name(sl("K3", 2), "E10", -1))
+    mm(old(sl("K3", 1), 1, -1) + second(sl("K3", 1), 0) + [(sl("K3", 1), I, sl("PR1", 3))])
+    mm([(sl("K3", 2), NIB, sl("N2", 1)), (sl("K3", 2), I, sl("PR1", 4))] + second(sl("K3", 2), 1))
     mm(old(sl("K3", 0), 1, -1), True, False)
     mm([(sl("K4", 0), IBL, ("ONE", 0, C)), (sl("K4", 0), IBL, sl("FL1", 2))])
-    mm([zero(sl("K6", 0, 3))] + old(sl("K6", 0), 1, 1) + name(sl("K6", 1), "E10", 1)
-       + [(sl("K6", 1), I, sl("PR1", 2)), (sl("K6", 2), I, sl("BK", 0))], True, False)
+    mm([zero(sl("K6", 0, 3))] + old(sl("K6", 0), 1, 1)
+       + [(sl("K6", 1), IB, sl("N2", 1)), (sl("K6", 2), I, sl("BK", 0))], True, False)
     mm(old(sl("K5", 0), 1, 1), True, False)
     for h in range(2):
         via(2, h)
@@ -526,37 +508,35 @@ def build(g, core, T, topo, PAR):
     for a, b in ((0, NB), (NB, H), (H, V - PAR["wt"]), (V - PAR["wt"], V)):
         if b == V:
             if a < b:
-                act(("G", a, b), ("TH", 0, HB[2] + b), F.Tanh, 2.0 * sgn, lst=("LS2", 2 * C + a // 16, 2 * C + b // 16))
+                act(("G", a, b), ("TH", 0, HB[2] + b), F.Tanh, -2.0, lst=("LS2", 2 * C + a // 16, 2 * C + b // 16))
                 act(("W3", a, b), ("G", a, b), F.Identity, 0.5, 0.5)
             continue
-        act(("W3", a, b), ("TH", 0, HB[2] + b), F.Sigmoid, 4.0 * sgn, lst=("LS2", 2 * C + a // 16, 2 * C + b // 16))
+        act(("W3", a, b), ("TH", 0, HB[2] + b), F.Sigmoid, -4.0, lst=("LS2", 2 * C + a // 16, 2 * C + b // 16))
         if a == 0:
             share("w3", "DW3", ("U1", 0), "U1", V)
     for h in range(2):
-        p_op(3, h * H, (h + 1) * H)
-        if "s4%d" % h in ALT:
-            ts(("SP", h * H, (h + 1) * H), ("P1", h * H, (h + 1) * H), -2.0 * sgn, A.mult, sgn, A.add)
-        else:
-            act(("SP", h * H, (h + 1) * H), ("P1", h * H, (h + 1) * H), F.Identity, -2.0 * sgn, sgn)
+        a, b = h * H, (h + 1) * H
+        p_op(3, a, b)
+        act(("P1", a, b), ("P1", a, b), F.Identity, 1.0, -1.0)
     mm([const(sl("K4", 0), -float(V)), (sl("K4", 0), I, sl("PR2", 3))])
     mm([(sl("K6", 0), I, sl("BK", 0))], True, False)
     z_op(3)
     tt(sl("PR3", 0), sl("K4", 0), sl("FL3", 2), A.mult)
     mm([(sl("K6", 0), I, sl("PR3", 0))], False, True)
     ts(sl("LS3", 0), sl("K6", 0), V + OFF, A.add)
-    cuts = (0, TC, 2 * TC, 3 * TC, 4 * TC, 4 * TC + 256, V)
+    cuts = PAR["cuts"]
     for a, b in zip(cuts, cuts[1:]):
-        gtt(("TH", HB[3] + a, HB[3] + b), ("W3", 0, WN), ("LS2", a // 16, b // 16), ("SP", a, b))
-        act(("YO", a, b), ("TH", 0, HB[3] + b), F.Tanh, 2.0 * sgn, lst=("LS3", a // 16, b // 16))
+        gtt(("TH", HB[3] + a, HB[3] + b), ("W3", 0, WN), ("LS2", a // 16, b // 16), ("P1", a, b))
+        act(("YO", a, b), ("TH", 0, HB[3] + b), F.Tanh, -2.0, lst=("LS3", a // 16, b // 16))
         dma([(T.y[:, a:b], T.P0[:, a:b])], [("YO", a, b)], [], 512 * (b - a))
 
     turns = lambda out, j, w, ks: [(out, w, sl("FL%d" % k, j)) for k in ks]
     for ks in ((1, 2), (3,)):
-        head = [zero(sl("K5", 0, 2)), (sl("K5", 0), IB16, sl("C3B", 2)), (sl("K5", 1), IB, sl("CB", 0))] if ks[0] == 1 else []
-        mm(head + turns(sl("K5", 0), 1, IB16, ks) + turns(sl("K5", 1), 2, IB16, ks), ks[0] == 1, ks[0] == 3)
+        head = [const(sl("K5", 0, 2), "wrap"), (sl("K5", 0), IB, sl("CB", 0)), (sl("K5", 0), IBW, sl("HH", 1)), (sl("K5", 1), IB, sl("HH", 1))] if ks[0] == 1 else []
+        mm(head + turns(sl("K5", 0), 1, IB, ks) + turns(sl("K5", 1), 2, IB, ks), ks[0] == 1, ks[0] == 3)
         head = [(sl("K7", 0), IB, sl("CB", 0))] if ks[0] == 1 else []
         mm(head + turns(sl("K7", 0), 1, IB, ks) + turns(sl("K7", 0), 2, IB16, ks), ks[0] == 1, False)
-    ts(sl("WR", 0, 2), sl("K5", 0, 2), 256.0, A.is_ge, -16.0, A.mult)
+    ts(sl("WR", 0, 2), sl("K5", 0, 2), 16.0, A.is_ge, -16.0, A.mult)
     mm([(sl("K7", 0), IB, sl("WR", 0)), (sl("K7", 0), IB16, sl("WR", 1))], False, True)
     turn(lambda b: T.NQ[:, :, b, :], lambda b: T.K7[:, b:C:5], sl("K7", 0), ("NQ",), 32)
     dma([(T.q[gg:8:2, :], T.NQ[:, gg]) for gg in range(2)], [("NQ",)], [], 8e4)
@@ -616,58 +596,129 @@ def lay_out(ops, dep, prio, back, PAR, slack):
     return order, end
 
 
-def replay(ops, dep, order, start=None):
-    end, free, pipe, func = [0.0] * len(ops), [0.0] * 6, 0.0, 0
+def replay(ops, dep, order, start=None, by=None):
+    end, free, last, pipe, func, piped = [0.0] * len(ops), [0.0] * 6, [-1] * 6, 0.0, 0, -1
     for i in order:
         q, dur, f, out, busy, home = ops[i]
-        t = free[q] if q else 0.0
+        t, w = (free[q], last[q]) if q else (0.0, -1)
         for j in dep[i]:
             if end[j] > t:
-                t = end[j]
+                t, w = end[j], j
         if start:
             start[i] = t
         t += dur
         if f and f != func:
             t, func = t + 1.4, f
-        free[q] = t
+        free[q], last[q] = t, i
         if busy:
             t += out
-            pipe = t = (t if t > pipe else pipe) + busy
+            if t < pipe:
+                t, w = pipe, piped
+            pipe, piped = t + busy, i
+            t = pipe
         end[i] = t + home
+        if by:
+            by[i] = w
+    if by:
+        by[-1] = max(order, key=lambda i: end[i])
     return max(end)
 
 
-def improve(order, dep, rev, queue, cost, by_time):
-    cur = cost(order)
-    best, seed, n, tries = (cur, order), 1, len(order), PAR["tries"]
+def resume(ops, dep, order, was, lo):
+    m = lo // MARK
+    end, marks = was[0][:], was[1][:m + 1]
+    free, pipe, func = marks[m]
+    free = free[:]
+    for at in range(m * MARK, len(order), MARK):
+        for i in order[at:at + MARK]:
+            q, dur, f, out, busy, home = ops[i]
+            t = free[q]
+            for j in dep[i]:
+                if end[j] > t:
+                    t = end[j]
+            t += dur
+            if f and f != func:
+                t, func = t + 1.4, f
+            if q:
+                free[q] = t
+            if busy:
+                t += out
+                pipe = t = (t if t > pipe else pipe) + busy
+            end[i] = t + home
+        marks.append((free[:], pipe, func))
+    return end, marks
+
+
+def improve(order, dep, rev, queue, use, by_time, tries, give):
+    n, seed, links = len(order), PAR["seed"], None
+    none = [([0.0] * n, [([0.0] * 6, 0.0, 0)])] * len(use)
+
+    def cost(o, was, lo, limit=1e9):
+        c, now = 0.0, []
+        for (t, m), w, floor in zip(use, was, floors):
+            now.append(resume(t, dep, o, w, lo))
+            c += max(now[-1][0]) / m / len(use)
+            if c + floor > limit:
+                return 1e9, None
+        return c, now
+    floors = [0.85 * (len(use) - 1 - k) / len(use) for k in range(len(use))]
+    cur, state = cost(order, none, 0)
+    best = (cur, order)
     for it in range(tries):
         if it % PAR["sort"] == 0:
-            order = by_time(order)
-            cur = cost(order)
-            if cur < best[0]:
-                best = (cur, order)
+            new = by_time(order)
+            c, now = cost(new, none, 0)
+            if c <= cur + 0.002:
+                order, cur, state, links = new, c, now, None
+            floors = [sum(max(w[0]) / m - 0.004 for (t, m), w in list(zip(use, state))[k + 1:]) / len(use) for k in range(len(use))]
+        if cur < best[0]:
+            best = (cur, order)
         seed = (seed * 1103515245 + 12345) % (1 << 31)
-        a, steps, back = (seed >> 8) % n, (1, 1, 2, 3, 5)[(seed >> 20) % 5], seed >> 28 & 1
+        steps, back = (1, 1, 2, 3, 5)[(seed >> 20) % 5], seed >> 28 & 1
         seq, link = (order[::-1], dep) if back else (order, rev)
-        i = seq[a]
-        near = [b for b in range(a + 1, min(n, a + 60)) if queue[seq[b]] == queue[i]][:steps]
-        if not queue[i] or not near:
-            continue
-        moved, rest, tied = [i], [], set(link[i])
-        for x in seq[a + 1:near[-1] + 1]:
+        if (seed >> 4) % 8 < PAR["aim"]:
+            if links is None or it % 16 == 0:
+                by, links = [-1] * (n + 1), []
+                replay(use[(seed >> 12) % len(use)][0], dep, order, None, by)
+                i = by[-1]
+                while by[i] >= 0:
+                    if by[i] not in dep[i]:
+                        links.append((by[i], i))
+                    i = by[i]
+            if not links:
+                continue
+            x, y = links[(seed >> 8) % len(links)][::-1 if back else 1]
+            a, stop = seq.index(x), seq.index(y)
+            stop = ([stop] + [b for b in range(stop + 1, min(n, stop + 60)) if queue[seq[b]] == queue[x]][:steps - 1])[-1]
+        else:
+            a = (seed >> 8) % n
+            near = [b for b in range(a + 1, min(n, a + 60)) if queue[seq[b]] == queue[seq[a]]][:steps]
+            if not queue[seq[a]] or not near:
+                continue
+            stop = near[-1]
+        moved, rest, tied = [seq[a]], [], set(link[seq[a]])
+        for x in seq[a + 1:stop + 1]:
             if x in tied:
                 moved.append(x)
                 tied.update(link[x])
             else:
                 rest.append(x)
-        if moved[-1] == seq[near[-1]] or len(moved) > 8:
+        if moved[-1] == seq[stop] or len(moved) > PAR["most"]:
             continue
-        new = seq[:a] + rest + moved + seq[near[-1] + 1:]
+        new = seq[:a] + rest + moved + seq[stop + 1:]
         new = new[::-1] if back else new
-        c = cost(new)
-        if c <= cur + PAR["give"] * (1 - it / tries):
-            order, cur = new, c
+        seed = (seed * 1103515245 + 12345) % (1 << 31)
+        limit = cur - give * (1.02 - it / tries) * math.log(((seed >> 8) + 1) / (1 << 23))
+        c, now = cost(new, state, n - 1 - stop if back else a, limit)
+        if c <= limit:
+            order, cur, state, links = new, c, now, None
     return best[1]
+
+
+def table(os, par):
+    return [((None, "v", "a", "t", "g", "s").index(o["q"]), o["dur"], {F.Sigmoid: 1, F.Tanh: 2}.get(o.get("f"), 0),
+             o.get("lat", 0.0) / 2 + o.get("once", 0.0), o.get("busy", 0.0),
+             o.get("lat", 0.0) / 2 + {"c": par["hop"], "r": 0.0}.get(o["kind"], par["wake"])) for o in os]
 
 
 def schedule(cases):
@@ -682,6 +733,16 @@ def schedule(cases):
         dep.append([j for j in d if j not in far])
         for j in dep[i]:
             rev[j].append(i)
+    tag = {}
+    for i, o in enumerate(ops):
+        x = "%s%s.%d" % (o["q"], o["wr"][0][0], o["wr"][0][1]) if o["wr"] else "out"
+        while x in tag:
+            x += "'"
+        tag[x] = i
+    for chain in PAR["first_then"]:
+        for x, y in zip(chain.split(), chain.split()[1:]):
+            dep[tag[y]].append(tag[x])
+            rev[tag[x]].append(tag[y])
     orders = []
     for os, par in cases:
         for slack in PAR["slack"]:
@@ -689,9 +750,7 @@ def schedule(cases):
             for r in range(PAR["rounds"]):
                 order, end = lay_out(os, dep, lay_out(os, rev, end, True, par, slack)[1], False, par, slack)
                 orders.append(order)
-    tabs = [[((None, "v", "a", "t", "g", "s").index(o["q"]), o["dur"], {F.Sigmoid: 1, F.Tanh: 2}.get(o.get("f"), 0),
-              o.get("lat", 0.0) / 2 + o.get("once", 0.0), o.get("busy", 0.0),
-              o.get("lat", 0.0) / 2 + {"c": par["hop"], "r": 0.0}.get(o["kind"], par["wake"])) for o in os] for os, par in cases]
+    tabs = [table(os, par) for os, par in cases]
     ends = [[replay(t, dep, order) for t in tabs] for order in orders]
     least = [min(e[c] for e in ends) for c in range(len(cases))]
     best = min(range(len(orders)), key=lambda j: sum(e / m for e, m in zip(ends[j], least)))
@@ -701,7 +760,10 @@ def schedule(cases):
         start = [0.0] * n
         replay(tabs[0], dep, order, start)
         return sorted(order, key=lambda i: start[i])
-    order = improve(orders[best], dep, rev, [t[0] for t in tabs[0]], lambda o: sum(replay(t, dep, o) / m for t, m in use) / len(use), by_time)
+    queue = [t[0] for t in tabs[0]]
+    order = improve(orders[best], dep, rev, queue, use, by_time, PAR["tries"], PAR["give"])
+    late = [[(q, d, f, out + 1.5 * (c % 2) * (o.get("x") == "s0"), b, h) for (q, d, f, out, b, h), o in zip(t, ops)] for c, t in enumerate(tabs)]
+    order = improve(order, dep, rev, queue, [(t, replay(t, dep, order)) for t in late], by_time, *PAR["again"])
     LOG.append([round(replay(t, dep, order), 1) for t in tabs])
     return order, full
 
@@ -716,7 +778,7 @@ def emit(g, T, ops):
         q = o["q"]
         o["at"] = at
         if o["kind"] == "arr":
-            o["sig"], o["clock"] = ("arr_" + o["x"], 2 * (N - 1)), {}
+            o["sig"], o["clock"] = ("arr_" + o["x"], (1 if o["x"] in LEAN else 2) * (N - 1)), {}
             count[o["sig"][0]] = o["sig"][1]
             continue
         for e in sorted(o["dep"], key=lambda e: -e["at"]):
@@ -741,7 +803,7 @@ def emit(g, T, ops):
                 x.then_inc(T.sem[s], 16)
         else:
             s = "out_" + o["x"]
-            count[s] = 2 * (N - 1)
+            count[s] = (1 if o["x"] in LEAN else 2) * (N - 1)
         o["sig"], o["clock"] = (s, count[s]), dict(known[q])
     for s, n in count.items():
         if max(known[q].get(s, 0) for q in Q) < n:

import math
from concourse.bass import DstId, RemoteDMATransfer
from concourse.mybir import AluOpType, ActivationFunctionType

V, NB, WN, N = 2560, 128, 3456, 8
C, H, HC = V // 16, V // 2, V // 32
OFF = 1728.0
HB = (0, WN, 2 * WN, 2 * WN + V)
TC = 512

SCRATCH = {}
for _n, _w, _d in [
    ("PT", V, "int32"), ("P0", V, "float32"), ("P1", V, "float32"), ("UL", V, "float32"), ("G", V, "float32"),
    ("U1", WN, "float32"), ("U2", WN, "float32"), ("U3", WN, "float32"), ("TH", HB[3] + V, "float32"),
    ("S0", WN, "bfloat16"), ("U0", WN, "bfloat16"), ("SG0", WN, "bfloat16"), ("SG1", WN, "bfloat16"), ("SG2", WN, "bfloat16"),
    ("SG3", V, "bfloat16"), ("PRD", V, "bfloat16"), ("VO", V, "bfloat16"), ("SB", NB, "bfloat16"), ("TB", NB, "float32"),
    ("BH", 128, "bfloat16"), ("ZR", TC, "bfloat16"), ("ONE", C, "bfloat16"), ("CK", 6 * C, "bfloat16"), ("NEG", H // 2, "bfloat16"), ("P2I", 128, "float32"),
    ("CB", C, "bfloat16"), ("HH", 3 * C, "bfloat16"), ("NP", 2 * C, "bfloat16"),
    ("MW", 512, "bfloat16"), ("LM", 32, "uint16"), ("LC", C, "uint16"),
    ("IOT", 160, "float32"), ("PI", 8, "int32"), ("PJ", 8, "int32"), ("PF", 24, "float32"),
    ("M3I", 16, "int32"), ("M3J", 16, "int32"), ("M3", 48, "float32"), ("SEL", 64, "float32"),
    ("ID", 128, "float32"), ("N2I", 128, "float32"),
    ("BZ", 144, "bfloat16"), ("BV", 144, "bfloat16"), ("BL", 144, "bfloat16"),
    ("IB", 128, "bfloat16"), ("NIB", 128, "bfloat16"), ("IB2", 128, "bfloat16"), ("IB16", 128, "bfloat16"), ("IBW", 128, "bfloat16"), ("IBL", 128, "bfloat16"),
    ("LW", 6 * C, "float16"), ("N2", 2 * C, "float16"), ("SF", WN - V, "bfloat16"), ("XP", 2 * C, "float32"),
    ("LS0", 2 * C, "uint16"), ("LS1", 2 * C + 8, "uint16"), ("LS2", 3 * C, "uint16"), ("LS3", C, "uint16"), ("LG", C, "uint16"),
    ("WR", 2 * C, "bfloat16"), ("PR1", 5 * C, "float32"), ("PR2", 4 * C, "float32"), ("PR3", C, "float32"),
    ("BC", C, "float32"), ("BK", C, "float32"),
]:
    SCRATCH[_n] = ("sbuf", [128, _w], _d)
for _k in range(4):
    SCRATCH["FL%d" % _k] = ("sbuf", [128, 5, C], "bfloat16")
SCRATCH["CN"] = ("sbuf", [128, 2, 5, 16], "int32")
SCRATCH["NF"] = ("sbuf", [128, 2, 5, 16], "bfloat16")
SCRATCH["NQ"] = ("sbuf", [128, 2, 5, 16], "float32")
SCRATCH["NA"] = ("sbuf", [128, 3, 2, 5, 16], "bfloat16")
for _k in range(8):
    SCRATCH["K%d" % _k] = ("psum", [128, TC], "float32")
for _n in ("DU1", "DU2", "DU3", "DT1", "DT2", "DW3"):
    SCRATCH[_n] = ("dram", [256, NB], "float32")
for _n in ("DS0", "DG1", "DG2", "DG3"):
    SCRATCH[_n] = ("dram", [256, NB], "bfloat16")

XCH = ["s0", "c1", "u1", "t1", "c2", "c3", "u2", "t2", "u3", "w3"]
LEAN = ("s0", "c1", "u1")
SEMAPHORES = (["e_v", "e_a", "e_t", "e_g"] + ["d%d" % _k for _k in range(70)] + ["arr_" + _x for _x in XCH]
              + ["out_" + _x for _x in XCH])

ALIAS = {"XS": ("S0", 0), "UL0": ("SG3", 0), "W3": ("U1", 0), "YO": ("P0", 0), "SR": ("PR2", 0),
         "R0": ("TH", HB[3]), "R1": ("TH", HB[3] + 2 * TC), "R2": ("TH", HB[2]),
         "A0": ("LW", 5 * C), "T0": ("LW", 4 * C)}

PAR = dict(cyc=0.00083 * 1.1, gat=1.4, pe=0.00042 * 1.1, vfix=0.05, afix=0.07, hop=0.06, wake=0.2, dma=1.5, gdma=1.8, far=1.6, first=6.5, next=2.0, again=(40000, 0.00015),
           rate=6.0e5, row=0.011, farrate=3.2e4, acc=1.6, slack=(0.07, 0.15, 0.25), lam=8.0, tries=120000, sort=200, give=0.0006, use=(1, 2, 4, 5, 6, 8),
           gis=0.5, ris=0.75, wt=128, rounds=4, aim=3, most=10, seed=7, tfix=0.012, cuts=(0, 512, 1024, 1536, 2048, 2304, V),
           first_then=("aONE.0 aMW.0 aMW.256", "vZR.0 vM3J.0 vPJ.2 vPJ.1 vPJ.0 vPF.0 vM3.16 vM3.32 vM3.0 vLM.0 vLM.16 vSEL.0 vBZ.0 vNF.0",
                       "gM3I.0 gPI.0 gIOT.0 gSEL.32 gIB.0 gID.0", "vP0.0 vBK.0", "vP0.0 vBL.0", "vP0.0 vBV.0", "vP0.0 vHH.0", "vP0.0 vHH.160",
                       "vP0.0 vHH.320", "vP0.0 vIB2.0", "vP0.0 vNIB.0"),
           alt="oc10 oc20 oc30 NIB IB2 HH NP BK BV sp11 sp22")
MARK = 16
CASES = [dict(gis=0.8), dict(cyc=0.00083, pe=0.00042, gat=1.56, dma=1.3, gdma=1.6, far=1.5, row=0.008, farrate=3.5e4, gis=1.1, ris=1.0, wake=0.15),
         dict(gat=1.3, dma=1.6, gdma=2.0, far=2.0, row=0.022, farrate=2.5e4, wake=0.3),
         dict(gat=1.3, dma=2.0, gdma=2.6, far=3.5, row=0.008, farrate=3.5e4, wake=0.4),
         dict(cyc=0.00083 * 1.35, pe=0.00042 * 1.35, gat=1.9, gis=1.0), dict(cyc=0.00083 * 1.3, pe=0.00042 * 1.3, gat=1.15),
         dict(cyc=0.00083 * 1.05, pe=0.00042 * 1.15, gat=1.1, row=0.015, farrate=2.4e4, hop=0.14, gis=1.0),
         dict(cyc=0.00083 * 1.2, pe=0.00042 * 1.2, gat=1.75, hop=0.14, wake=0.35, far=2.5),
         dict(cyc=0.00083 * 1.1, pe=0.00042 * 1.1, gat=2.0, hop=0.1, gis=1.0),
         dict(cyc=0.00083 * 1.4, pe=0.00042 * 1.4, gat=1.05, gis=0.8), dict(cyc=0.00083 * 1.15, pe=0.00042 * 1.15, gat=1.15, gis=1.0)]
LOG = []
ORDER = {}

A = AluOpType
F = ActivationFunctionType


def build(g, core, T, topo, PAR):
    rank = T.rank_of(core)
    ops = []
    ALT = PAR["alt"].split()

    def real(x):
        if x[0] not in ALIAS:
            return x
        n, o = ALIAS[x[0]]
        return (n, x[1] + o, x[2] + o) + tuple(x[3:])

    def ap(x):
        if len(x) == 1:
            return T[x[0]][:]
        x = real(x)
        if x[0][:2] == "FL":
            j, a, b = x[1] // C, x[1] % C, x[2] - x[1] // C * C
            return T[x[0]][:, j, a:b] if b <= C else T[x[0]][:, j:x[2] // C, :]
        if x[-1] == "row":
            return T[x[0]][0:1, x[1]:x[2]]
        if len(x) == 3:
            return T[x[0]][:, x[1]:x[2]]
        p0, p1 = (x + ((0, 128),))[4]
        return T[x[0]][p0:p1, x[1]:x[2]:x[3]]

    def width(x):
        return C if len(x) == 1 else len(range(x[1], x[2], x[3] if len(x) > 3 and x[3] != "row" else 1))

    def size(x):
        return 4 if SCRATCH[real(x)[0] if len(x) > 1 else x[0]][2] in ("float32", "int32") else 2

    def reg(x):
        return (x[0], 0, 1 << 20) if len(x) == 1 else real(x)[:3]

    def op(q, fn, rd, wr, dur, kind="c", **kw):
        ops.append(dict(q=q, fn=fn, rd=[reg(x) for x in rd], wr=[reg(x) for x in wr], kind=kind, dur=dur, **kw))

    def vdur(n, c):
        return PAR["vfix"] + max(64, n * c) * PAR["cyc"]

    def sc(s):
        return ap(s) if isinstance(s, tuple) else s

    def ts(out, x, s1, o0, s2=None, o1=None):
        rd = [x] + [s for s in (s1, s2) if isinstance(s, tuple)]
        d = vdur(width(x), max(size(out), size(x)) / 4)
        if o1 is None:
            op("v", lambda: g.vector.tensor_scalar(ap(out), ap(x), sc(s1), None, o0), rd, [out], d)
        else:
            op("v", lambda: g.vector.tensor_scalar(ap(out), ap(x), sc(s1), sc(s2), o0, o1), rd, [out], d)

    def tt(out, x, y, o):
        op("v", lambda: g.vector.tensor_tensor(ap(out), ap(x), ap(y), o), [x, y], [out], vdur(width(x), 1 if "K" in (x[0][0], y[0][0]) else 2))

    def cp(out, x):
        op("v", lambda: g.vector.tensor_copy(ap(out), ap(x)), [x], [out], vdur(width(x), max(size(out), size(x)) / 4))

    def fill(out, c):
        op("v", lambda: g.vector.memset(ap(out), c), [], [out], vdur(width(out), size(out) / 4))

    def gtt(out, win, lst, y):
        op("v", lambda: g.vector.tensor_tensor(ap(out), ap(win).indirect(ap(lst)), ap(y), A.mult), [win, lst, y], [out], vdur(width(out), PAR["gat"]))

    def act(out, x, f, scale=1.0, bias=0.0, lst=None):
        d = PAR["afix"] + max(64, width(out) * (1 if lst is None else PAR["gat"])) * PAR["cyc"]
        if lst is None:
            op("a", lambda: g.scalar.activation(ap(out), ap(x), f, bias=sc(bias), scale=sc(scale)),
               [x] + [s for s in (scale, bias) if isinstance(s, tuple)], [out], d, f=f)
        else:
            op("a", lambda: g.scalar.activation(ap(out), ap(x).indirect(ap(lst)), f, bias=bias, scale=scale), [x, lst], [out], d, f=f)

    def mm(terms, first=True, last=True, each=False):
        def fn():
            ins = None
            for j, (o, l, r) in enumerate(terms):
                ins = g.tensor.matmul(ap(o), ap(l), ap(r), each or first and j == 0, each or last and j == len(terms) - 1)
            return ins
        d = sum(max(min(64, width(l)), width(r)) * (4 if size(r) == 4 else 1) * PAR["pe"] + PAR["tfix"] for o, l, r in terms)
        op("t", fn, [x for t in terms for x in t[1:]], [t[0] for t in terms], d)

    def iota(out, pat, base, cm, flt):
        d = 0.13 + 2 * width(out) * PAR["cyc"]
        if flt:
            op("g", lambda: g.iota(ap(out), pat, base, cm, allow_small_or_imprecise_dtypes=True), [], [out], d)
        else:
            op("g", lambda: g.iota(ap(out), pat, base, cm), [], [out], d)

    def dma(pairs, rd, wr, nbytes, q="s"):
        e = g.sync if q == "s" else g.scalar
        op(q, lambda: [e.dma_start(o, i) for o, i in pairs], rd, wr, 0.1 * len(pairs), kind="d", lat=PAR["dma"],
           busy=8 * len(pairs) * PAR["row"] + nbytes / PAR["rate"])

    def add(x, o, i, rd, nbytes, **cut):
        first = not any(e["q"] == "g" and e["kind"] == "d" for e in ops)
        op("g", lambda: [g.dma_start(o, i, accum_op=A.add, **cut)], rd + [x], [x], PAR["gis"] + (1.5 if first else 0), kind="d",
           lat=PAR["gdma"], busy=PAR["acc"] * nbytes / PAR["rate"])

    def turn(out, src, rd, wr, n):
        for b in range(5):
            op("v", lambda b=b: g.vector.transpose(out(b), src(b)), [rd], [wr], vdur(n, size(rd) / 4), par=1)

    peers = [T.cores[(rank + d) % N] for d in range(1, N)]

    def engines(k):
        masks, nxt = [], [0, k // 2]
        for c in peers:
            e = topo.engines(core, c)
            near = int(topo.die(c) == topo.die(core))
            j = 4 * nxt[near] + (near + k) % 2
            if XCH[k] in LEAN:
                masks.append(1 << e[(4 * (nxt[near] - near * (k // 2)) + (2 * near, 3 - 2 * near)[k % 2]) % len(e)])
            else:
                masks.append((1 << e[j % len(e)]) | (1 << e[(j + 2) % len(e)]))
            nxt[near] += 1
        return masks

    def share(x, dn, src, win, c0, after=()):
        s, s0, masks = T[src[0]], src[1], engines(XCH.index(x))
        dma([(T[dn][16:128, :], s[16:128, s0:s0 + NB]), (T[dn][128:240, :], s[0:112, s0:s0 + NB])],
            [] if src[0] == "s0" else [(src[0], s0, s0 + NB)], [(dn,)], 1e5)

        def fn():
            trs = []
            for d in range(1, N):
                rid, pid, _se = topo.addr(peers[d - 1])
                r0 = 16 * ((d * (d + 1) // 2) % 8)
                trs.append(RemoteDMATransfer(src=T[dn][r0:r0 + 128, :], dst=T[win][:, c0 + (d - 1) * NB:c0 + d * NB],
                                             dst_ids=[DstId(rid=rid, pnc=pid)], dma_engine_mask=masks[d - 1], remote_sem=T.sem["arr_" + x]))
            return g.remote_dma_fused(trs, local_sem=T.sem["out_" + x])
        busy = 60 * (PAR["row"] + NB * size((dn,)) / PAR["farrate"])
        op("g", fn, [(dn,)] + list(after), [("X" + x,)], PAR["ris"], kind="r", x=x, lat=PAR["far"] + 2 * busy * (x in LEAN),
           once={"s0": PAR["first"], "c1": PAR["next"]}.get(x, 0.0) - busy * (x in LEAN), busy=busy)
        ops.append(dict(q=None, kind="arr", x=x, rd=[reg(("X" + x,))], wr=[(win, c0, c0 + WN - V)], dur=0.0))

    dma([(T.CN[:, gg], T.cur[gg:8:2, :]) for gg in range(2)], [], [("CN",)], 8e4, "a")
    for a, b in ((0, TC), (TC, 3 * TC), (3 * TC, V)):
        dma([(T.PT[:, a:b], T.pt[:, a:b])], [], [("PT", a, b)], 512 * (b - a), "s" if a else "a")
    dma([(T.S0[:, 0:V], T.s0[:, :])], [], [("S0", 0, V)], 256 * V)

    iota(("PI", 0, 8), [[0, 8]], 0, 1, False)
    iota(("M3I", 0, 16), [[-1, 16]], 16, 1, False)
    iota(("IOT", 0, 160), [[1, 160]], -15, 0, True)
    dma([(T.S0[:, V:WN], T.s0[:, 0:WN - V])], [], [("S0", V, WN)], 256 * (WN - V))
    share("s0", "DS0", ("s0", 0), "SF", 0)
    iota(("BC", 0, C), [[16, C]], HB[2] - int(OFF), 0, True)
    fill(("ZR", 0, TC), 0.0)
    act(("ONE", 0, C), ("ZR", 0, C), F.Sigmoid, 1.0, 256.0)
    for x, n in ((-1, ("NEG", 0, H // 2)), (-OFF, ("CK", 0, 128)), (-V, ("CK", 2 * C, 3 * C)), (-6, ("CK", 3 * C, 4 * C))):
        iota(n, [[0, width(n)]], int(x), 0, True)
    iota(("CK", 4 * C, 6 * C), [[-144 * 17, 2], [0, C]], 144 * 16, 0, True)
    row = {1.0: ("ONE", 0), -1.0: ("NEG", 0), -OFF: ("CK", 0), -float(V): ("CK", 2 * C), -6.0: ("CK", 3 * C), "wrap": ("CK", 4 * C)}

    def const(out, x, by=("ONE", 0, 128, "row")):
        n, c0 = row[x]
        return (out, by, (n, c0, c0 + width(out)) + by[3:])

    for a, b in ((0, H), (H, V), (V, WN)):
        iota(("U3", a, b), [[0, b - a]], 1, 0, True)
        add(("U3", a, b), T.U3[:, a:b], T.s0[:, a:b] if a < V else T.SF[:], [] if a < V else [("SF", 0, WN - V)], 512 * (b - a))
    col = lambda j: ("PF", j, j + 1)
    for j, m in enumerate((112, 115, 15)):
        ts(("PJ", j, j + 1), ("PI", j, j + 1), m, A.bitwise_and)
    ts(("M3J", 0, 16), ("M3I", 0, 16), 15, A.bitwise_and)
    cp(("PF", 0, 3), ("PJ", 0, 3))
    ts(("M3", 16, 32), ("M3J", 0, 16), 3.0, A.is_lt)
    ts(("M3", 32, 48), ("M3J", 0, 16), 0.0, A.is_equal, -2.0, A.mult)
    tt(("M3", 0, 16), ("M3", 16, 32), ("M3", 32, 48), A.add)
    ts(("LM", 0, 16), ("IOT", 15, 31), 0.0, A.mult, col(2), A.add)
    cp(("LM", 16, 32), ("IOT", 15, 31))
    for tau in range(2):
        act(("MW", 256 * tau, 256 * (tau + 1)), ("M3", 0, 16), F.Identity, (1.0, 2.0 ** -12)[tau], lst=("LM", 16 * tau, 16 * (tau + 1)))
    for tau in range(2):
        fill(("PF", 4, 5, 1, (32 * tau, 32 * tau + 32)), (0.0, -0.42)[tau])
    iota(("SEL", 32, 64), [[1, 4], [16, 8]], 0, 0, True)
    ts(("SEL", 0, 32), ("SEL", 32, 64), col(1), A.is_equal)
    ts(("BZ", 0, 144), ("IOT", 0, 144), col(0), A.is_equal)
    ts(("PF", 12, 15), ("IOT", 15, 27, 4), col(2), A.is_equal)

    def lin(out, x, scale, bias):
        if out[0] in ALT:
            ts(out, x, scale, A.mult, bias, A.add)
        else:
            act(out, x, F.Identity, scale, bias)

    act(col(13), col(13), F.Identity, 1.0, col(14))
    ts(("BL", 0, 144), ("BZ", 0, 144), col(12), A.mult, -float(WN), A.mult)
    lin(("BV", 0, 144), ("BZ", 0, 144), col(13), 0.0)
    for n, w in (("IB", 1.0), ("NIB", -1.0), ("IB2", 2.0), ("ID", 1.0), ("N2I", -2.0), ("P2I", 2.0), ("IBL", -float(WN)), ("IB16", 16.0), ("IBW", -16.0)):
        if n in ALT:
            ts((n, 0, 128), ("IB", 0, 128), w, A.mult)
            continue
        op("g", lambda n=n, w=w: g.affine_select(T[n][:], T.ZR[:, 0:128], [[-1, 128]], A.not_equal, w, 0, 1),
           [("ZR", 0, 128)], [(n, 0, 128)], 0.17 + 256 * PAR["cyc"])
    lin(("BK", 0, C), ("BC", 0, C), 1.0, col(2))
    act(col(10), col(2), F.Identity, 56.0, V - OFF)
    act(("BH", 0, 56), ("ZR", 0, 56), F.Identity, 1.0, col(10))
    iota(("BH", 64, 64 + 56), [[1, 56]], 0, 0, True)
    I, N2I, IB, NIB, IB2, IB16, IBW, IBL = ((n, 0, 128) for n in ("ID", "N2I", "IB", "NIB", "IB2", "IB16", "IBW", "IBL"))
    sl = lambda n, j, w=1: (n, j * C, (j + w) * C)

    cp(("NF",), ("CN",))
    turn(lambda b: T.CB[:, b:C:5], lambda b: T.NF[:, :, b, :], ("NF",), ("CB", 0, C), 32)
    cp(("LC", 0, C), ("CB", 0, C))
    for j, (d, o) in enumerate(((2, 128 - 0.2), (16, 144 - 0.47), (32, 200 - 0.49))):
        lin(sl("HH", j), sl("CB", 0), 1.0 / d, o)
    mm([(sl("K5", 0), IB2, sl("HH", 0)), (sl("K5", 0), NIB, sl("CB", 0))])
    mm([(sl("K5", 1), IB2, sl("HH", 2)), (sl("K5", 1), NIB, sl("HH", 1))])
    lin(sl("NP", 0, 2), sl("K5", 0, 2), 1.0, -255.0)

    WC = (0, 32, C)

    def masked(tau, h):
        for a, b in (((0, TC),), ((TC, 3 * TC), (3 * TC, V)))[h]:
            gtt(("P%d" % tau, a, b), ("MW", 256 * tau, 256 * (tau + 1)), ("LC", a // 16, b // 16), ("PT", a, b))

    def classes(tau, h):
        k, m = ("K0", "K%d" % (1 + 2 * tau))[h], ((32 * tau, 32 * tau + 32), (0, 128))[h]
        for j0 in range(0, 16, 4):
            mm([((k, j, TC, 16, m), ("P%d" % tau, 16 * WC[h] + j, 16 * WC[h + 1], 16), ("SEL", 0, 32)) for j in range(j0, j0 + 4)], each=True)

    def signed(tau, h, s):
        a = TC * (s > 0)
        if h:
            act(("R%d" % (1 + tau), a, a + TC), ("K%d" % (1 + 2 * tau), 0, TC), F.Relu, s, (0.0, -0.42)[tau])
        elif tau == 0:
            act(("R0", a, a + TC, 1, (0, 64)), ("K0", 0, TC, 1, (0, 64)), F.Relu, s, ("PF", 4, 5, 1, (0, 64)))

    def route(tau, h, s, out, some):
        a, o = TC * (s > 0), (out[0], out[1] + WC[h], out[1] + WC[h + 1])
        r, m = ("R0", "R%d" % (1 + tau))[h], ((32 * tau, 32 * tau + 32), (0, 128))[h]
        mm([const(o, -OFF)] * (tau == 0) + [(o, (r, a + 128 * c, a + 128 * (c + 1), 1, m), ("ID",) + m + (1, m)) for c in some])

    def low(out, k, r):
        ts(r, k, 1.5 * 2.0 ** 35, A.add, -1.5 * 2.0 ** 35, A.add)
        tt(out, k, r, A.subtract)

    def apart(out, tau):
        return [(out, IB, sl("LW", 2 * tau + 1)), (out, NIB, sl("LW", 2 * tau))]

    def second(out, tau):
        return [(out, IB, sl("LW", 2 * tau)), (out, I, sl("XP", tau))]

    def zero(out):
        return (out, ("ZR", 0, 128, "row"), ("ZR", 0, width(out), "row"))

    def parts(k, src):
        hi, lo = sl("FL%d" % k, 3), sl("FL%d" % k, 4)
        cp(hi, src)
        tt(lo, src, hi, A.subtract)

    def rows(k):
        j0 = 1 if k == 0 else 0
        fl = T["FL%d" % k]
        turn(lambda b: T.NA[:, j0:3, :, b, :], lambda b: fl[:, 2 + j0:5, b:C:5], sl("FL%d" % k, 2 + j0, 3 - j0), ("NA",), 32 * (3 - j0))
        dma([(T.S0[16 * gg + 4 * j:128:32, 0:V], T.NA[:, j, gg]) for j in range(j0, 3) for gg in range(2)], [("NA",)], [("XS", 0, V)], 1e5)

    def own_copy(k, a, b):
        o = T.SG3 if k == 0 else T.UL
        if "oc%d%d" % (k, a // H) in ALT:
            for c in range(a, b, H // 2):
                x, y = ("UL0" if k == 0 else "UL", c, c + H // 2), ("U%d" % k, c, c + H // 2)
                op("g", lambda x=x, y=y: g.affine_select(ap(x), ap(y), [[0, H // 2]], A.is_ge, 0.0, 0, 0), [y], [x], 0.17 + H * PAR["cyc"])
            return
        dma([(o[:, a:b], T["U%d" % k][:, a:b])], [("U%d" % k, a, b)], [("UL0" if k == 0 else "UL", a, b)], (256 if k == 0 else 512) * (b - a))

    for tau, h in ((0, 0), (1, 0), (0, 1)):
        masked(tau, h)
        classes(tau, h)
    for h in range(2):
        act(("U0", h * H, (h + 1) * H), ("S0", h * H, (h + 1) * H), F.Abs)
        own_copy(0, h * H, (h + 1) * H)
    for h in range(2):
        act(("SG0", h * H, (h + 1) * H), ("S0", h * H, (h + 1) * H), F.Sign, 1.0, 2.0 ** -30)
    act(("U0", V, WN), ("SF", 0, WN - V), F.Abs)
    for h in range(2):
        a, b, kb = WC[h], WC[h + 1], "K%d" % (6 + h)
        signed(0, h, -1)
        route(0, h, -1, (kb, 0), range(4))
        low(("A0", a, b), (kb, a, b), ("SR", a, b))
        ts(("LS0", a, b), ("A0", a, b), OFF, A.add)
    mm([(sl("K6", 1), IB, sl("A0", 0))])
    parts(0, sl("K6", 1))
    masked(1, 1)
    classes(1, 1)
    for h in range(2):
        signed(1, h, -1)
        route(1, h, -1, sl("K5", 0), range(4))
    cp(sl("LS0", 1), sl("K5", 0))
    ts(sl("T0", 0), sl("LS0", 1), -OFF, A.add)
    for tau in range(2):
        for h in range(2):
            signed(tau, h, 1)
            for odd in range(2):
                route(tau, h, 1, sl("K%d" % (4 + tau), odd), (odd, odd + 2))
    low(sl("LW", 0, 2), sl("K4", 0, 2), sl("SR", 1, 2))
    ts(sl("LW", 2, 2), sl("K5", 0, 2), 1.5 * 2.0 ** 23, A.add, -1.5 * 2.0 ** 23 - OFF, A.add)
    for tau in range(2):
        mm(apart(sl("K4", tau), tau))
    tt(sl("XP", 0, 2), sl("K4", 0, 2), sl("NP", 0, 2), A.mult)

    LA = ("LS0", "LS0", "LS1", "LS2")
    SGB = 1.75 + 2.0 ** -23
    nsp = [0]

    def p_op(k, a, b):
        gtt(("P%d" % (k % 2), a, b), ("U%d" % k, 0, WN), (LA[k], a // 16, b // 16), ("UL0" if k == 0 else "UL", a, b))

    def u_op(k, a, b):
        w = math.sqrt(2.0) if k == 2 else 1.0
        act(("U%d" % (k + 1), a, b), ("P%d" % (k % 2), a, b), F.Abs, -2.0 * w, w)

    def sg_op(k, a, b):
        e = 1.0 if k % 2 else -1.0
        act(("SG%d" % (k + 1), a, b), ("P%d" % (k % 2), a, b), F.Sign, -3.5 * e, SGB * e)

    def cross(k, h):
        o, i, a, b = "SG%d" % (k - 1), "SG%d" % k, h * H, (h + 1) * H
        if "cw%d" % k not in ALT:
            add((o, a, b), T[o][:, a:b], T[i][:, a:b], [(i, a, b)], 256 * H)
        elif h:
            add((o, 0, V), T[o][:, 0:V], T[i][:, 0:V], [(i, 0, V)], 256 * V, max_dma_last_dim=2 * H)

    def s_path(k):
        p_op(k, 0, NB)
        u_op(k, 0, NB)
        sg_op(k, 0, NB)
        mm([(("K7", 0, NB), IB, ("SG%d" % j, 0, NB)) for j in (k, k + 1)])
        act(("SB", 0, NB), ("K7", 0, NB), F.Identity)
        share("u%d" % (k + 1), "DU%d" % (k + 1), ("U%d" % (k + 1), 0), "U%d" % (k + 1), V,
              [("TH", 0, V)] if k == 1 else [])
        share("c%d" % (k + 1), "DG%d" % (k + 1), ("SB", 0), "SG%d" % k, V)
        p_op(k, NB, H)
        p_op(k, H, V)

    def s_rest(k):
        for h in range(2):
            sg_op(k, max(NB, h * H), (h + 1) * H)
            cross(k + 1, h)
        for h in range(2):
            u_op(k, max(NB, h * H), (h + 1) * H)
            own_copy(k + 1, h * H, (h + 1) * H)

    def y_path(k):
        if k == 0:
            for a, b in ((0, NB), (NB, H), (H, V)):
                act(("G", a, b), ("P0", a, b), F.Identity, 1.0, -0.5)
                gtt(("TH", a, b), ("U3", 0, WN), ("LS0", a // 16, b // 16), ("G", a, b))
                if a == 0:
                    share("t1", "DT1", ("TH", 0), "TH", V)
            return
        for a, b in ((0, TC), (TC, 3 * TC), (3 * TC, V)):
            act(("G", a, b), ("TH", 0, k * WN), F.Sigmoid, -4.0, lst=(("LS0", "LG")[k - 1], a // 16, b // 16))
        for a in range(0, V, TC):
            kb, p = ("K%d" % (nsp[0] % 2), 0, TC), ("P%d" % (k % 2), a, a + TC)
            nsp[0] += 1
            if "sp%d%d" % (k, a // TC) in ALT:
                act(kb, p, F.Identity, 2.0, -1.0)
            else:
                mm([const(kb, -1.0), (kb, ("P2I", 0, 128), p)])
            tt(("TH", HB[k] + a, HB[k] + a + TC), ("G", a, a + TC), kb, A.mult)

    def via(k, h):
        act(("VO", h * H, (h + 1) * H), ("XS", 0, WN), F.Identity, lst=(LA[k], HC * h, HC * (h + 1)))

    def wrap(out, sel, src, h):
        return [((out[0], out[1] + HC * h, out[1] + HC * (h + 1)), (sel, 15 - i, 143 - i), (src, h * H + i, (h + 1) * H, 16)) for i in range(16)]

    def z_op(k):
        for h in range(2):
            gtt(("PRD", h * H, (h + 1) * H), ("SG%d" % (k - 1), 0, WN), (LA[k], C + HC * h, C + HC * (h + 1)), ("SG%d" % k, h * H, (h + 1) * H))
            mm([const(sl("K2", 0), -6.0)] * (h == 0) + wrap(sl("K2", 0), "BZ", "PRD", h), h == 0, h == 1)
        fl, z = "FL%d" % k, sl("K2", 0)
        if k < 3:
            ts(sl(fl, 0), z, 1.5 * 2.0 ** 26 + 8, A.add, 1.5 * 2.0 ** 26 + 8, A.is_equal)
        ts(sl(fl, 1), z, 3.0, A.is_ge)
        ts(sl(fl, 2), z, -13.0, A.is_le)

    def old(out, k, s):
        d = IB if s > 0 else NIB
        return [(out, d, sl(("A0", "N2")[k], 0))]

    dma([(T.S0[4 * j:128:16, V:WN], x) for j, x in enumerate((T.ZR[:, 0:56], T.BH[:, 0:56], T.BH[:, 64:120]))], [("ZR", 0, 56), ("BH", 0, 128)], [("XS", V, WN)], 5e4)
    rows(0)
    s_path(0)
    s_rest(0)
    y_path(0)

    s_path(1)
    mm(old(sl("K3", 1), 0, -1) + second(sl("K3", 1), 0))
    mm([(sl("K3", 2), NIB, sl("T0", 0))] + second(sl("K3", 2), 1))
    mm(old(sl("K3", 0), 0, -1), True, False)
    for h in range(2):
        via(1, h)
        mm(wrap(sl("K3", 0), "BV", "VO", h), False, h == 1)
    for tau in range(2):
        mm(apart(sl("K4", tau), tau) + [(sl("K4", tau), N2I, sl("XP", tau))])
    lb, lo = ("K6", 0, 2 * C + 8), ("K6", 2 * C, 2 * C + 8)
    mm([zero(lb)] + old(sl("K6", 0), 0, 1) + [(sl("K6", 1), IB, sl("T0", 0)), (lo, IBL, ("ONE", 0, 8)), (lo, I, ("BK", 0, 8))], True, False)
    z_op(1)
    s_rest(1)
    tt(sl("PR1", 0, 3), sl("K3", 0, 3), sl("FL1", 0, 3), A.mult)
    mm([(sl("K6", 0), I, sl("PR1", 0)), (sl("K6", 0), I, sl("PR1", 1)), (sl("K6", 1), I, sl("PR1", 2)), (lo, IBL, ("FL1", 2 * C, 2 * C + 8))], False, True)
    ts(("LS1", 0, 2 * C + 8), lb, OFF, A.add)
    ts(sl("N2", 0, 2), sl("LS1", 0, 2), -OFF, A.add)
    parts(1, sl("K6", 0))
    rows(1)
    tt(sl("PR1", 3, 2), sl("K4", 0, 2), sl("FL1", 1, 2), A.mult)
    y_path(1)
    act(("TB", 0, NB), ("TH", 0, WN + NB), F.Identity, lst=("LS1", 2 * C, 2 * C + 8))
    share("t2", "DT2", ("TB", 0), "TH", WN + V, [("P1", 0, V)])

    s_path(2)
    mm(old(sl("K3", 1), 1, -1) + second(sl("K3", 1), 0) + [(sl("K3", 1), I, sl("PR1", 3))])
    mm([(sl("K3", 2), NIB, sl("N2", 1)), (sl("K3", 2), I, sl("PR1", 4))] + second(sl("K3", 2), 1))
    mm(old(sl("K3", 0), 1, -1), True, False)
    mm([(sl("K4", 0), IBL, ("ONE", 0, C)), (sl("K4", 0), IBL, sl("FL1", 2))])
    mm([zero(sl("K6", 0, 3))] + old(sl("K6", 0), 1, 1)
       + [(sl("K6", 1), IB, sl("N2", 1)), (sl("K6", 2), I, sl("BK", 0))], True, False)
    mm(old(sl("K5", 0), 1, 1), True, False)
    for h in range(2):
        via(2, h)
        mm(wrap(sl("K5", 0), "BL", "VO", h), False, h == 1)
        mm(wrap(sl("K3", 0), "BV", "VO", h), False, h == 1)
    ts(sl("LG", 0), sl("K5", 0), OFF + WN, A.add)
    z_op(2)
    s_rest(2)
    tt(sl("PR2", 0, 3), sl("K3", 0, 3), sl("FL2", 0, 3), A.mult)
    tt(sl("PR2", 3), sl("K4", 0), sl("FL2", 2), A.mult)
    mm([(sl("K6", 0), I, sl("PR2", 0)), (sl("K6", 0), I, sl("PR2", 1)), (sl("K6", 1), I, sl("PR2", 2)), (sl("K6", 2), I, sl("PR2", 3))], False, True)
    ts(sl("LS2", 0, 3), sl("K6", 0, 3), OFF, A.add)
    y_path(2)

    for a, b in ((0, NB), (NB, H), (H, V - PAR["wt"]), (V - PAR["wt"], V)):
        if b == V:
            if a < b:
                act(("G", a, b), ("TH", 0, HB[2] + b), F.Tanh, -2.0, lst=("LS2", 2 * C + a // 16, 2 * C + b // 16))
                act(("W3", a, b), ("G", a, b), F.Identity, 0.5, 0.5)
            continue
        act(("W3", a, b), ("TH", 0, HB[2] + b), F.Sigmoid, -4.0, lst=("LS2", 2 * C + a // 16, 2 * C + b // 16))
        if a == 0:
            share("w3", "DW3", ("U1", 0), "U1", V)
    for h in range(2):
        a, b = h * H, (h + 1) * H
        p_op(3, a, b)
        act(("P1", a, b), ("P1", a, b), F.Identity, 1.0, -1.0)
    mm([const(sl("K4", 0), -float(V)), (sl("K4", 0), I, sl("PR2", 3))])
    mm([(sl("K6", 0), I, sl("BK", 0))], True, False)
    z_op(3)
    tt(sl("PR3", 0), sl("K4", 0), sl("FL3", 2), A.mult)
    mm([(sl("K6", 0), I, sl("PR3", 0))], False, True)
    ts(sl("LS3", 0), sl("K6", 0), V + OFF, A.add)
    cuts = PAR["cuts"]
    for a, b in zip(cuts, cuts[1:]):
        gtt(("TH", HB[3] + a, HB[3] + b), ("W3", 0, WN), ("LS2", a // 16, b // 16), ("P1", a, b))
        act(("YO", a, b), ("TH", 0, HB[3] + b), F.Tanh, -2.0, lst=("LS3", a // 16, b // 16))
        dma([(T.y[:, a:b], T.P0[:, a:b])], [("YO", a, b)], [], 512 * (b - a))

    turns = lambda out, j, w, ks: [(out, w, sl("FL%d" % k, j)) for k in ks]
    for ks in ((1, 2), (3,)):
        head = [const(sl("K5", 0, 2), "wrap"), (sl("K5", 0), IB, sl("CB", 0)), (sl("K5", 0), IBW, sl("HH", 1)), (sl("K5", 1), IB, sl("HH", 1))] if ks[0] == 1 else []
        mm(head + turns(sl("K5", 0), 1, IB, ks) + turns(sl("K5", 1), 2, IB, ks), ks[0] == 1, ks[0] == 3)
        head = [(sl("K7", 0), IB, sl("CB", 0))] if ks[0] == 1 else []
        mm(head + turns(sl("K7", 0), 1, IB, ks) + turns(sl("K7", 0), 2, IB16, ks), ks[0] == 1, False)
    ts(sl("WR", 0, 2), sl("K5", 0, 2), 16.0, A.is_ge, -16.0, A.mult)
    mm([(sl("K7", 0), IB, sl("WR", 0)), (sl("K7", 0), IB16, sl("WR", 1))], False, True)
    turn(lambda b: T.NQ[:, :, b, :], lambda b: T.K7[:, b:C:5], sl("K7", 0), ("NQ",), 32)
    dma([(T.q[gg:8:2, :], T.NQ[:, gg]) for gg in range(2)], [("NQ",)], [], 8e4)
    return ops


def conflict(o, e):
    q = o["q"]
    for (mine, theirs, ww) in ((o["rd"], e["wr"], 0), (o["wr"], e["wr"], 1), (o["wr"], e["rd"], 0), (o["rd"], e["rd"], 2)):
        for x in mine:
            for y in theirs:
                if x[0] != y[0]:
                    continue
                if x[0][0] == "K" and (e["q"] != q or q == "t"):
                    return True
                if ww == 2 or (ww == 1 and o.get("par") and e.get("par") and e["q"] == q and e["rd"] == o["rd"]):
                    continue
                if x[1] < y[2] and y[1] < x[2]:
                    return True
    return False


def lay_out(ops, dep, prio, back, PAR, slack):
    n = len(ops)
    hop = [PAR["hop"] if e["kind"] == "c" else (0.0 if e["kind"] == "r" else PAR["wake"]) for e in ops]
    fly = [o.get("lat", 0.0) + o.get("busy", 0.0) + o.get("once", 0.0) for o in ops]
    nxt = [[] for o in ops]
    for i in range(n):
        for j in dep[i]:
            nxt[j].append(i)
    need, at = [len(d) for d in dep], [0.0] * n
    end, free, pipe, func, order = [0.0] * n, {}, 0.0, None, []
    ready = [i for i in range(n) if not dep[i]]
    while ready:
        start = {i: max(free.get(ops[i]["q"], 0.0), at[i] + (fly[i] + hop[i] if back else 0.0)) for i in ready}
        first = min(ready, key=lambda i: (start[i], i))
        q = ops[first]["q"]
        i = max((j for j in ready if ops[j]["q"] == q and start[j] <= start[first] + slack),
                key=lambda j: (prio[j] - PAR["lam"] * max(0.0, start[j] - start[first] - 0.1), -j))
        o, t = ops[i], start[i]
        d = o["dur"]
        if o.get("f") in (F.Sigmoid, F.Tanh) and o["f"] != func:
            d, func = d + 1.4, o["f"]
        if q is not None:
            free[q] = t + d
        end[i] = t + d
        if "busy" in o and not back:
            pipe = max(pipe, t + d + o["lat"] / 2 + o.get("once", 0.0)) + o["busy"]
            end[i] = pipe + o["lat"] / 2
        order.append(i)
        ready.remove(i)
        for j in nxt[i]:
            at[j] = max(at[j], end[i] + (0.0 if back else hop[i]))
            need[j] -= 1
            if need[j] == 0:
                ready.append(j)
    return order, end


def replay(ops, dep, order, start=None, by=None):
    end, free, last, pipe, func, piped = [0.0] * len(ops), [0.0] * 6, [-1] * 6, 0.0, 0, -1
    for i in order:
        q, dur, f, out, busy, home = ops[i]
        t, w = (free[q], last[q]) if q else (0.0, -1)
        for j in dep[i]:
            if end[j] > t:
                t, w = end[j], j
        if start:
            start[i] = t
        t += dur
        if f and f != func:
            t, func = t + 1.4, f
        free[q], last[q] = t, i
        if busy:
            t += out
            if t < pipe:
                t, w = pipe, piped
            pipe, piped = t + busy, i
            t = pipe
        end[i] = t + home
        if by:
            by[i] = w
    if by:
        by[-1] = max(order, key=lambda i: end[i])
    return max(end)


def resume(ops, dep, order, was, lo):
    m = lo // MARK
    end, marks = was[0][:], was[1][:m + 1]
    free, pipe, func = marks[m]
    free = free[:]
    for at in range(m * MARK, len(order), MARK):
        for i in order[at:at + MARK]:
            q, dur, f, out, busy, home = ops[i]
            t = free[q]
            for j in dep[i]:
                if end[j] > t:
                    t = end[j]
            t += dur
            if f and f != func:
                t, func = t + 1.4, f
            if q:
                free[q] = t
            if busy:
                t += out
                pipe = t = (t if t > pipe else pipe) + busy
            end[i] = t + home
        marks.append((free[:], pipe, func))
    return end, marks


def improve(order, dep, rev, queue, use, by_time, tries, give):
    n, seed, links = len(order), PAR["seed"], None
    none = [([0.0] * n, [([0.0] * 6, 0.0, 0)])] * len(use)

    def cost(o, was, lo, limit=1e9):
        c, now = 0.0, []
        for (t, m), w, floor in zip(use, was, floors):
            now.append(resume(t, dep, o, w, lo))
            c += max(now[-1][0]) / m / len(use)
            if c + floor > limit:
                return 1e9, None
        return c, now
    floors = [0.85 * (len(use) - 1 - k) / len(use) for k in range(len(use))]
    cur, state = cost(order, none, 0)
    best = (cur, order)
    for it in range(tries):
        if it % PAR["sort"] == 0:
            new = by_time(order)
            c, now = cost(new, none, 0)
            if c <= cur + 0.002:
                order, cur, state, links = new, c, now, None
            floors = [sum(max(w[0]) / m - 0.004 for (t, m), w in list(zip(use, state))[k + 1:]) / len(use) for k in range(len(use))]
        if cur < best[0]:
            best = (cur, order)
        seed = (seed * 1103515245 + 12345) % (1 << 31)
        steps, back = (1, 1, 2, 3, 5)[(seed >> 20) % 5], seed >> 28 & 1
        seq, link = (order[::-1], dep) if back else (order, rev)
        if (seed >> 4) % 8 < PAR["aim"]:
            if links is None or it % 16 == 0:
                by, links = [-1] * (n + 1), []
                replay(use[(seed >> 12) % len(use)][0], dep, order, None, by)
                i = by[-1]
                while by[i] >= 0:
                    if by[i] not in dep[i]:
                        links.append((by[i], i))
                    i = by[i]
            if not links:
                continue
            x, y = links[(seed >> 8) % len(links)][::-1 if back else 1]
            a, stop = seq.index(x), seq.index(y)
            stop = ([stop] + [b for b in range(stop + 1, min(n, stop + 60)) if queue[seq[b]] == queue[x]][:steps - 1])[-1]
        else:
            a = (seed >> 8) % n
            near = [b for b in range(a + 1, min(n, a + 60)) if queue[seq[b]] == queue[seq[a]]][:steps]
            if not queue[seq[a]] or not near:
                continue
            stop = near[-1]
        moved, rest, tied = [seq[a]], [], set(link[seq[a]])
        for x in seq[a + 1:stop + 1]:
            if x in tied:
                moved.append(x)
                tied.update(link[x])
            else:
                rest.append(x)
        if moved[-1] == seq[stop] or len(moved) > PAR["most"]:
            continue
        new = seq[:a] + rest + moved + seq[stop + 1:]
        new = new[::-1] if back else new
        seed = (seed * 1103515245 + 12345) % (1 << 31)
        limit = cur - give * (1.02 - it / tries) * math.log(((seed >> 8) + 1) / (1 << 23))
        c, now = cost(new, state, n - 1 - stop if back else a, limit)
        if c <= limit:
            order, cur, state, links = new, c, now, None
    return best[1]


def table(os, par):
    return [((None, "v", "a", "t", "g", "s").index(o["q"]), o["dur"], {F.Sigmoid: 1, F.Tanh: 2}.get(o.get("f"), 0),
             o.get("lat", 0.0) / 2 + o.get("once", 0.0), o.get("busy", 0.0),
             o.get("lat", 0.0) / 2 + {"c": par["hop"], "r": 0.0}.get(o["kind"], par["wake"])) for o in os]


def schedule(cases):
    ops = cases[0][0]
    n = len(ops)
    dep, rev, below, full = [], [[] for o in ops], [], []
    for i in range(n):
        d = [j for j in range(i) if conflict(ops[i], ops[j])]
        full.append(d)
        far = set().union(*[below[j] for j in d])
        below.append(far.union(d))
        dep.append([j for j in d if j not in far])
        for j in dep[i]:
            rev[j].append(i)
    tag = {}
    for i, o in enumerate(ops):
        x = "%s%s.%d" % (o["q"], o["wr"][0][0], o["wr"][0][1]) if o["wr"] else "out"
        while x in tag:
            x += "'"
        tag[x] = i
    for chain in PAR["first_then"]:
        for x, y in zip(chain.split(), chain.split()[1:]):
            dep[tag[y]].append(tag[x])
            rev[tag[x]].append(tag[y])
    orders = []
    for os, par in cases:
        for slack in PAR["slack"]:
            end = list(range(n))
            for r in range(PAR["rounds"]):
                order, end = lay_out(os, dep, lay_out(os, rev, end, True, par, slack)[1], False, par, slack)
                orders.append(order)
    tabs = [table(os, par) for os, par in cases]
    ends = [[replay(t, dep, order) for t in tabs] for order in orders]
    least = [min(e[c] for e in ends) for c in range(len(cases))]
    best = min(range(len(orders)), key=lambda j: sum(e / m for e, m in zip(ends[j], least)))
    use = [(tabs[c], least[c]) for c in PAR["use"]]

    def by_time(order):
        start = [0.0] * n
        replay(tabs[0], dep, order, start)
        return sorted(order, key=lambda i: start[i])
    queue = [t[0] for t in tabs[0]]
    order = improve(orders[best], dep, rev, queue, use, by_time, PAR["tries"], PAR["give"])
    late = [[(q, d, f, out + 1.5 * (c % 2) * (o.get("x") == "s0"), b, h) for (q, d, f, out, b, h), o in zip(t, ops)] for c, t in enumerate(tabs)]
    order = improve(order, dep, rev, queue, [(t, replay(t, dep, order)) for t in late], by_time, *PAR["again"])
    LOG.append([round(replay(t, dep, order), 1) for t in tabs])
    return order, full


def emit(g, T, ops):
    Q = {"v": g.vector, "a": g.scalar, "t": g.tensor, "g": g, "s": g.sync}
    esem = {"v": "e_v", "a": "e_a", "t": "e_t", "g": "e_g"}
    known = {q: {} for q in Q}
    count = {}
    nd = [0]
    for at, o in enumerate(ops):
        q = o["q"]
        o["at"] = at
        if o["kind"] == "arr":
            o["sig"], o["clock"] = ("arr_" + o["x"], (1 if o["x"] in LEAN else 2) * (N - 1)), {}
            count[o["sig"][0]] = o["sig"][1]
            continue
        for e in sorted(o["dep"], key=lambda e: -e["at"]):
            s, n = e["sig"]
            if known[q].get(s, 0) >= n or q == e["q"] == "t":
                continue
            Q[q].wait_ge(T.sem[s], n)
            known[q][s] = n
            for s2, n2 in e["clock"].items():
                if known[q].get(s2, 0) < n2:
                    known[q][s2] = n2
        ins = o["fn"]()
        if o["kind"] == "c":
            s = esem[q]
            count[s] = count.get(s, 0) + 1
            ins.then_inc(T.sem[s], 1)
        elif o["kind"] == "d":
            s = "d%d" % nd[0]
            nd[0] += 1
            count[s] = 16 * len(ins)
            for x in ins:
                x.then_inc(T.sem[s], 16)
        else:
            s = "out_" + o["x"]
            count[s] = (1 if o["x"] in LEAN else 2) * (N - 1)
        o["sig"], o["clock"] = (s, count[s]), dict(known[q])
    for s, n in count.items():
        if max(known[q].get(s, 0) for q in Q) < n:
            g.sync.wait_ge(T.sem[s], n)


def rank_program(g, core, T, topo):
    if T.rank_of(core) is None:
        return
    cases = [(build(g, core, T, topo, dict(PAR, **c)), dict(PAR, **c)) for c in CASES]
    if repr(PAR) not in ORDER:
        ORDER[repr(PAR)] = schedule(cases)
    order, dep = ORDER[repr(PAR)]
    ops = cases[0][0]
    for o, d in zip(ops, dep):
        o["dep"] = [ops[j] for j in d]
    emit(g, T, [ops[j] for j in order])
